import numpy as np, ml_dtypes
CORES = [51,54,179,182]
N = 4
BF = ml_dtypes.bfloat16
def gentries(a):
    return np.ascontiguousarray(a.reshape(8, 16, -1).transpose(0, 2, 1)).reshape(8, -1)
def gtable(e):
    e = np.asarray(e); return np.ascontiguousarray(e.reshape(8, -1, 16).transpose(0, 2, 1)).reshape(128, -1).astype(np.int32)
A, B, RO, DB, XM = 1152, 256, 2, 4, (2, 3)
P = 3 * A + B
def tie(L, u, v):
    L[u] = v; L[v] = u
def net(rng, nf, pairs, nb, how=""):
    o = rng.permutation(A); k = 3 * A + rng.permutation(B); L = np.arange(P); e = nf + 2 * pairs
    if how == "ends":
        o = o[(o != 0) & (o != A - 1)]; k = k[(k != 3 * A) & (k != P - 1)]
        o = np.concatenate([o[:e], [0, A - 1], o[e:]]); k = np.concatenate([[3 * A, P - 1], k])
    fr, a, b, bd, w = o[:nf], o[nf:nf + pairs], o[nf + pairs:e], o[e:e + nb], o[e + nb:]
    tie(L, a, b); tie(L, bd, k[:nb])
    if how == "chains":
        j = 0; M = 2 ** DB
        for m, shut in ((M - 1, 0), (M, 0), (M + 1, 0), (2 * M, 0), (1, 0), (1, 1), (3, 1), (M + 1, 0)):
            for i in (1, 2):
                tie(L, i * A + b[j:j + m - 1], i * A + a[j + 1:j + m])
                if shut: tie(L, i * A + b[j + m - 1], i * A + a[j])
            j += m
    if how == "selves": tie(L, A + bd, 2 * A + bd)
    if how == "mates": tie(L, A + bd[:nb // 2], A + bd[nb // 2:nb // 2 * 2])
    h = 0 if how in ("selves", "mates") else min(nb, len(w)) * 3 // 4
    tie(L, w[:h], A + bd[:h])
    idle = L == np.arange(P)
    for i in range(3): idle[i * A + fr] = False
    aux = rng.permutation(A + np.flatnonzero(idle[A:3 * A])); n = len(w) - h
    tie(L, w[h:], aux[:n])
    rest = rng.permutation(np.concatenate([aux[n:], 3 * A + np.flatnonzero(idle[3 * A:])])); n = len(rest) // 2
    tie(L, rest[:n], rest[n:2 * n])
    return L, a, b
def sizes(rng):
    nf = int(rng.integers(A // 8, A // 4 + 1)); nb = int(rng.integers(5 * B // 8, 7 * B // 8 + 1)); nw = int(rng.integers(A // 16, A // 8 + 1))
    return nf, (A - nf - nb - nw) // 2, nb
def blank(rng):
    return np.zeros((N, 8, P), np.int64), rng.integers(0, 16, (N, 8, 16, A)), rng.integers(2, 9, (N, 8, 16, RO))
def manned(v):
    at = v[3 * A:]
    return (at < A) & (v[np.minimum(at, A - 1)] == 3 * A + np.arange(B))
def pack(L, x, t):
    return {"lk": np.stack([gtable(v) for v in L]), "x0": np.ascontiguousarray(x.reshape(N, 128, A)).astype(np.int32), "th": np.ascontiguousarray(t.reshape(N, 128, RO)).astype(np.int32)}
def setup_inputs(rng):
    L, x, t = blank(rng)
    for r in range(N):
        for g in range(8): L[r, g] = net(rng, *sizes(rng))[0]
    return pack(L, x, t)
def setup_inputs_chains(rng):
    L, x, t = blank(rng); M = 2 ** DB
    for r in range(N):
        for g in range(8):
            c = (g + r) % 4; nf, n, nb = sizes(rng)
            if c % 2 == 1:
                L[r, g] = net(rng, nf, n, nb)[0]; continue
            if c == 2:
                n = n + nf // 2; nf = 0; t[r, g, :, 0] = 0; t[r, g, :, 1] = 15
            else: t[r, g, :, 0] = 15
            v, a, b = net(rng, nf, n, nb, "chains")
            to = np.array([i * A + p for i in (1, 2) for p in (a[M - 1], a[3 * M], a[5 * M + 1], a[5 * M + 2], b[5 * M + 3], a[5 * M + 5])])
            k = 3 * A + rng.permutation(np.flatnonzero(v[3 * A:] >= A))[:len(to)]
            v[k] = to; L[r, g] = v
            xa = rng.integers(0, 2, (16, M)); xa[0] = 1
            x[r, g][:, a[M - 1:2 * M - 1]] = xa; x[r, g][:, b[M - 1:2 * M - 1]] = rng.integers(14, 16, (16, M))
            x[r, g][:, a[6 * M + 5]] = 0; x[r, g][:, b[6 * M + 5]] = 15
    return pack(L, x, t)
def setup_inputs_room(rng):
    L, x, t = blank(rng); f = A // 8
    for r in range(0, N, 2):
        for g in range(8):
            n = A // 4
            nf, c = ((f, f // 2), (f, f // 2 + 1), (f, f // 2 - 1), (f, 0), (0, f // 2), (1, f // 2), (f + 1, f // 2), (f + 1, f // 2 + 1))[(g + r) % 8]
            L[r, g], a, b = net(rng, nf, n, 3 * B // 4); t[r, g, :, 0] = 5
            xa = rng.integers(0, 16, (16, n)); xb = xa ^ 1; m = rng.permutation(n)[:c]
            xa[:, m] = xa[:, m] & 7; xb[:, m] = xa[:, m] + 8
            x[r, g][:, a] = xa; x[r, g][:, b] = xb
    for r in range(1, N, 2):
        t[r] = rng.integers(1, 8, (8, 16, RO))
        for g in range(8):
            if g == (r + 3) % 8:
                L[r, g] = net(rng, A // 2, A // 4, 0)[0]; t[r, g, :, 0] = 0; t[r, g, :, 1:] = 15; continue
            if g == (r + 4) % 8:
                L[r, g] = net(rng, 0, A // 2, 0)[0]; t[r, g, :, 0] = 15; t[r, g, :, 1:] = 0; continue
            L[r, g], a, b = net(rng, *sizes(rng)); n = len(a); j = np.arange(n)
            xa = rng.integers(0, 8, (16, n)); xb = xa + t[r, g, :, :1]; i = rng.integers(0, 16, n)
            xb[i, j] = xb[i, j] + rng.integers(-1, 2, n)
            if g == (r + 1) % 8:
                t[r, g] = 0; xb = np.where(rng.random(n) < 0.5, xa, xb)
            if g == (r + 2) % 8:
                t[r, g] = 15; xa = np.zeros((16, n), np.int64); xb = xa + 15; xb[i, j] = 14 + rng.integers(0, 2, n)
            x[r, g][:, a] = xa; x[r, g][:, b] = xb
    return pack(L, x, t)
def setup_inputs_border(rng):
    L, x, t = blank(rng); s = int(rng.integers(0, 8))
    for r in range(N):
        for g in range(8):
            how = ("full", "none", "odd", "selves", "mates", "few", "ends", "")[(g + s) % 8]; nf, n, nb = sizes(rng)
            if how == "full" or (how == "odd" and r % 2 == 1): nb = B
            elif how == "none" or how == "odd": nb = 0
            elif how == "few": nb = B // 8
            L[r, g] = net(rng, nf, (A - nf - nb - A // 16) // 2, nb, how)[0]
    return pack(L, x, t)
def setup_inputs_loose(rng):
    L, x, t = blank(rng); z = int(rng.integers(0, 8))
    for g in range(8):
        kk = 3 * A + rng.permutation(B)
        for r in range(N):
            if g == (z + r) % 8:
                L[r, g] = rng.integers(0, P, P); continue
            nf = sizes(rng)[0]; nb = 7 * B // 8
            v, a, b = net(rng, nf, (A - nf - nb - A // 4) // 2, nb)
            fr = np.flatnonzero(v[:A] == np.arange(A)); w = rng.permutation(np.flatnonzero((v[:A] >= A) & (v[:A] < 3 * A)))
            s = B // 8 + r * (B // 16)
            k = np.concatenate([kk[:B // 8], kk[s:s + B // 8]])
            hold = np.ones(P, bool); hold[k] = False
            m = 3 * A + np.flatnonzero((v[3 * A:] < A) & hold[3 * A:]); bd = v[m]
            kind = np.arange(len(k)) % 4
            v[k] = np.where(kind == 0, rng.choice(w, len(k)), np.where(kind == 1, rng.choice(np.concatenate([a, b]), len(k)), np.where(kind == 2, rng.choice(bd, len(k)), rng.choice(fr, len(k)))))
            n = len(w) // 2; kind = np.arange(n) % 3
            v[w[:n]] = np.where(kind == 0, rng.choice(np.concatenate([a, b]), n), np.where(kind == 1, rng.choice(bd, n), rng.choice(m, n)))
            q = A + rng.permutation(2 * A)[:A // 4]
            v[q] = rng.integers(0, 3, len(q)) * A + rng.choice(np.concatenate([fr, a, b]), len(q))
            L[r, g] = v
    for r in range(N):
        q = r ^ XM[0]
        for g in range(8):
            if r > q or g in ((z + r) % 8, (z + q) % 8): continue
            v = L[r, g]; k = int(rng.choice(np.flatnonzero(manned(v) & manned(L[q, g]))))
            v[A - 1] = 3 * A + k; v[3 * A + k] = 2 * A - 1
            k = 3 * A + rng.permutation(np.flatnonzero(manned(v) & manned(L[q, g])))[:8]; c = np.array(v[k])
            v[A + c[:4]] = c[np.array([1, 2, 0, 3])]
            h = np.array(v[:A]); a = np.flatnonzero((h < A) & (h > np.arange(A)) & (v[np.minimum(h, A - 1)] == np.arange(A)))
            a = rng.permutation(a)[:4]; b = np.array(v[a])
            v[k[4:]] = A + a; v[A + b] = c[4:]; x[r, g][:, b] = x[r, g][:, a] ^ 1
    return pack(L, x, t)
def setup_inputs_spread(rng):
    L, x, t = blank(rng)
    x = np.minimum((np.exp2(4.2 * rng.random((N, 8, 1, A))) * rng.random((N, 8, 16, A))).astype(np.int64), 15)
    t = np.minimum((np.exp2(4 * rng.random((N, 8, 16, RO))) * rng.random((N, 8, 16, RO))).astype(np.int64), 15)
    for r in range(N):
        for g in range(8):
            nf = int(rng.integers(0, A // 2)); nb = int(rng.integers(0, B + 1)); nw = int(rng.integers(0, A // 4))
            L[r, g] = net(rng, nf, (A - nf - nb - nw) // 2, nb)[0]
    return pack(L, x, t)
def check_inputs(d):
    bad = []
    for k, hi in (("lk", P - 1), ("x0", 15), ("th", 15)):
        if np.min(d[k]) < 0 or np.max(d[k]) > hi: bad.append("range of " + k)
    return bad
def meet(L, ph, x, th):
    own = np.arange(P); col = np.arange(A); q = L[:A]; c = np.minimum(q, A - 1)
    pair = (q < A) & (q != col) & (L[c] == col)
    dif = np.abs(x - x[:, c]); near = np.add.reduce(dif, axis=0) < th
    free = np.flatnonzero(q == col)
    a = np.flatnonzero(pair & near); b = q[a]
    u = np.flatnonzero(pair & ~near & (col < q))[:len(free) // 2]; v = q[u]
    f1 = free[0:2 * len(u):2]; f2 = free[1:2 * len(u):2]
    J = np.arange(P); S = np.zeros((16, P), np.int64)
    for i in (1, 2):
        J[i * A + a] = L[i * A + b]; S[:, i * A + a] = (ph[:, i * A + b] + dif[:, a]) & 15
    J[A + u] = v; J[2 * A + u] = f1; J[A + v] = u; J[2 * A + v] = f2
    for k in range(DB):
        S = (S + S[:, J]) & 15; J = J[J]
    to = J[L]; ps = (ph + S[:, L]) & 15
    nl = np.array(to); nph = np.array(ps); nx = np.array(x)
    for new, old in ((u, A + v), (v, A + u), (f1, 2 * A + u), (f2, 2 * A + v)):
        nl[new] = to[old]; nph[:, new] = ps[:, old]
    for e, f in ((A + u, A + v), (2 * A + u, A + f1), (2 * A + v, A + f2), (2 * A + f1, 2 * A + f2)):
        nl[e] = f; nl[f] = e; nph[:, e] = 0; nph[:, f] = 0
    for i in range(3):
        nl[i * A + a] = own[i * A + a]; nph[:, i * A + a] = 0
    nx[:, f1] = (x[:, u] + x[:, v]) & 15; nx[:, f2] = dif[:, u]
    return nl, nph, nx
def border(L, ph, x, m):
    at = L[:, :, 3 * A:]; up = (at < A) & (np.take_along_axis(L, np.minimum(at, A - 1), 2) == 3 * A + np.arange(B))
    nl = np.array(L); nph = np.array(ph); nx = np.array(x)
    for r in range(N):
        q = r ^ m
        for g in range(8):
            k = np.flatnonzero(up[r, g] & up[q, g]); a = at[r, g][k]; b = at[q, g][k]
            rho = np.arange(P); rho[a] = A + a; rho[A + a] = a
            nl[r, g] = rho[L[r, g][rho]]
            n = ph[r, g][:, rho]; s = (ph[r, g][:, 3 * A + k] + ph[q, g][:, 3 * A + k]) & 15
            n[:, 3 * A + k] = s; n[:, A + a] = s; nph[r, g] = n
            nx[r, g][:, a] = x[q, g][:, b]
    return nl, nph, nx
def reference(lk, x0, th):
    L = np.stack([gentries(v) for v in lk]).astype(np.int64); x = x0.astype(np.int64).reshape(N, 8, 16, A); ph = np.zeros((N, 8, 16, P), np.int64)
    t = np.add.reduce(th.astype(np.int64).reshape(N, 8, 16, RO), axis=2)
    for rnd in range(RO):
        for r in range(N):
            for g in range(8):
                L[r, g], ph[r, g], x[r, g] = meet(L[r, g], ph[r, g], x[r, g], t[r, g, rnd])
        L, ph, x = border(L, ph, x, XM[rnd])
    return {"yl": L.astype(np.float32), "yp": ph.reshape(N, 128, P).astype(np.float32).astype(BF), "yx": x.reshape(N, 128, A).astype(np.float32).astype(BF)}

@@ -1,0 +1,782 @@
+from concourse.mybir import AluOpType, ActivationFunctionType
+
+A, B, RO, XM = 1152, 256, 2, (2, 3)
+P = 3 * A + B
+C = 32768.0
+Z = 128.0 * C
+OFA = 65.0 * 128.0
+OFF = 65.0 * 192.0
+MAGIC = 1.5 * 2.0 ** 27
+BIG = 16384.0
+oUL, oFL, oD, oU, oF = 0, 576, 1728, 2240, 5952
+oFA, oF2, oT, oC, WEND = 9664, 10240, 10816, 11392, 11968
+DM = 512
+oXF = DM + A + 16
+POOL = {"SF": 5300, "SU": 2400, "SB": 8800, "SI": 600}
+CFG = {"xc": "vvv", "ll": "sssssv", "sh": "ggy", "rn": "vvvvsvsss", "up": "ss", "n1": "sss", "n2": "svv", "ld": "sss", "u4": "gssggs",
+       "u0": "svsvss", "mod": "vsvvvvvvv", "yl": "ssssv"}
+
+F32 = {"W": WEND, "V": 7168, "UP": 3 * A, "U4": DM + P, "IN1": 2 * A, "RHO": DM + P, "SV": 512, "SF": POOL["SF"]}
+TWO = {"FB": P, "CB0": P, "CB1": 2 * A, "CB5": 2560, "DR": DM + P, "XA": oXF + 576, "XB": oXF + 576, "XC": A, "LL": A, "DIF": A + 16,
+       "N1": A + 16, "SB": POOL["SB"], "LP0": B + 16, "LP1": B + 16, "LX0": B, "LX1": B, "LF0": 16, "LF1": 16}
+I32S = {"XI": A + 16, "LKI": 232, "THI": 2, "SI": POOL["SI"]}
+SCRATCH = {"SU": ("sbuf", [128, POOL["SU"]], "uint16")}
+SCRATCH.update({k: ("sbuf", [128, v], "float32") for k, v in F32.items()})
+SCRATCH.update({k: ("sbuf", [128, v], "bfloat16") for k, v in TWO.items()})
+SCRATCH.update({k: ("sbuf", [128, v], "int32") for k, v in I32S.items()})
+SCRATCH.update({"PS%d" % k: ("psum", [128, 512], "float32") for k in range(8)})
+
+NDMA = 44
+SEMAPHORES = ["ev", "es", "et", "eg", "sent"] + ["dm%d" % k for k in range(NDMA)] + ["ar%d" % k for k in range(3 * RO)]
+
+op = AluOpType
+fn = ActivationFunctionType
+CY, PE = 0.00083 * 1.2, 0.000417 * 1.2
+
+
+def sub(v, lo, hi, st=1):
+    return (v[0], v[1] + lo, v[1] + hi, st)
+
+
+def cnt(v):
+    if v[0] == "ind":
+        return 16 * cnt(v[2])
+    return len(range(v[1], v[2], v[3]))
+
+
+def ap(T, v):
+    if not isinstance(v, tuple):
+        return v
+    if v[0] == "ind":
+        return ap(T, v[1]).indirect(ap(T, v[2]))
+    if v[3] == 1:
+        return T[v[0]][:, v[1]:v[2]]
+    return T[v[0]][:, v[1]:v[2]:v[3]]
+
+
+def regs(vs):
+    out = []
+    for v in vs:
+        if not isinstance(v, tuple):
+            continue
+        if v[0] == "ind":
+            out += regs([v[1], v[2]])
+        elif v[0].startswith("PS"):
+            out.append((v[0], 0, 512))
+        else:
+            out.append((v[0], v[1], v[2]))
+    return out
+
+
+def build(GA, SC):
+    ops = []
+    top = {"SF": 0, "SU": 0, "SB": 0, "SI": 0, "bank": 0, "big": 0, "dma": 0}
+
+    def new(pool, n):
+        lo = top[pool]
+        top[pool] = lo + (n + 15) // 16 * 16
+        assert top[pool] <= POOL[pool], pool
+        return (pool, lo, lo + n, 1)
+
+    def W(lo, hi, st=1):
+        return ("W", lo, hi, st)
+
+    def t(name, lo, hi, st=1):
+        return (name, lo, hi, st)
+
+    def U(lo, hi):
+        return ("U4", DM + lo, DM + hi, 1)
+
+    def hot(v):
+        ops[-1]["bump"] = v
+
+    def ind(win, lst):
+        return ("ind", win, lst)
+
+    def bank(n):
+        top["bank"] += 1
+        return ("PS%d" % (3 + top["bank"] % 5), 0, n, 1)
+
+    def big(n):
+        top["big"] += 1
+        return ("PS%d" % (top["big"] % 3), 0, n, 1)
+
+    def add(eng, f, rd, wr, cost, kind="c", lat=0.0, sem=None):
+        ops.append({"eng": eng, "f": f, "rd": regs(list(rd) + [v[2] for v in wr if v[0] == "ind"]),
+                    "wr": regs([v[1] if v[0] == "ind" else v for v in wr]), "cost": cost, "kind": kind, "lat": lat, "sem": sem, "bump": 0.0})
+
+    def vcost(out, ins, both=False):
+        if out[0] == "ind":
+            r = SC
+        elif ins[0][0] == "ind":
+            r = GA
+        else:
+            r = (0.5 if all(v[0] in TWO for v in [out] + ins) else 1.0) * (2.0 if both else 1.0)
+        return 0.06 + max(64, cnt(out) * r) * CY
+
+    def cp(out, a):
+        add("v", lambda q, T, x: q.tensor_copy(ap(T, out), ap(T, a)), [a], [out], vcost(out, [a]))
+        return out
+
+    def ts(out, a, s1, o0, s2=None, o1=None):
+        if o1 is None:
+            f = lambda q, T, x: q.tensor_scalar(ap(T, out), ap(T, a), ap(T, s1), None, o0)
+        else:
+            f = lambda q, T, x: q.tensor_scalar(ap(T, out), ap(T, a), ap(T, s1), ap(T, s2), o0, o1)
+        add("v", f, [a, s1, s2], [out], vcost(out, [a]))
+        return out
+
+    def tt(out, a, b, o):
+        both = not (a[0].startswith("PS") or b[0].startswith("PS"))
+        add("v", lambda q, T, x: q.tensor_tensor(ap(T, out), ap(T, a), ap(T, b), o), [a, b], [out], vcost(out, [a, b], both))
+        return out
+
+    def scan(out, d0, d1, init):
+        add("v", lambda q, T, x: q.tensor_tensor_scan(ap(T, out), ap(T, d0), ap(T, d1), init, op.mult, op.add), [d0, d1], [out], 0.14)
+        return out
+
+    def act(out, a, func=None, bias=0.0, scale=1.0):
+        fu = fn.Identity if func is None else func
+        add("s", lambda q, T, x: q.activation(ap(T, out), ap(T, a), fu, ap(T, bias), ap(T, scale)), [a, bias, scale], [out],
+            0.07 + max(64, cnt(out) * (GA if a[0] == "ind" else 1.0)) * CY)
+        return out
+
+    def gat(eng, out, win, lst):
+        return act(out, ind(win, lst)) if eng == "s" else cp(out, ind(win, lst))
+
+    def mm(groups, first=True, final=True):
+        def f(q, T, x):
+            last = None
+            for out, terms in groups:
+                for k, (l, r) in enumerate(terms):
+                    last = q.matmul(ap(T, out), ap(T, l), ap(T, r), first and k == 0, final and k == len(terms) - 1)
+            return last
+        rd = [v for o, terms in groups for lr in terms for v in lr]
+        add("t", f, rd, [o for o, terms in groups],
+            0.06 + sum(max(64, cnt(r)) * (1 if r[0] in TWO else 4) for o, terms in groups for l, r in terms) * PE)
+
+    def wrap(src, pick, extra=()):
+        st = src[3]
+        ps = bank(cnt(src) // 16)
+        terms = [(sub(pick, 15 - i, 143 - i), (src[0], src[1] + i * st, src[2], 16 * st)) for i in range(16)]
+        mm([(ps, terms + list(extra))])
+        return ps
+
+    def iota(out, pat, base, cm):
+        if out[0] not in I32S:
+            f = lambda q, T, x: q.iota(ap(T, out), pat, base, cm, allow_small_or_imprecise_dtypes=True)
+        else:
+            f = lambda q, T, x: q.iota(ap(T, out), pat, base, cm)
+        add("g", f, [], [out], 0.15 + 2 * cnt(out) * CY)
+        return out
+
+    def sel(out, a, cmp):
+        add("g", lambda q, T, x: q.affine_select(ap(T, out), ap(T, a), [[-1, 128]], cmp, 0.0, 0, 1), [a], [out], 0.17 + 256 * CY)
+        return out
+
+    def fill(out, val):
+        return iota(out, [[0, cnt(out)]], int(val), 0)
+
+    def dma(eng, f, rd, wr, lat):
+        add(eng, f, rd, wr, 0.1 if eng != "g" else 1.0, "d", lat, "dm%d" % top["dma"])
+        top["dma"] += 1
+
+    def cast(eng, out, a):
+        if eng == "g":
+            dma("g", lambda q, T, x: q.dma_start(ap(T, out), ap(T, a)), [a], [out], 2.5 + cnt(out) * 0.0012)
+        else:
+            act(sub(out, 0, 576), sub(a, 0, 576))
+            act(sub(out, 576, A), sub(a, 576, A))
+
+    def twin(eng, out, a):
+        if eng == "g":
+            add("g", lambda q, T, x: q.affine_select(ap(T, out), ap(T, a), [[0, cnt(a)]], op.is_ge, 0.0, 0, 0), [a], [out], 0.17 + 2 * cnt(a) * CY)
+        elif eng == "s":
+            act(out, a)
+        else:
+            dma("y", lambda q, T, x: q.dma_start(ap(T, out), ap(T, a)), [a], [out], 3.2)
+
+    def send(rnd, k, src, dst):
+        s = "ar%d" % (3 * rnd + k)
+        tok = ("tok%d" % (3 * rnd + k), 0, 1, 1)
+        add("g", lambda q, T, x: q.remote_dma(ap(T, dst), ap(T, src), T.sem[s], T.sem["sent"], x["pid"][rnd], x["rid"][rnd], x["mask"][rnd]),
+            [src], [tok], 0.6, "r")
+        add("n", None, [tok], [dst], 0.01, "a", 4.5 + cnt(src) * 0.006, s)
+
+    F, Bf, U16, I32 = (lambda n: new("SF", n)), (lambda n: new("SB", n)), (lambda n: new("SU", n)), (lambda n: new("SI", n))
+
+    dma("y", lambda q, T, x: q.dma_start(T["LKI"][:, :], T["lk"][:, :]), [], [t("LKI", 0, 232)], 2.2)
+    dma("s", lambda q, T, x: q.dma_start(T["XI"][:, 0:A], T["x0"][:, :]), [], [t("XI", 0, A)], 3.5)
+    dma("y", lambda q, T, x: q.dma_start(T["THI"][:, :], T["th"][:, :]), [], [t("THI", 0, 2)], 2.2)
+
+    pc = iota(I32(1), [[0, 1]], 0, 1)
+    ROW = iota(F(144), [[1, 144]], 0, 0)
+    I64 = sub(ROW, 0, 64)
+    pcf = iota(F(1), [[0, 1]], 0, 1)
+    AWp = iota(F(232), [[16, 232]], 0, 1)
+    P16 = iota(Bf(232), [[16, 232]], 0, 0)
+    oddi = ts(I32(1), pc, 1, op.bitwise_and)
+    oddC = ts(F(1), oddi, C, op.mult)
+    evnC = act(F(1), oddC, None, C, -1.0)
+    FBv = t("FB", 0, P)
+    ts(sub(FBv, 0, 64), I64, oddC, op.mult, Z, op.add)
+    EC = act(F(64), I64, None, 0.0, evnC)
+    for k in range(4):
+        w = 64 << k
+        ts(sub(FBv, w, 2 * w), sub(FBv, 0, w), sub(EC, 1 << k, (1 << k) + 1), op.add)
+    ts(sub(FBv, 1024, 2048), sub(FBv, 0, 1024), sub(EC, 16, 17), op.add)
+    act(sub(FBv, 2048, 2688), sub(FBv, 0, 640), None, sub(EC, 32, 33))
+    ts(sub(FBv, 2688, P), sub(FBv, 0, 1024), sub(EC, 42, 43), op.add)
+    dma("g", lambda q, T, x: q.dma_start(T["W"][:, oF:oF + P], T["FB"][:, :]), [FBv], [W(oF, oF + P)], 7.0)
+    g16i = ts(I32(1), pc, 112, op.bitwise_and)
+    g16 = cp(F(1), g16i)
+    i16 = act(F(1), g16, None, pcf, -1.0)
+    g15 = act(F(1), g16, None, 15.0)
+    ioff = act(F(1), i16, None, -OFF)
+    iBB = act(F(1), i16, None, 2 * BIG)
+    w0 = ts(F(1), i16, 0.0, op.is_equal, 64.0, op.mult)
+    w1 = ts(F(1), i16, 1.0, op.is_equal, w0, op.add)
+    BD = ts(Bf(144), ROW, g15, op.is_equal, w1, op.mult)
+    BDA = act(Bf(144), BD, None, 0.0, 1.0 / C)
+    BD2 = act(Bf(144), BD, None, 0.0, 2.0 / C)
+    BS = ts(Bf(144), ROW, g15, op.is_equal)
+    ONE = fill(Bf(128), 1)
+    ID = sel(Bf(128), ONE, op.is_equal)
+    NID = act(Bf(128), ID, None, 0.0, -1.0)
+    IDF = act(F(128), ID)
+    BI = act(Bf(128), ID, None, 0.0, BIG)
+    NBI = act(Bf(128), ID, None, 0.0, -BIG)
+    NPI = act(Bf(128), ID, None, 0.0, -float(P))
+    N8 = act(Bf(128), ID, None, 0.0, -8.0)
+    N4 = act(Bf(128), ID, None, 0.0, -4096.0)
+    ps = bank(128)
+    mm([(ps, [(ID, sub(BS, 15 - i, 143 - i)) for i in range(16)])])
+    BO = act(Bf(128), ps)
+    b1 = sel(Bf(128), BO, op.is_gt)
+    ps = bank(128)
+    mm([(ps, [(NID, b1), (N4, ID)])])
+    TRC = act(Bf(128), ps)
+    ng16 = act(F(1), g16, None, 0.0, -1.0)
+    AW = act(F(232), AWp, None, ng16)
+    ONE = sub(ONE, 0, 72)
+    thb = cp(Bf(2), t("THI", 0, 2))
+    psth = bank(2)
+    mm([(psth, [(BO, thb)])])
+    TH = act(F(2), psth)
+    aw = sub(AW, 0, 72)
+    u0, f0 = float(oU - oFL), float(oF - oFL)
+    BA = act(F(72), aw, None, f0 - u0)
+    AWB = act(F(16), sub(AW, 216, 232), None, OFA)
+    KK = act(F(32), sub(AW, 0, 32), None, 2 * BIG - DM)
+    CA = fill(Bf(16), A)
+    iP = act(F(1), i16, None, float(P))
+    for xb in ("XA", "XB"):
+        fill(t(xb, DM + A, oXF), C / 2)
+    fill(t("XI", A, A + 16), C / 2)
+    fill(t("DIF", A, A + 16), 0)
+    fill(t("N1", A, A + 16), Z + 40 * C)
+    fill(W(0, oFL), Z)
+    fill(W(oFL, oD), Z)
+    for lo, hi in ((0, 576), (576, A), (3 * A, 3 * A + 256), (3 * A + 256, 4 * A), (6 * A, 6 * A + 256)):
+        fill(t("V", lo, hi), 0)
+    for rnd in range(RO):
+        fill(t("LP%d" % rnd, B, B + 16), 0)
+    fill(W(oD, oU), 0)
+    fill(t("U4", 0, DM), 0)
+    for xb in ("XA", "XB"):
+        fill(t(xb, 0, DM), 0)
+    for lo, hi in ((0, 832), (832, DM + A), (DM + 2 * A, DM + 2 * A + 704), (DM + 2 * A + 704, DM + P)):
+        fill(t("DR", lo, hi), 0)
+    DS = act(Bf(256), sub(FBv, 0, 256), None, sub(EC, 18, 19), 0.0)
+    for k in range(6):
+        iota(t("RHO", k * 704, (k + 1) * 704), [[1, 704]], k * 704 - DM, 0)
+
+    L0 = cp(U16(232), t("LKI", 0, 232))
+    Lw = cp(F(232), t("LKI", 0, 232))
+    for k, (lo, hi) in enumerate(((0, 38), (38, 74), (74, 110), (110, 146), (146, 190), (190, 232))):
+        gat(CFG["u0"][k], W(oU + 16 * lo, oU + 16 * hi), FBv, sub(L0, lo, hi))
+    cp(t("XA", DM, DM + 576), t("XI", 0, 576))
+    cp(t("XA", DM + 576, DM + A), t("XI", 576, A))
+
+    VW = (t("V", 0, P), t("V", 3 * A, 3 * A + P))
+    VX = (t("V", A, 3 * A), t("V", 4 * A, 6 * A))
+    CBS = (t("CB0", 0, P), t("CB1", 0, 2 * A))
+    Lw1 = F(232)
+    PAY = [(Bf(256), Bf(256), Bf(16)) for rnd in range(RO)]
+    keep = (top["SF"], top["SB"], top["SU"])
+
+    for rnd in range(RO):
+        top["SF"], top["SB"], top["SU"] = keep
+        last = rnd == RO - 1
+        Xc, Xn = ("XA", "XB") if rnd % 2 == 0 else ("XB", "XA")
+        x = t(Xc, DM, DM + A)
+        L = sub(Lw, 0, 72)
+        thr = sub(TH, rnd, rnd + 1)
+        LC = ts(U16(72), L, float(A), op.min)
+        for k in range(3):
+            lo, hi = 384 * k, 384 * (k + 1)
+            lst = sub(LC, 24 * k, 24 * (k + 1))
+            gat(CFG["xc"][k], t("XC", lo, hi), t(Xc, DM, oXF) if rnd else t("XI", 0, A + 16), lst)
+            gat(CFG["ll"][3 * rnd + k], t("LL", lo, hi), W(oU, oU + A + 16), lst)
+            ps = big(384)
+            mm([(ps, [(NID, sub(FBv, lo, hi)), (NID, sub(x, lo, hi))])], True, False)
+            mm([(ps, [(ID, t("XC", lo, hi)), (ID, t("LL", lo, hi))])], False, True)
+            act(t("DIF", lo, hi), ps, fn.Abs)
+        psD = wrap(t("DIF", 0, A), BS)
+        k0a = tt(F(72), L, aw, op.subtract)
+        free = ts(Bf(72), k0a, 0.0, op.is_equal)
+        LTh = ts(F(72), k0a, 0.0, op.is_gt, 240.5, op.mult)
+        psf = bank(144)
+        mm([(sub(psf, 0, 72), [(BO, free)]), (sub(psf, 72, 144), [(TRC, free)])])
+        incf = scan(F(72), ONE, sub(psf, 0, 72), 0.0)
+        rfx = tt(F(72), incf, sub(psf, 72, 144), op.add)
+        nf = sub(incf, 71, 72)
+        nfi = ts(I32(1), nf, 0.5, op.mult, -0.25, op.add)
+        nfe = ts(F(1), nfi, 2.0, op.mult, -1.0, op.add)
+        nfr = act(F(1), nfe, None, 2 * OFA)
+        a1 = tt(F(72), aw, rfx, op.subtract)
+        nfm = act(F(1), nf, None, -4095.0)
+        a2 = act(F(72), a1, None, nfm)
+        pf = tt(F(72), a2, rfx, op.min)
+        fc = act(F(72), L, None, f0)
+        near = ts(Bf(72), psD, thr, op.is_lt)
+        u2 = tt(Bf(72), psD, LTh, op.is_lt)
+        nbb = act(Bf(72), psD, fn.Relu, -240.5 * 4096.0, 4096.0)
+        cand = tt(Bf(72), u2, near, op.is_gt)
+        nann = tt(Bf(72), near, free, op.is_le)
+        psc = bank(144)
+        mm([(sub(psc, 0, 72), [(BO, cand)]), (sub(psc, 72, 144), [(TRC, cand)])])
+        incc = scan(F(72), ONE, sub(psc, 0, 72), -576.0)
+        rcx = tt(F(72), incc, sub(psc, 72, 144), op.add)
+        LN = ts(U16(72), rcx, 4671.0, op.add, 1000.0, op.min)
+        pm = tt(F(72), rcx, pf, op.min)
+        LS = ts(U16(72), pm, 4671.0, op.add)
+        for k in range(3):
+            cp(ind(W(0, oD), sub(LS, 24 * k, 24 * (k + 1))), sub(FBv, 384 * k, 384 * (k + 1)))
+        for k in range(3):
+            gat(CFG["n1"][k], t("N1", 384 * k, 384 * (k + 1)), t("FB", 0, 1008), sub(LN, 24 * k, 24 * (k + 1)))
+        for k in range(3):
+            gat(CFG["n2"][k], t("XC", 384 * k, 384 * (k + 1)), t("N1", 0, A + 16), sub(LC, 24 * k, 24 * (k + 1)))
+        psN = wrap(t("XC", 0, A), BD2, [(ID, nbb)])
+        rc2 = act(F(72), rcx, None, 2 * (4671.0 + OFA) - 1.0, 2.0)
+        r = tt(F(72), psN, rc2, op.min)
+        nd = ts(Bf(72), r, nfr, op.is_ge, BIG, op.mult)
+        pse = bank(144)
+        mm([(sub(pse, 0, 72), [(ID, sub(P16, 0, 72)), (BI, nann)]), (sub(pse, 72, 144), [(IDF, L), (BI, nann)])])
+        LD = ts(U16(72), sub(pse, 0, 72), i16, op.add, float(A), op.min)
+        hot(5.0)
+        e0 = tt(F(72), sub(pse, 72, 144), BA, op.min)
+        for k in range(3):
+            gat(CFG["ld"][k], t("LL", 384 * k, 384 * (k + 1)), t("DIF", 0, A + 16), sub(LD, 24 * k, 24 * (k + 1)))
+        for k in range(6):
+            ps = big(384)
+            mm([(ps, [(NID, sub(FBv, A + 384 * k, A + 384 * (k + 1))), (ID, t("LL", 384 * (k % 3), 384 * (k % 3 + 1)))])])
+            act(t("IN1", 384 * k, 384 * (k + 1)), ps)
+        E12, K12, S1, LS1 = F(144), F(144), F(144), U16(144)
+        act(sub(E12, 0, 72), e0, None, u0 + A)
+        act(sub(E12, 72, 144), e0, None, u0 + 2 * A - 1 + 2 * OFA)
+        tt(sub(K12, 0, 72), nd, fc, op.add)
+        tt(sub(K12, 72, 144), nd, r, op.add)
+        tt(S1, K12, E12, op.min)
+        cp(sub(LS1, 0, 72), sub(S1, 0, 72))
+        ts(sub(LS1, 72, 144), sub(S1, 72, 144), 1.0 - 2 * OFA, op.add)
+        JL = [U16(144) for k in range(4)]
+
+        def jlist(k, c):
+            lo, hi = 768 * c, 768 * (c + 1)
+            cb = act(sub(CBS[k % 2], lo, hi), sub(VX[k % 2], lo, hi), None, 192.0, 1.0 / C)
+            ps = wrap(cb, BD, [(ID, sub(P16, 72 + 48 * c, 72 + 48 * (c + 1)))])
+            ts(sub(JL[k], 48 * c, 48 * (c + 1)), ps, ioff, op.add)
+            twin(CFG["sh"][c], t("IN1", lo, hi), sub(VX[k % 2], lo, hi))
+        for c in range(3):
+            tt(sub(VX[0], 768 * c, 768 * (c + 1)), ind(W(oFL, oF + P), sub(LS1, 48 * c, 48 * (c + 1))), t("IN1", 768 * c, 768 * (c + 1)), op.add)
+            jlist(0, c)
+        for k in range(4):
+            for c in range(3):
+                lo, hi = 768 * c, 768 * (c + 1)
+                tt(sub(VX[(k + 1) % 2], lo, hi), ind(VW[k % 2], sub(JL[k], 48 * c, 48 * (c + 1))), t("IN1", lo, hi), op.add)
+                if k < 3:
+                    jlist(k + 1, c)
+        UVb = Bf(576)
+        act(sub(UVb, 0, 576, 2), W(oUL, oUL + 288))
+        ps = wrap(sub(UVb, 0, 576, 2), BDA)
+        LU = ts(U16(18), ps, -OFA, op.add)
+        act(sub(UVb, 1, 576, 2), ind(W(oU, oU + A), LU))
+        ps = wrap(UVb, BDA)
+        LUV = ts(U16(36), ps, -OFA, op.add, float(A - 1), op.min)
+        for c in range(2):
+            gat("s", W(oT + 288 * c, oT + 288 * (c + 1)), W(oU + 2 * A, oU + 3 * A), sub(LUV, 18 * c, 18 * (c + 1)))
+        act(W(oC, oC + 576), UVb, None, sub(EC, 36, 37))
+        act(W(oFA, oFA + 576), W(oFL, oFL + 576), None, sub(EC, 18, 19))
+        act(W(oF2, oF2 + 576, 2), W(oFL + 1, oFL + 576, 2), None, sub(EC, 36, 37))
+        act(W(oF2 + 1, oF2 + 576, 2), W(oFL, oFL + 576, 2), None, sub(EC, 36, 37))
+        XU = Bf(576)
+        for c in range(2):
+            gat("s", sub(XU, 288 * c, 288 * (c + 1)), x, sub(LUV, 18 * c, 18 * (c + 1)))
+        xe, xo = sub(XU, 0, 576, 2), sub(XU, 1, 576, 2)
+        ps = big(288)
+        mm([(ps, [(ID, xe), (NID, xo)])])
+        act(t(Xc, oXF + 1, oXF + 576, 2), ps, fn.Abs)
+        ps = big(288)
+        mm([(ps, [(ID, xe), (ID, xo)])])
+        xs = act(Bf(288), ps, fn.Sign, -15.5)
+        ps = big(288)
+        mm([(ps, [(ID, xe), (ID, xo), (N8, xs)])])
+        act(t(Xc, oXF, oXF + 576, 2), ps, None, -8.0)
+        n1 = act(F(1), sub(incc, 71, 72), None, 2 * 576.0 - 1.0, 2.0)
+        n2 = ts(F(1), n1, nfe, op.min, 1.0 - 4095.0, op.add)
+        g3 = ts(Bf(72), rfx, n2, op.is_ge, BIG, op.mult)
+        rm = tt(F(72), g3, a1, op.add)
+        cm = tt(F(72), k0a, nd, op.subtract)
+        r0 = tt(F(72), r, aw, op.subtract)
+        rd_ = tt(F(72), r0, nd, op.subtract)
+        Ra, Rb = F(216), F(216)
+        ps2 = bank(216)
+        grp = []
+        for i, (src, k1, k2) in enumerate(((cm, A, oT - oU), (cm, P, oC - oU - A), (rd_, oFA - oU - 2 * A + 1 - 2 * OFA, oF2 - oU - 2 * A))):
+            lo, hi = 72 * i, 72 * (i + 1)
+            act(sub(Ra, lo, hi), src, fn.Relu, float(k1))
+            act(sub(Rb, lo, hi), rm, fn.Relu, k2 + 4095.0, -1.0)
+            grp.append((sub(ps2, lo, hi), [(ID, sub(P16, lo, hi)), (NPI, nann), (IDF, sub(Ra, lo, hi)), (IDF, sub(Rb, lo, hi))]))
+        mm(grp)
+        LS2 = ts(U16(216), ps2, iP, op.add)
+        hot(8.0)
+        LP = U16(232)
+        ps3 = bank(144)
+        mm([(sub(ps3, 72 * i, 72 * (i + 1)), [(IDF, sub(Lw, 72 * (i + 1), 72 * (i + 2))), (BI, nann), (ID, nd), (ID, g3)]) for i in range(2)])
+        ts(sub(LP, 72, 216), ps3, -3 * BIG, op.add, 0.0, op.max)
+        cp(sub(LP, 216, 232), sub(Lw, 216, 232))
+        x1 = act(F(72), rm, fn.Relu, oXF - DM + 4095.0, -1.0)
+        ps = bank(72)
+        mm([(ps, [(ID, sub(P16, 0, 72)), (IDF, x1)])])
+        LX = ts(U16(72), ps, i16, op.add)
+        hot(8.0)
+        for c in range(12):
+            act(t("UP", 288 * c, 288 * (c + 1)), ind(W(oU, WEND), sub(LS2, 18 * c, 18 * (c + 1))), None, -7.5 if last else 0.0)
+        cbp = Bf(A)
+        cast(CFG["up"][rnd], cbp, t("UP", 0, A))
+        ps = wrap(cbp, BDA)
+        ts(sub(LP, 0, 72), ps, -OFA, op.add)
+        hot(4.0)
+        for c in range(4):
+            gat("s", t(Xn, DM + 288 * c, DM + 288 * (c + 1)), t(Xc, DM, oXF + 576), sub(LX, 18 * c, 18 * (c + 1)))
+        xn = t(Xn, DM, DM + A)
+        U4b = U(3 * A, P)
+        tt(U4b, ind(VW[0], sub(LP, 216, 232)), W(oU + 3 * A, oU + P), op.add)
+        for c in range(6):
+            tt(U(576 * c, 576 * (c + 1)), ind(VW[0], sub(LP, 36 * c, 36 * (c + 1))), t("UP", 576 * c, 576 * (c + 1)), op.add)
+        L4 = F(232)
+        L4u = U16(232)
+        cb0 = CBS[0]
+        act(sub(cb0, 3 * A, P), U4b)
+        ps = wrap(sub(cb0, 3 * A, P), BDA)
+        LB = ts(U16(16), ps, -OFA, op.add, float(A - 1), op.min)
+        ts(sub(L4u, 216, 232), ps, -OFA, op.add)
+        Lb = act(sub(L4, 216, 232), ps, None, -OFA)
+        PP, PX, PF = PAY[rnd]
+        if last:
+            pi1, pi2 = I32(256), I32(256)
+            cp(pi1, U4b)
+            ts(pi2, pi1, 15, op.bitwise_and)
+            cp(PP, pi2)
+        else:
+            ps = big(256)
+            mm([(ps, [(IDF, U4b), (NID, sub(cb0, 3 * A, P))])])
+            act(PP, ps)
+        LPv, LXv, LFv = t("LP%d" % rnd, 0, B), t("LX%d" % rnd, 0, B), t("LF%d" % rnd, 0, 16)
+        send(rnd, 0, PP, LPv)
+        gat("s", PX, xn, LB)
+        hot(10.0)
+        send(rnd, 1, PX, LXv)
+        bk = act(Bf(256), ind(U(0, A), LB))
+        h1 = act(Bf(16), Lb, fn.Relu, (1.0 - A) * 8192.0, 8192.0)
+        psb = wrap(bk, BDA, [(ID, h1)])
+        tt(PF, psb, AWB, op.is_equal)
+        send(rnd, 2, PF, LFv)
+        for c in range(3):
+            lo, hi = A * c, A * (c + 1)
+            cast(CFG["u4"][3 * rnd + c], sub(cb0, lo, hi), U(lo, hi))
+            ps = wrap(sub(cb0, lo, hi), BDA)
+            if c < 2:
+                act(sub(L4, 72 * c, 72 * (c + 1)), ps, None, -OFA)
+            else:
+                ts(sub(L4u, 72 * c, 72 * (c + 1)), ps, -OFA, op.add)
+        if last:
+            for c in range(9):
+                lo, hi = 384 * c, 384 * (c + 1)
+                ps = big(384)
+                if CFG["mod"][c] == "v":
+                    ts(ps, U(lo, hi), MAGIC, op.add, -MAGIC, op.add)
+                else:
+                    act(ps, U(lo, hi), None, MAGIC)
+                    act(ps, ps, None, -MAGIC)
+                tt(t("DR", DM + lo, DM + hi), U(lo, hi), ps, op.subtract)
+                act(t("DR", DM + lo, DM + hi), t("DR", DM + lo, DM + hi), None, 7.5)
+            dma("y", lambda q, T, x: q.dma_start(T["yp"][:, 2 * A:3 * A], T["DR"][:, DM + 2 * A:DM + 3 * A]), [t("DR", DM + 2 * A, DM + 3 * A)], [], 3.0)
+            gat("s", t("SV", 256, 512), t("RHO", DM, DM + A), LB)
+            act(t("SV", 0, 256), t("SV", 256, 512), None, float(A))
+            SVb = Bf(512)
+            gat("s", sub(SVb, 0, 256), t("DR", DM + A, DM + 2 * A), LB)
+        else:
+            gat("s", t("SV", 0, 256), U(A, 2 * A), LB)
+            ps = big(256)
+            mm([(ps, [(ID, sub(FBv, 3 * A, P)), (ID, PP), (ID, LPv)])])
+            act(t("SV", 256, 512), ps)
+        dl = tt(F(72), sub(L4, 72, 144), sub(L4, 0, 72), op.subtract)
+        psq = bank(48)
+        mm([(sub(psq, 0, 16), [(IDF, Lb), (BI, PF), (BI, LFv)]), (sub(psq, 16, 32), [(IDF, Lb), (ID, CA), (BI, PF), (BI, LFv)]),
+            (sub(psq, 32, 48), [(ID, sub(P16, 0, 16)), (NBI, PF), (NBI, LFv)])])
+        Q2 = tt(F(32), sub(psq, 0, 32), KK, op.max)
+        LQ = ts(U16(32), Q2, DM - 2 * BIG, op.add)
+        LK = ts(U16(16), sub(psq, 32, 48), iBB, op.add, 256.0, op.min)
+        lpw = t("LP%d" % rnd, 0, B + 16)
+        mk = "CB5" if last else "DR"
+        if last:
+            fill(t("CB5", 0, 832), 0)
+            fill(t("CB5", 832, DM + A), 0)
+        cp(ind(t(mk, 0, DM + A), sub(LQ, 0, 16)), DS)
+        ps = wrap(t(mk, DM, DM + A), BD)
+        m1 = ts(F(72), ps, 0.5, op.is_gt)
+        m2 = tt(F(72), m1, dl, op.mult)
+        L5 = F(144)
+        tt(sub(L5, 0, 72), sub(L4, 0, 72), m2, op.add)
+        tt(sub(L5, 72, 144), sub(L4, 72, 144), m2, op.subtract)
+        cp(sub(L4u, 0, 144), L5)
+        if not last:
+            ts(t("DR", DM + A, DM + 2 * A), t("DR", DM, DM + A), -1.0, op.mult)
+            cp(ind(t("U4", 0, DM + 2 * A), LQ), t("SV", 0, 512))
+            cp(ind(t(Xn, 0, DM + A), sub(LQ, 0, 16)), LXv)
+            for k, (lo, hi) in enumerate(((0, 38), (38, 74), (74, 98), (98, 122), (122, 144), (216, 232), (144, 168), (168, 192), (192, 216))):
+                if CFG["rn"][k] == "v":
+                    tt(W(oU + 16 * lo, oU + 16 * hi), ind(t("DR", DM, DM + P), sub(L4u, lo, hi)), U(16 * lo, 16 * hi), op.add)
+                else:
+                    d = gat("s", t("CB1", A + 384 * (k % 3), A + 384 * (k % 3) + 16 * (hi - lo)), t("DR", DM, DM + P), sub(L4u, lo, hi))
+                    ps = big(16 * (hi - lo))
+                    mm([(ps, [(IDF, U(16 * lo, 16 * hi)), (ID, d)])])
+                    act(W(oU + 16 * lo, oU + 16 * hi), ps)
+            Lw = Lw1
+            for c in range(2):
+                gat("s", t("CB1", 576 * c, 576 * (c + 1)), t("DR", DM, DM + P), sub(L4u, 36 * c, 36 * (c + 1)))
+            ps = wrap(t("CB1", 0, A), BDA, [(IDF, sub(L5, 0, 72))])
+            cp(sub(Lw, 0, 72), ps)
+            tt(W(oU + 3 * A, oU + P), ind(lpw, LK), W(oU + 3 * A, oU + P), op.add)
+            cb5 = t("CB5", 0, 2560)
+            cast("g", cb5, W(oU + A, oU + P))
+            ps = wrap(cb5, BDA)
+            act(sub(Lw, 72, 232), ps, None, -OFA)
+        else:
+            cp(ind(t("RHO", 0, DM + 2 * A), LQ), t("SV", 0, 512))
+            for k, (lo, hi) in enumerate(((144, 188), (188, 232), (0, 48), (48, 96), (96, 144))):
+                gat(CFG["yl"][k], W(oF + 16 * lo, oF + 16 * hi), t("RHO", DM, DM + P), sub(L4u, lo, hi))
+            dma("y", lambda q, T, x: q.dma_start(T["yl"][:, 2 * A:P], T["W"][0:128:16, oF + 2 * A:oF + P]), [W(oF + 2 * A, oF + P)], [], 2.2)
+            dma("y", lambda q, T, x: q.dma_start(T["yl"][:, 0:2 * A], T["W"][0:128:16, oF:oF + 2 * A]), [W(oF, oF + 2 * A)], [], 2.2)
+            tt(pi1, ind(lpw, LK), PP, op.add)
+            ts(pi2, pi1, 15, op.bitwise_and)
+            cp(sub(SVb, 256, 512), pi2)
+            dma("y", lambda q, T, x: q.dma_start(T["yp"][:, 3 * A:P], ap(T, sub(SVb, 256, 512))), [sub(SVb, 256, 512)], [], 2.2)
+            cp(ind(t("DR", 0, DM + 2 * A), LQ), SVb)
+            dma("y", lambda q, T, x: q.dma_start(T["yp"][:, 0:2 * A], T["DR"][:, DM:DM + 2 * A]), [t("DR", DM, DM + 2 * A)], [], 3.5)
+            cp(ind(t(Xn, 0, DM + A), sub(LQ, 0, 16)), LXv)
+            dma("y", lambda q, T, x: q.dma_start(T["yx"][:, :], ap(T, xn)), [xn], [], 3.0)
+    assert top["dma"] <= NDMA
+    return ops
+
+
+def hit(a, b):
+    for n, lo, hi in a:
+        for m, l2, h2 in b:
+            if n == m and lo < h2 and l2 < hi:
+                return True
+    return False
+
+
+def schedule(ops, costs):
+    n = len(ops)
+    anc, pre = [], []
+    for j, o in enumerate(ops):
+        pj = [r for r in o["rd"] if r[0].startswith("PS")]
+        o["dep"] = [i for i in range(j) if hit(ops[i]["wr"], o["rd"]) or hit(ops[i]["wr"], o["wr"]) or hit(ops[i]["rd"], o["wr"])
+                    or (pj and ops[i]["eng"] != o["eng"] and hit(ops[i]["rd"], pj))]
+        m, keep = 0, []
+        for i in reversed(o["dep"]):
+            if not m >> i & 1:
+                keep.append((i, (HOP[0] if ops[i]["eng"] == o["eng"] else HOP[1]) + ops[i]["lat"]))
+                m |= anc[i] | 1 << i
+        anc.append(0 if o["kind"] == "a" else m)
+        pre.append(keep)
+    eng = [o["eng"] for o in ops]
+    lat = [o["lat"] for o in ops]
+    suc = [[] for o in ops]
+    up = []
+    for j in range(n):
+        m = 1 << j
+        for i, h in pre[j]:
+            suc[i].append((j, h))
+            m |= up[i]
+        up.append(m)
+
+    def place(key, back=False):
+        busy, st, en = {e: [] for e in eng}, [0.0] * n, [0.0] * n
+        for j in sorted(range(n), key=lambda j: key[j]):
+            c = ops[j]["cost"]
+            s = lat[j] if back else 0.0
+            for i, h in (suc[j] if back else pre[j]):
+                if en[i] + h > s:
+                    s = en[i] + h
+            iv = busy[eng[j]]
+            k = len(iv)
+            while k > 0 and iv[k - 1][1] > s:
+                k -= 1
+            while k < len(iv) and s + c > iv[k][0]:
+                s = max(s, iv[k][1])
+                k += 1
+            iv.insert(k, (s, s + c))
+            st[j], en[j] = s, s + c
+        return [-v for v in en] if back else st
+
+    def judge(st):
+        tot = 0.0
+        seq = sorted(range(n), key=lambda j: (st[j], j))
+        for cost in costs:
+            free, en, last = {e: 0.0 for e in eng}, [0.0] * n, 0.0
+            for j in seq:
+                s = free[eng[j]]
+                for i, h in pre[j]:
+                    if en[i] + h > s:
+                        s = en[i] + h
+                en[j] = free[eng[j]] = s + cost[j]
+                last = max(last, en[j] + lat[j])
+            tot += last / sum(cost)
+        return tot
+
+    def ranks(bump):
+        rk = [0.0] * n
+        for j in range(n - 1, -1, -1):
+            rk[j] += ops[j]["cost"] + bump[j] + (lat[j] if rk[j] == 0.0 else 0.0)
+            for i, h in pre[j]:
+                rk[i] = max(rk[i], rk[j] + h)
+        return rk
+
+    def chain(st):
+        en = [st[j] + ops[j]["cost"] for j in range(n)]
+        prev, lastq = [None] * n, {}
+        for j in sorted(range(n), key=lambda j: (st[j], j)):
+            prev[j] = lastq.get(eng[j])
+            lastq[eng[j]] = j
+        j, out = max(range(n), key=lambda j: en[j] + lat[j]), []
+        while j is not None:
+            out.append(j)
+            c = [(en[i] + h, i) for i, h in pre[j]] + ([(en[prev[j]] - 0.001, prev[j])] if prev[j] is not None else [])
+            j = max(c)[1] if c else None
+        return out
+    seed = [SEED]
+
+    def rnd():
+        seed[0] = (seed[0] * 6364136223846793005 + 1442695040888963407) % 2 ** 64
+        return (seed[0] >> 11) / 2.0 ** 53
+    st = place([-v for v in ranks([o["bump"] for o in ops])])
+    cur = best = (judge(st), st)
+    crit = []
+    for k in range(ROUNDS):
+        if k % 20 == 0:
+            crit = chain(cur[1])
+        key = list(cur[1])
+        u = rnd()
+        if u < 0.03:
+            key = place([-key[j] - ops[j]["cost"] for j in range(n)], True)
+        else:
+            j = crit[int(rnd() * len(crit))] if u < 0.6 else int(rnd() * n)
+            d = 0.1 + rnd() ** 3 * 12.0
+            if rnd() < 0.7:
+                m = up[j]
+                key = [key[i] - d if m >> i & 1 else key[i] for i in range(n)]
+            else:
+                key = [key[i] + d if up[i] >> j & 1 else key[i] for i in range(n)]
+        st = place(key)
+        v = judge(st)
+        if v <= cur[0] + TEMP * (1.0 - k / ROUNDS) * rnd():
+            cur = (v, st)
+            if v < best[0]:
+                best = cur
+    for j, o in enumerate(ops):
+        o["start"] = best[1][j]
+        o["end"] = o["start"] + o["cost"] + o["lat"]
+    order = sorted(range(n), key=lambda j: (ops[j]["start"], j))
+    pos = {j: k for k, j in enumerate(order)}
+    seen = {}
+    for j in order:
+        o = ops[j]
+        need = {}
+        for i, h in pre[j]:
+            e = ops[i]
+            if o["kind"] == "a":
+                continue
+            key = e["sem"] if e["kind"] != "c" else "e" + e["eng"]
+            if key not in need or pos[i] > pos[need[key]]:
+                need[key] = i
+        o["wait"] = []
+        for key in sorted(need):
+            i = need[key]
+            if seen.get((o["eng"], key), -1) < pos[i]:
+                seen[(o["eng"], key)] = pos[i]
+                o["wait"].append((key, i))
+                ops[i]["sig"] = True
+    count = {}
+    for j in order:
+        o = ops[j]
+        if o["kind"] == "c" and o.get("sig"):
+            count[o["eng"]] = count.get(o["eng"], 0) + 1
+            o["val"] = count[o["eng"]]
+    return order, count
+
+
+PLAN = {}
+ROUNDS, SEED, HOP, TEMP = 20000, 1, (0.08, 0.15), 0.004
+
+
+def rank_program(g, core, T, topo):
+    rank = T.rank_of(core)
+    if rank is None:
+        return
+    if not PLAN:
+        PLAN["ops"] = build(1.56, 3.8)
+        costs = [[o["cost"] for o in build(a, b)] for a, b in ((1.56, 3.8), (1.15, 2.2), (1.95, 5.4))]
+        PLAN["order"], PLAN["count"] = schedule(PLAN["ops"], costs)
+    ops = PLAN["ops"]
+    x = {"pid": [], "rid": [], "mask": []}
+    ne = []
+    sent = 0
+    for rnd in range(RO):
+        peer = T.cores[rank ^ XM[rnd]]
+        rid, pid = topo.addr(peer, core)
+        x["pid"].append(pid)
+        x["rid"].append(rid)
+        x["mask"].append(topo.mask(core, peer))
+        ne.append(len(topo.engines(peer, core)))
+        sent += 3 * len(topo.engines(core, peer))
+    queue = {"v": g.vector, "s": g.scalar, "t": g.tensor, "g": g, "y": g.sync}
+
+    def full(e):
+        if e["kind"] == "c":
+            return e["val"]
+        if e["kind"] == "d":
+            return 16
+        return ne[int(e["sem"][2:]) // 3]
+    for j in PLAN["order"]:
+        o = ops[j]
+        if o["kind"] == "a":
+            continue
+        q = queue[o["eng"]]
+        for key, i in o["wait"]:
+            q.wait_ge(T.sem[key], full(ops[i]))
+        ins = o["f"](q, T, x)
+        if o["kind"] == "d":
+            ins.then_inc(T.sem[o["sem"]], 16)
+        elif o["kind"] == "c" and o.get("sig"):
+            ins.then_inc(T.sem["e" + o["eng"]], 1)
+    g.wait_ge(T.sem["sent"], sent)
+    for e in sorted(PLAN["count"]):
+        g.wait_ge(T.sem["e" + e], PLAN["count"][e])
+    for o in ops:
+        if o["kind"] in ("d", "a"):
+            g.wait_ge(T.sem[o["sem"]], full(o))

@@ -13,7 +13,7 @@ oFA, oF2, oT, oC, WEND = 9664, 10240, 10816, 11392, 11968
 DM = 512
 oXF = DM + A + 16
 POOL = {"SF": 5300, "SU": 2400, "SB": 8800, "SI": 600}
-CFG = {"xc": "vvv", "ll": "sssssv", "sh": "ggy", "rn": "vvvvsvsss", "up": "ss", "n1": "sss", "n2": "svv", "ld": "sss", "u4": "gssggs",
+CFG = {"xc": "vvv", "ll": "sssssv", "sh": "ggy", "rn": "vvvvsvsss", "up": "ss", "n1": "sss", "n2": "svv", "ld": "sss", "u4": "gsvggs",
        "u0": "svsvss", "mod": "vsvvvvvvv", "yl": "ssssv"}
 
 F32 = {"W": WEND, "V": 7168, "UP": 3 * A, "U4": DM + P, "IN1": 2 * A, "RHO": DM + P, "SV": 512, "SF": POOL["SF"]}
@@ -31,7 +31,7 @@ SEMAPHORES = ["ev", "es", "et", "eg", "sent"] + ["dm%d" % k for k in range(NDMA)
 
 op = AluOpType
 fn = ActivationFunctionType
-CY, PE = 0.00083 * 1.2, 0.000417 * 1.2
+CY, PE = 0.00083 * 1.1, 0.000417 * 1.1
 
 
 def sub(v, lo, hi, st=1):
@@ -70,7 +70,7 @@ def regs(vs):
 
 def build(GA, SC):
     ops = []
-    top = {"SF": 0, "SU": 0, "SB": 0, "SI": 0, "bank": 0, "big": 0, "dma": 0}
+    top = {"SF": 0, "SU": 0, "SB": 0, "SI": 0, "bank": 0, "big": 0, "dma": 0, "set": (3, 4, 5, 6, 7)}
 
     def new(pool, n):
         lo = top[pool]
@@ -95,7 +95,7 @@ def build(GA, SC):
 
     def bank(n):
         top["bank"] += 1
-        return ("PS%d" % (3 + top["bank"] % 5), 0, n, 1)
+        return ("PS%d" % top["set"][top["bank"] % len(top["set"])], 0, n, 1)
 
     def big(n):
         top["big"] += 1
@@ -185,8 +185,8 @@ def build(GA, SC):
         if eng == "g":
             dma("g", lambda q, T, x: q.dma_start(ap(T, out), ap(T, a)), [a], [out], 2.5 + cnt(out) * 0.0012)
         else:
-            act(sub(out, 0, 576), sub(a, 0, 576))
-            act(sub(out, 576, A), sub(a, 576, A))
+            for lo in (0, 576):
+                (act if eng == "s" else cp)(sub(out, lo, lo + 576), sub(a, lo, lo + 576))
 
     def twin(eng, out, a):
         if eng == "g":
@@ -244,6 +244,7 @@ def build(GA, SC):
     ID = sel(Bf(128), ONE, op.is_equal)
     NID = act(Bf(128), ID, None, 0.0, -1.0)
     IDF = act(F(128), ID)
+    NDF = act(F(128), ID, None, 0.0, -1.0)
     BI = act(Bf(128), ID, None, 0.0, BIG)
     NBI = act(Bf(128), ID, None, 0.0, -BIG)
     NPI = act(Bf(128), ID, None, 0.0, -float(P))
@@ -269,6 +270,8 @@ def build(GA, SC):
     AWB = act(F(16), sub(AW, 216, 232), None, OFA)
     KK = act(F(32), sub(AW, 0, 32), None, 2 * BIG - DM)
     CA = fill(Bf(16), A)
+    iR = act(F(1), i16, None, oFA - oU - 2 * A + 1 - 2 * OFA, -1.0)
+    C3 = fill(Bf(16), 3 * BIG)
     iP = act(F(1), i16, None, float(P))
     for xb in ("XA", "XB"):
         fill(t(xb, DM + A, oXF), C / 2)
@@ -301,7 +304,8 @@ def build(GA, SC):
     VW = (t("V", 0, P), t("V", 3 * A, 3 * A + P))
     VX = (t("V", A, 3 * A), t("V", 4 * A, 6 * A))
     CBS = (t("CB0", 0, P), t("CB1", 0, 2 * A))
-    Lw1 = F(232)
+    cb5 = t("CB5", 0, 2560)
+    Lw1, LC1 = F(232), U16(72)
     PAY = [(Bf(256), Bf(256), Bf(16)) for rnd in range(RO)]
     keep = (top["SF"], top["SB"], top["SU"])
 
@@ -310,9 +314,11 @@ def build(GA, SC):
         last = rnd == RO - 1
         Xc, Xn = ("XA", "XB") if rnd % 2 == 0 else ("XB", "XA")
         x = t(Xc, DM, DM + A)
+        top["set"] = (5, 6, 7)
         L = sub(Lw, 0, 72)
         thr = sub(TH, rnd, rnd + 1)
-        LC = ts(U16(72), L, float(A), op.min)
+        if rnd == 0:
+            LC = ts(U16(72), L, float(A), op.min)
         for k in range(3):
             lo, hi = 384 * k, 384 * (k + 1)
             lst = sub(LC, 24 * k, 24 * (k + 1))
@@ -331,14 +337,16 @@ def build(GA, SC):
         incf = scan(F(72), ONE, sub(psf, 0, 72), 0.0)
         rfx = tt(F(72), incf, sub(psf, 72, 144), op.add)
         nf = sub(incf, 71, 72)
-        nfi = ts(I32(1), nf, 0.5, op.mult, -0.25, op.add)
-        nfe = ts(F(1), nfi, 2.0, op.mult, -1.0, op.add)
+        nfh = act(F(1), nf, None, -0.25, 0.5)
+        nfi = act(F(1), nfh, None, MAGIC / 16)
+        nfj = act(F(1), nfi, None, -MAGIC / 16)
+        nfe = act(F(1), nfj, None, -1.0, 2.0)
         nfr = act(F(1), nfe, None, 2 * OFA)
         a1 = tt(F(72), aw, rfx, op.subtract)
         nfm = act(F(1), nf, None, -4095.0)
         a2 = act(F(72), a1, None, nfm)
         pf = tt(F(72), a2, rfx, op.min)
-        fc = act(F(72), L, None, f0)
+        fc = act(F(72), L, None, f0 - 1 + 2 * OFA)
         near = ts(Bf(72), psD, thr, op.is_lt)
         u2 = tt(Bf(72), psD, LTh, op.is_lt)
         nbb = act(Bf(72), psD, fn.Relu, -240.5 * 4096.0, 4096.0)
@@ -372,15 +380,15 @@ def build(GA, SC):
             ps = big(384)
             mm([(ps, [(NID, sub(FBv, A + 384 * k, A + 384 * (k + 1))), (ID, t("LL", 384 * (k % 3), 384 * (k % 3 + 1)))])])
             act(t("IN1", 384 * k, 384 * (k + 1)), ps)
-        E12, K12, S1, LS1 = F(144), F(144), F(144), U16(144)
-        act(sub(E12, 0, 72), e0, None, u0 + A)
+        E12, S1, LS1 = F(144), F(144), U16(144)
+        act(sub(E12, 0, 72), e0, None, u0 + A - 1 + 2 * OFA)
         act(sub(E12, 72, 144), e0, None, u0 + 2 * A - 1 + 2 * OFA)
-        tt(sub(K12, 0, 72), nd, fc, op.add)
-        tt(sub(K12, 72, 144), nd, r, op.add)
+        K12 = bank(144)
+        mm([(sub(K12, 0, 72), [(IDF, fc), (ID, nd)]), (sub(K12, 72, 144), [(IDF, r), (ID, nd)])])
         tt(S1, K12, E12, op.min)
-        cp(sub(LS1, 0, 72), sub(S1, 0, 72))
-        ts(sub(LS1, 72, 144), sub(S1, 72, 144), 1.0 - 2 * OFA, op.add)
+        ts(LS1, S1, 1.0 - 2 * OFA, op.add)
         JL = [U16(144) for k in range(4)]
+        top["set"] = (3, 4)
 
         def jlist(k, c):
             lo, hi = 768 * c, 768 * (c + 1)
@@ -397,6 +405,7 @@ def build(GA, SC):
                 tt(sub(VX[(k + 1) % 2], lo, hi), ind(VW[k % 2], sub(JL[k], 48 * c, 48 * (c + 1))), t("IN1", lo, hi), op.add)
                 if k < 3:
                     jlist(k + 1, c)
+        top["set"] = (5, 6, 7)
         UVb = Bf(576)
         act(sub(UVb, 0, 576, 2), W(oUL, oUL + 288))
         ps = wrap(sub(UVb, 0, 576, 2), BDA)
@@ -426,27 +435,28 @@ def build(GA, SC):
         n1 = act(F(1), sub(incc, 71, 72), None, 2 * 576.0 - 1.0, 2.0)
         n2 = ts(F(1), n1, nfe, op.min, 1.0 - 4095.0, op.add)
         g3 = ts(Bf(72), rfx, n2, op.is_ge, BIG, op.mult)
-        rm = tt(F(72), g3, a1, op.add)
-        cm = tt(F(72), k0a, nd, op.subtract)
-        r0 = tt(F(72), r, aw, op.subtract)
-        rd_ = tt(F(72), r0, nd, op.subtract)
+        ps = bank(216)
+        rm, cm, rd_ = sub(ps, 0, 72), sub(ps, 72, 144), sub(ps, 144, 216)
+        mm([(rm, [(IDF, a1), (ID, g3)]), (cm, [(IDF, k0a), (NID, nd)]), (rd_, [(IDF, r), (NID, sub(P16, 0, 72)), (NID, nd)])])
+        x1 = act(F(72), rm, fn.Relu, oXF - DM + 4095.0, -1.0)
         Ra, Rb = F(216), F(216)
         ps2 = bank(216)
         grp = []
-        for i, (src, k1, k2) in enumerate(((cm, A, oT - oU), (cm, P, oC - oU - A), (rd_, oFA - oU - 2 * A + 1 - 2 * OFA, oF2 - oU - 2 * A))):
+        for i, (src, k1, k2) in enumerate(((cm, float(A), oT - oU), (cm, float(P), oC - oU - A), (rd_, iR, oF2 - oU - 2 * A))):
             lo, hi = 72 * i, 72 * (i + 1)
-            act(sub(Ra, lo, hi), src, fn.Relu, float(k1))
+            act(sub(Ra, lo, hi), src, fn.Relu, k1)
             act(sub(Rb, lo, hi), rm, fn.Relu, k2 + 4095.0, -1.0)
             grp.append((sub(ps2, lo, hi), [(ID, sub(P16, lo, hi)), (NPI, nann), (IDF, sub(Ra, lo, hi)), (IDF, sub(Rb, lo, hi))]))
         mm(grp)
         LS2 = ts(U16(216), ps2, iP, op.add)
         hot(8.0)
         LP = U16(232)
-        ps3 = bank(144)
-        mm([(sub(ps3, 72 * i, 72 * (i + 1)), [(IDF, sub(Lw, 72 * (i + 1), 72 * (i + 2))), (BI, nann), (ID, nd), (ID, g3)]) for i in range(2)])
-        ts(sub(LP, 72, 216), ps3, -3 * BIG, op.add, 0.0, op.max)
-        cp(sub(LP, 216, 232), sub(Lw, 216, 232))
-        x1 = act(F(72), rm, fn.Relu, oXF - DM + 4095.0, -1.0)
+        if rnd:
+            act(sub(Lw, 72, 232), wrap(cb5, BDA), None, -OFA)
+        ps3 = bank(160)
+        mm([(sub(ps3, 72 * i, 72 * (i + 1)), [(IDF, sub(Lw, 72 * (i + 1), 72 * (i + 2))), (BI, nann), (ID, nd), (ID, g3)]) for i in range(2)]
+           + [(sub(ps3, 144, 160), [(IDF, sub(Lw, 216, 232)), (ID, C3)])])
+        ts(sub(LP, 72, 232), ps3, -3 * BIG, op.add, 0.0, op.max)
         ps = bank(72)
         mm([(ps, [(ID, sub(P16, 0, 72)), (IDF, x1)])])
         LX = ts(U16(72), ps, i16, op.add)
@@ -465,6 +475,7 @@ def build(GA, SC):
         tt(U4b, ind(VW[0], sub(LP, 216, 232)), W(oU + 3 * A, oU + P), op.add)
         for c in range(6):
             tt(U(576 * c, 576 * (c + 1)), ind(VW[0], sub(LP, 36 * c, 36 * (c + 1))), t("UP", 576 * c, 576 * (c + 1)), op.add)
+        top["set"] = (3, 4, 5, 6, 7)
         L4 = F(232)
         L4u = U16(232)
         cb0 = CBS[0]
@@ -476,13 +487,12 @@ def build(GA, SC):
         PP, PX, PF = PAY[rnd]
         if last:
             pi1, pi2 = I32(256), I32(256)
-            cp(pi1, U4b)
-            ts(pi2, pi1, 15, op.bitwise_and)
-            cp(PP, pi2)
-        else:
-            ps = big(256)
-            mm([(ps, [(IDF, U4b), (NID, sub(cb0, 3 * A, P))])])
-            act(PP, ps)
+            pr = act(F(256), U4b, None, -7.5)
+            act(pr, pr, None, MAGIC)
+            act(pr, pr, None, MAGIC, -1.0)
+        ps = big(256)
+        mm([(ps, [(IDF, U4b), (IDF, pr) if last else (NID, sub(cb0, 3 * A, P))])])
+        act(PP, ps)
         LPv, LXv, LFv = t("LP%d" % rnd, 0, B), t("LX%d" % rnd, 0, B), t("LF%d" % rnd, 0, 16)
         send(rnd, 0, PP, LPv)
         gat("s", PX, xn, LB)
@@ -522,7 +532,9 @@ def build(GA, SC):
             ps = big(256)
             mm([(ps, [(ID, sub(FBv, 3 * A, P)), (ID, PP), (ID, LPv)])])
             act(t("SV", 256, 512), ps)
-        dl = tt(F(72), sub(L4, 72, 144), sub(L4, 0, 72), op.subtract)
+        ps = bank(72)
+        mm([(ps, [(IDF, sub(L4, 72, 144)), (NDF, sub(L4, 0, 72))])])
+        dl = act(F(72), ps)
         psq = bank(48)
         mm([(sub(psq, 0, 16), [(IDF, Lb), (BI, PF), (BI, LFv)]), (sub(psq, 16, 32), [(IDF, Lb), (ID, CA), (BI, PF), (BI, LFv)]),
             (sub(psq, 32, 48), [(ID, sub(P16, 0, 16)), (NBI, PF), (NBI, LFv)])])
@@ -538,10 +550,9 @@ def build(GA, SC):
         ps = wrap(t(mk, DM, DM + A), BD)
         m1 = ts(F(72), ps, 0.5, op.is_gt)
         m2 = tt(F(72), m1, dl, op.mult)
-        L5 = F(144)
-        tt(sub(L5, 0, 72), sub(L4, 0, 72), m2, op.add)
-        tt(sub(L5, 72, 144), sub(L4, 72, 144), m2, op.subtract)
-        cp(sub(L4u, 0, 144), L5)
+        ps = bank(144)
+        mm([(sub(ps, 0, 72), [(IDF, sub(L4, 0, 72)), (IDF, m2)]), (sub(ps, 72, 144), [(IDF, sub(L4, 72, 144)), (NDF, m2)])])
+        cp(sub(L4u, 0, 144), ps)
         if not last:
             ts(t("DR", DM + A, DM + 2 * A), t("DR", DM, DM + A), -1.0, op.mult)
             cp(ind(t("U4", 0, DM + 2 * A), LQ), t("SV", 0, 512))
@@ -550,20 +561,19 @@ def build(GA, SC):
                 if CFG["rn"][k] == "v":
                     tt(W(oU + 16 * lo, oU + 16 * hi), ind(t("DR", DM, DM + P), sub(L4u, lo, hi)), U(16 * lo, 16 * hi), op.add)
                 else:
-                    d = gat("s", t("CB1", A + 384 * (k % 3), A + 384 * (k % 3) + 16 * (hi - lo)), t("DR", DM, DM + P), sub(L4u, lo, hi))
-                    ps = big(16 * (hi - lo))
+                    d = gat("s", sub(cb0, 16 * lo, 16 * hi), t("DR", DM, DM + P), sub(L4u, lo, hi))
+                    ps = ("PS%d" % (3 + k % 2), 0, 16 * (hi - lo), 1)
                     mm([(ps, [(IDF, U(16 * lo, 16 * hi)), (ID, d)])])
                     act(W(oU + 16 * lo, oU + 16 * hi), ps)
             Lw = Lw1
             for c in range(2):
                 gat("s", t("CB1", 576 * c, 576 * (c + 1)), t("DR", DM, DM + P), sub(L4u, 36 * c, 36 * (c + 1)))
-            ps = wrap(t("CB1", 0, A), BDA, [(IDF, sub(L5, 0, 72))])
-            cp(sub(Lw, 0, 72), ps)
+            top["set"] = (5,)
+            ps = wrap(t("CB1", 0, A), BDA, [(IDF, sub(L4, 0, 72)), (IDF, m2)])
+            LC = ts(LC1, ps, float(A), op.min)
+            act(sub(Lw, 0, 72), ps)
             tt(W(oU + 3 * A, oU + P), ind(lpw, LK), W(oU + 3 * A, oU + P), op.add)
-            cb5 = t("CB5", 0, 2560)
             cast("g", cb5, W(oU + A, oU + P))
-            ps = wrap(cb5, BDA)
-            act(sub(Lw, 72, 232), ps, None, -OFA)
         else:
             cp(ind(t("RHO", 0, DM + 2 * A), LQ), t("SV", 0, 512))
             for k, (lo, hi) in enumerate(((144, 188), (188, 232), (0, 48), (48, 96), (96, 144))):
@@ -731,7 +741,7 @@ def schedule(ops, costs):
 
 
 PLAN = {}
-ROUNDS, SEED, HOP, TEMP = 20000, 1, (0.08, 0.15), 0.004
+ROUNDS, SEED, HOP, TEMP = 24000, 1, (0.08, 0.15), 0.003
 
 
 def rank_program(g, core, T, topo):
@@ -740,7 +750,7 @@ def rank_program(g, core, T, topo):
         return
     if not PLAN:
         PLAN["ops"] = build(1.56, 3.8)
-        costs = [[o["cost"] for o in build(a, b)] for a, b in ((1.56, 3.8), (1.15, 2.2), (1.95, 5.4))]
+        costs = [[o["cost"] for o in build(a, b)] for a, b in ((1.3, 2.7), (1.8, 4.9))]
         PLAN["order"], PLAN["count"] = schedule(PLAN["ops"], costs)
     ops = PLAN["ops"]
     x = {"pid": [], "rid": [], "mask": []}

@@ -8,17 +8,18 @@ OFA = 65.0 * 128.0
 OFF = 65.0 * 192.0
 MAGIC = 1.5 * 2.0 ** 27
 BIG = 16384.0
-oUL, oFL, oD, oU, oF = 0, 576, 1728, 2240, 5952
-oFA, oF2, oT, oC, WEND = 9664, 10240, 10816, 11392, 11968
+oUL, oFL, oD, oU, oF = 0, 576, 1728, 2880, 6592
+oF2, oT, oC, WEND = 10304, 10880, 11456, 12032
 DM = 512
 oXF = DM + A + 16
 POOL = {"SF": 5300, "SU": 2400, "SB": 8800, "SI": 600}
-CFG = {"xc": "vvv", "ll": "sssssv", "sh": "ggy", "rn": "vvvvsvsss", "up": "ss", "n1": "sss", "n2": "svv", "ld": "sss", "u4": "gsvggs",
-       "u0": "svsvss", "mod": "vsvvvvvvv", "yl": "ssssv"}
+CFG = {"xc": "vvsvvs", "ll": "ssssss", "sh": ("ggs",) * 8, "rn": "vvddevdde", "up": "tg", "g2": "ssssss", "u4": "gsgggs",
+       "u0": "svsvss", "mod": "tAbaABaAb", "yl": "ssssv", "lc": "s", "in1": "eded", "ch": (0, 48, 96, 144),
+       "jl": ("sss",) * 8, "tb": "ggggg", "pi": "t"}
 
-F32 = {"W": WEND, "V": 7168, "UP": 3 * A, "U4": DM + P, "IN1": 2 * A, "RHO": DM + P, "SV": 512, "SF": POOL["SF"]}
+F32 = {"W": WEND, "V": 7184, "UP": 3 * A, "U4": DM + P, "IN1": 2 * A, "RHO": DM + P, "SV": 512, "SF": POOL["SF"]}
 TWO = {"FB": P, "CB0": P, "CB1": 2 * A, "CB5": 2560, "DR": DM + P, "XA": oXF + 576, "XB": oXF + 576, "XC": A, "LL": A, "DIF": A + 16,
-       "N1": A + 16, "SB": POOL["SB"], "LP0": B + 16, "LP1": B + 16, "LX0": B, "LX1": B, "LF0": 16, "LF1": 16}
+       "SB": POOL["SB"], "LP0": B + 16, "LP1": B + 16, "LX0": B, "LX1": B, "LF0": 16, "LF1": 16}
 I32S = {"XI": A + 16, "LKI": 232, "THI": 2, "SI": POOL["SI"]}
 SCRATCH = {"SU": ("sbuf", [128, POOL["SU"]], "uint16")}
 SCRATCH.update({k: ("sbuf", [128, v], "float32") for k, v in F32.items()})
@@ -26,7 +27,7 @@ SCRATCH.update({k: ("sbuf", [128, v], "bfloat16") for k, v in TWO.items()})
 SCRATCH.update({k: ("sbuf", [128, v], "int32") for k, v in I32S.items()})
 SCRATCH.update({"PS%d" % k: ("psum", [128, 512], "float32") for k in range(8)})
 
-NDMA = 44
+NDMA = 64
 SEMAPHORES = ["ev", "es", "et", "eg", "sent"] + ["dm%d" % k for k in range(NDMA)] + ["ar%d" % k for k in range(3 * RO)]
 
 op = AluOpType
@@ -68,7 +69,7 @@ def regs(vs):
     return out
 
 
-def build(GA, SC):
+def build(GA, SC, PE=PE):
     ops = []
     top = {"SF": 0, "SU": 0, "SB": 0, "SI": 0, "bank": 0, "big": 0, "dma": 0, "set": (3, 4, 5, 6, 7)}
 
@@ -188,19 +189,31 @@ def build(GA, SC):
             for lo in (0, 576):
                 (act if eng == "s" else cp)(sub(out, lo, lo + 576), sub(a, lo, lo + 576))
 
+    def accum(out, a):
+        dma("g", lambda q, T, x: q.dma_start(ap(T, out), ap(T, a), accum_op=op.add), [a, out], [out], 2.5 + cnt(out) * (0.001 if out[0] in TWO else 0.002))
+
     def twin(eng, out, a):
         if eng == "g":
             add("g", lambda q, T, x: q.affine_select(ap(T, out), ap(T, a), [[0, cnt(a)]], op.is_ge, 0.0, 0, 0), [a], [out], 0.17 + 2 * cnt(a) * CY)
         elif eng == "s":
             act(out, a)
+        elif eng == "v":
+            cp(out, a)
         else:
-            dma("y", lambda q, T, x: q.dma_start(ap(T, out), ap(T, a)), [a], [out], 3.2)
+            dma("y", lambda q, T, x: q.dma_start(ap(T, out), ap(T, a)), [a], [out], 2.0 + cnt(a) * 0.0016)
+
+    def mod16(ps, parts, shifted=False):
+        one = sub(ONES, 0, cnt(ps))
+        neg = [(NDF if v[0] not in TWO else NID, v) for v in parts]
+        pos = [(IDF if v[0] not in TWO else ID, v) for v in parts]
+        mm([(ps, ([] if shifted else [(I75, one)]) + neg + [(NM, one), (IM, one)] + pos + ([(I75, one)] if shifted else []))])
+        return ps
 
     def send(rnd, k, src, dst):
         s = "ar%d" % (3 * rnd + k)
         tok = ("tok%d" % (3 * rnd + k), 0, 1, 1)
         add("g", lambda q, T, x: q.remote_dma(ap(T, dst), ap(T, src), T.sem[s], T.sem["sent"], x["pid"][rnd], x["rid"][rnd], x["mask"][rnd]),
-            [src], [tok], 0.6, "r")
+            [src] + ([("tok0", 0, 1, 1)] if rnd == 0 and k else []), [tok], 0.6 if rnd or k else 2.5, "r")
         add("n", None, [tok], [dst], 0.01, "a", 4.5 + cnt(src) * 0.006, s)
 
     F, Bf, U16, I32 = (lambda n: new("SF", n)), (lambda n: new("SB", n)), (lambda n: new("SU", n)), (lambda n: new("SI", n))
@@ -238,18 +251,23 @@ def build(GA, SC):
     w1 = ts(F(1), i16, 1.0, op.is_equal, w0, op.add)
     BD = ts(Bf(144), ROW, g15, op.is_equal, w1, op.mult)
     BDA = act(Bf(144), BD, None, 0.0, 1.0 / C)
-    BD2 = act(Bf(144), BD, None, 0.0, 2.0 / C)
     BS = ts(Bf(144), ROW, g15, op.is_equal)
     ONE = fill(Bf(128), 1)
     ID = sel(Bf(128), ONE, op.is_equal)
-    NID = act(Bf(128), ID, None, 0.0, -1.0)
-    IDF = act(F(128), ID)
-    NDF = act(F(128), ID, None, 0.0, -1.0)
-    BI = act(Bf(128), ID, None, 0.0, BIG)
-    NBI = act(Bf(128), ID, None, 0.0, -BIG)
-    NPI = act(Bf(128), ID, None, 0.0, -float(P))
-    N8 = act(Bf(128), ID, None, 0.0, -8.0)
-    N4 = act(Bf(128), ID, None, 0.0, -4096.0)
+
+    def diag(out, v, eng="g"):
+        if eng == "s":
+            return act(out, ID, None, 0.0, v)
+        add("g", lambda q, T, x: q.affine_select(ap(T, out), ap(T, ID), [[-1, 128]], op.not_equal, v, 0, 1), [ID], [out], 0.17 + 256 * CY)
+        return out
+    NID, IDF, BI = diag(Bf(128), -1.0, "s"), diag(F(128), 1.0), diag(Bf(128), BIG)
+    NDF, NBI, NPI = diag(F(128), -1.0), diag(Bf(128), -BIG), diag(Bf(128), -float(P))
+    IM, NM, I75, N75 = diag(Bf(128), MAGIC), diag(Bf(128), -MAGIC), diag(Bf(128), 7.5), diag(Bf(128), -7.5)
+    ONES = fill(Bf(384), 1)
+    BDF = act(F(144), BD, None, 0.0, 1.0 / C)
+    ifr = act(F(1), i16, None, -0.491)
+    ifg = act(F(1), i16, None, -0.3)
+    N4 = diag(Bf(128), -4096.0)
     ps = bank(128)
     mm([(ps, [(ID, sub(BS, 15 - i, 143 - i)) for i in range(16)])])
     BO = act(Bf(128), ps)
@@ -269,27 +287,33 @@ def build(GA, SC):
     BA = act(F(72), aw, None, f0 - u0)
     AWB = act(F(16), sub(AW, 216, 232), None, OFA)
     KK = act(F(32), sub(AW, 0, 32), None, 2 * BIG - DM)
-    CA = fill(Bf(16), A)
-    iR = act(F(1), i16, None, oFA - oU - 2 * A + 1 - 2 * OFA, -1.0)
-    C3 = fill(Bf(16), 3 * BIG)
+    CA = Bf(48)
+    fill(sub(CA, 0, 16), 0)
+    fill(sub(CA, 16, 32), A)
+    iota(sub(CA, 32, 48), [[16, 16]], 0, 0)
+    P4 = diag(Bf(128), 4096.0)
+    BOH = act(F(128), BO, None, 0.0, 0.5)
+    CN = fill(Bf(72), -BIG)
+    act(t("V", 3 * A + P, 3 * A + P + 16), sub(ROW, 0, 16), None, sub(EC, 36, 37), 0.0)
     iP = act(F(1), i16, None, float(P))
     for xb in ("XA", "XB"):
         fill(t(xb, DM + A, oXF), C / 2)
     fill(t("XI", A, A + 16), C / 2)
     fill(t("DIF", A, A + 16), 0)
-    fill(t("N1", A, A + 16), Z + 40 * C)
     fill(W(0, oFL), Z)
-    fill(W(oFL, oD), Z)
-    for lo, hi in ((0, 576), (576, A), (3 * A, 3 * A + 256), (3 * A + 256, 4 * A), (6 * A, 6 * A + 256)):
-        fill(t("V", lo, hi), 0)
+    twin("y", W(oFL, oFL + 576), W(0, oFL))
+    twin("y", W(oFL + 576, oD), W(0, oFL))
+    fill(t("V", 0, 576), 0)
+    for lo, hi in ((576, A), (3 * A, 3 * A + 576), (3 * A + 576, 4 * A), (6 * A, 6 * A + 256)):
+        twin("y", t("V", lo, hi), t("V", 0, hi - lo))
     for rnd in range(RO):
         fill(t("LP%d" % rnd, B, B + 16), 0)
-    fill(W(oD, oU), 0)
-    fill(t("U4", 0, DM), 0)
+    twin("y", t("U4", 0, DM), t("V", 0, DM))
+    fill(t("DR", 0, 832), 0)
     for xb in ("XA", "XB"):
-        fill(t(xb, 0, DM), 0)
-    for lo, hi in ((0, 832), (832, DM + A), (DM + 2 * A, DM + 2 * A + 704), (DM + 2 * A + 704, DM + P)):
-        fill(t("DR", lo, hi), 0)
+        twin("y", t(xb, 0, DM), t("DR", 0, DM))
+    for lo, hi in ((832, DM + A), (DM + 2 * A, DM + 2 * A + 704), (DM + 2 * A + 704, DM + P)):
+        twin("y", t("DR", lo, hi), t("DR", 0, hi - lo))
     DS = act(Bf(256), sub(FBv, 0, 256), None, sub(EC, 18, 19), 0.0)
     for k in range(6):
         iota(t("RHO", k * 704, (k + 1) * 704), [[1, 704]], k * 704 - DM, 0)
@@ -301,8 +325,10 @@ def build(GA, SC):
     cp(t("XA", DM, DM + 576), t("XI", 0, 576))
     cp(t("XA", DM + 576, DM + A), t("XI", 576, A))
 
-    VW = (t("V", 0, P), t("V", 3 * A, 3 * A + P))
-    VX = (t("V", A, 3 * A), t("V", 4 * A, 6 * A))
+    VW = (t("V", 3 * A, 3 * A + P), t("V", 0, P))
+    VX = (t("V", 4 * A, 6 * A), t("V", A, 3 * A))
+    VF = t("V", 3 * A, 3 * A + P + 16)
+    CH = CFG["ch"]
     CBS = (t("CB0", 0, P), t("CB1", 0, 2 * A))
     cb5 = t("CB5", 0, 2560)
     Lw1, LC1 = F(232), U16(72)
@@ -322,12 +348,15 @@ def build(GA, SC):
         for k in range(3):
             lo, hi = 384 * k, 384 * (k + 1)
             lst = sub(LC, 24 * k, 24 * (k + 1))
-            gat(CFG["xc"][k], t("XC", lo, hi), t(Xc, DM, oXF) if rnd else t("XI", 0, A + 16), lst)
+            e = CFG["xc"][3 * rnd + k]
+            gat(e, t("XC", lo, hi), t(Xc, DM, oXF) if rnd or e == "s" else t("XI", 0, A + 16), lst)
             gat(CFG["ll"][3 * rnd + k], t("LL", lo, hi), W(oU, oU + A + 16), lst)
             ps = big(384)
             mm([(ps, [(NID, sub(FBv, lo, hi)), (NID, sub(x, lo, hi))])], True, False)
             mm([(ps, [(ID, t("XC", lo, hi)), (ID, t("LL", lo, hi))])], False, True)
             act(t("DIF", lo, hi), ps, fn.Abs)
+        if rnd:
+            later()
         psD = wrap(t("DIF", 0, A), BS)
         k0a = tt(F(72), L, aw, op.subtract)
         free = ts(Bf(72), k0a, 0.0, op.is_equal)
@@ -341,73 +370,98 @@ def build(GA, SC):
         nfi = act(F(1), nfh, None, MAGIC / 16)
         nfj = act(F(1), nfi, None, -MAGIC / 16)
         nfe = act(F(1), nfj, None, -1.0, 2.0)
-        nfr = act(F(1), nfe, None, 2 * OFA)
+        nfb = act(F(1), nfj, None, 576.5, -1.0)
+        mn = tt(F(72), L, aw, op.min)
         a1 = tt(F(72), aw, rfx, op.subtract)
         nfm = act(F(1), nf, None, -4095.0)
         a2 = act(F(72), a1, None, nfm)
         pf = tt(F(72), a2, rfx, op.min)
-        fc = act(F(72), L, None, f0 - 1 + 2 * OFA)
+        fc = act(F(72), L, None, f0 - u0)
         near = ts(Bf(72), psD, thr, op.is_lt)
         u2 = tt(Bf(72), psD, LTh, op.is_lt)
         nbb = act(Bf(72), psD, fn.Relu, -240.5 * 4096.0, 4096.0)
         cand = tt(Bf(72), u2, near, op.is_gt)
         nann = tt(Bf(72), near, free, op.is_le)
-        psc = bank(144)
-        mm([(sub(psc, 0, 72), [(BO, cand)]), (sub(psc, 72, 144), [(TRC, cand)])])
+        psc = bank(216)
+        mm([(sub(psc, 0, 72), [(BO, cand)]), (sub(psc, 72, 144), [(TRC, cand)]), (sub(psc, 144, 216), [(NID, cand), (TRC, cand), (P4, cand)])])
         incc = scan(F(72), ONE, sub(psc, 0, 72), -576.0)
         rcx = tt(F(72), incc, sub(psc, 72, 144), op.add)
-        LN = ts(U16(72), rcx, 4671.0, op.add, 1000.0, op.min)
         pm = tt(F(72), rcx, pf, op.min)
         LS = ts(U16(72), pm, 4671.0, op.add)
         for k in range(3):
             cp(ind(W(0, oD), sub(LS, 24 * k, 24 * (k + 1))), sub(FBv, 384 * k, 384 * (k + 1)))
+        rca = tt(F(72), incc, sub(psc, 144, 216), op.add)
+        sg, acc = F(72), F(1)
+        add("s", lambda q, T, x, sg=sg, rca=rca, nfb=nfb, acc=acc: q.activation(ap(T, sg), ap(T, rca), fn.Sign, ap(T, nfb), 1.0, accum_out=ap(T, acc)),
+            [rca, nfb], [sg, acc], 0.09 + 72 * CY)
+        ps = bank(2)
+        mm([(sub(ps, 0, 1), [(BOH, acc)])])
+        lim = act(F(1), sub(ps, 0, 1), None, 576.0, -1.0)
+        ps = bank(72)
+        mm([(ps, [(IDF, mn), (BI, near), (ID, nbb), (BI, free)])])
+        nd = ts(Bf(72), ps, lim, op.is_ge, BIG, op.mult)
+        rc2 = act(F(72), rcx, None, 2 * 4671.0, 2.0)
+        LG = ts(U16(72), rc2, 1.0, op.add, A - 1.0, op.min)
         for k in range(3):
-            gat(CFG["n1"][k], t("N1", 384 * k, 384 * (k + 1)), t("FB", 0, 1008), sub(LN, 24 * k, 24 * (k + 1)))
-        for k in range(3):
-            gat(CFG["n2"][k], t("XC", 384 * k, 384 * (k + 1)), t("N1", 0, A + 16), sub(LC, 24 * k, 24 * (k + 1)))
-        psN = wrap(t("XC", 0, A), BD2, [(ID, nbb)])
-        rc2 = act(F(72), rcx, None, 2 * (4671.0 + OFA) - 1.0, 2.0)
-        r = tt(F(72), psN, rc2, op.min)
-        nd = ts(Bf(72), r, nfr, op.is_ge, BIG, op.mult)
+            gat(CFG["g2"][3 * rnd + k], W(oD + 384 * k, oD + 384 * (k + 1)), W(oFL, oD), sub(LG, 24 * k, 24 * (k + 1)))
+        r = tt(F(72), rc2, act(F(72), L, None, float(oD - oFL)), op.min)
         pse = bank(144)
         mm([(sub(pse, 0, 72), [(ID, sub(P16, 0, 72)), (BI, nann)]), (sub(pse, 72, 144), [(IDF, L), (BI, nann)])])
         LD = ts(U16(72), sub(pse, 0, 72), i16, op.add, float(A), op.min)
         hot(5.0)
         e0 = tt(F(72), sub(pse, 72, 144), BA, op.min)
         for k in range(3):
-            gat(CFG["ld"][k], t("LL", 384 * k, 384 * (k + 1)), t("DIF", 0, A + 16), sub(LD, 24 * k, 24 * (k + 1)))
-        for k in range(6):
-            ps = big(384)
-            mm([(ps, [(NID, sub(FBv, A + 384 * k, A + 384 * (k + 1))), (ID, t("LL", 384 * (k % 3), 384 * (k % 3 + 1)))])])
-            act(t("IN1", 384 * k, 384 * (k + 1)), ps)
+            act(t("LL", 384 * k, 384 * (k + 1)), ind(t("DIF", 0, A + 16), sub(LD, 24 * k, 24 * (k + 1))), None, 0.0, -1.0)
+        for i in range(2):
+            if CFG["in1"][2 * rnd + i] == "d":
+                if rnd:
+                    twin("y", t("IN1", i * A, (i + 1) * A), W(oF + (i + 1) * A, oF + (i + 2) * A))
+                else:
+                    cast("g", t("IN1", i * A, (i + 1) * A), sub(FBv, (i + 1) * A, (i + 2) * A))
+                accum(t("IN1", i * A, (i + 1) * A), t("LL", 0, A))
+            else:
+                for k in range(3 * i, 3 * i + 3):
+                    ps = big(384)
+                    mm([(ps, [(ID, sub(FBv, A + 384 * k, A + 384 * (k + 1))), (ID, t("LL", 384 * (k % 3), 384 * (k % 3 + 1)))])])
+                    act(t("IN1", 384 * k, 384 * (k + 1)), ps)
         E12, S1, LS1 = F(144), F(144), U16(144)
-        act(sub(E12, 0, 72), e0, None, u0 + A - 1 + 2 * OFA)
-        act(sub(E12, 72, 144), e0, None, u0 + 2 * A - 1 + 2 * OFA)
+        act(sub(E12, 0, 72), e0, None, float(A))
+        act(sub(E12, 72, 144), e0, None, u0 + 2 * A)
         K12 = bank(144)
         mm([(sub(K12, 0, 72), [(IDF, fc), (ID, nd)]), (sub(K12, 72, 144), [(IDF, r), (ID, nd)])])
         tt(S1, K12, E12, op.min)
-        ts(LS1, S1, 1.0 - 2 * OFA, op.add)
+        cp(LS1, S1)
         JL = [U16(144) for k in range(4)]
         top["set"] = (3, 4)
 
         def jlist(k, c):
-            lo, hi = 768 * c, 768 * (c + 1)
-            cb = act(sub(CBS[k % 2], lo, hi), sub(VX[k % 2], lo, hi), None, 192.0, 1.0 / C)
-            ps = wrap(cb, BD, [(ID, sub(P16, 72 + 48 * c, 72 + 48 * (c + 1)))])
-            ts(sub(JL[k], 48 * c, 48 * (c + 1)), ps, ioff, op.add)
-            twin(CFG["sh"][c], t("IN1", lo, hi), sub(VX[k % 2], lo, hi))
-        for c in range(3):
-            tt(sub(VX[0], 768 * c, 768 * (c + 1)), ind(W(oFL, oF + P), sub(LS1, 48 * c, 48 * (c + 1))), t("IN1", 768 * c, 768 * (c + 1)), op.add)
+            lo, hi = CH[c], CH[c + 1]
+            src, own = sub(VX[k % 2], 16 * lo, 16 * hi), [(ID, sub(P16, 72 + lo, 72 + hi))]
+            cb, e = sub(CBS[k % 2], 16 * lo, 16 * hi), CFG["jl"][4 * rnd + k][c]
+            if e == "t":
+                ts(sub(JL[k], lo, hi), wrap(src, BDF, own), ifr, op.add)
+            elif e == "g":
+                twin("g", cb, src)
+                ts(sub(JL[k], lo, hi), wrap(cb, BDA, own), ifg, op.add)
+            else:
+                act(cb, src, None, 192.0, 1.0 / C)
+                ts(sub(JL[k], lo, hi), wrap(cb, BD, own), ioff, op.add)
+            twin(CFG["sh"][4 * rnd + k][c], t("IN1", 16 * lo, 16 * hi), src)
+        cuts = sorted(set(CH) | {72})
+        for lo, hi in zip(cuts, cuts[1:]):
+            win = W(oU, oF + P) if lo < 72 else W(oFL, oF + P)
+            tt(sub(VX[0], 16 * lo, 16 * hi), ind(win, sub(LS1, lo, hi)), t("IN1", 16 * lo, 16 * hi), op.subtract)
+        for c in range(len(CH) - 1):
             jlist(0, c)
         for k in range(4):
-            for c in range(3):
-                lo, hi = 768 * c, 768 * (c + 1)
-                tt(sub(VX[(k + 1) % 2], lo, hi), ind(VW[k % 2], sub(JL[k], 48 * c, 48 * (c + 1))), t("IN1", lo, hi), op.add)
+            for c in range(len(CH) - 1):
+                lo, hi = CH[c], CH[c + 1]
+                tt(sub(VX[(k + 1) % 2], 16 * lo, 16 * hi), ind(VW[k % 2], sub(JL[k], lo, hi)), t("IN1", 16 * lo, 16 * hi), op.add)
                 if k < 3:
                     jlist(k + 1, c)
         top["set"] = (5, 6, 7)
         UVb = Bf(576)
-        act(sub(UVb, 0, 576, 2), W(oUL, oUL + 288))
+        twin(CFG["tb"][0], sub(UVb, 0, 576, 2), W(oUL, oUL + 288))
         ps = wrap(sub(UVb, 0, 576, 2), BDA)
         LU = ts(U16(18), ps, -OFA, op.add)
         act(sub(UVb, 1, 576, 2), ind(W(oU, oU + A), LU))
@@ -415,10 +469,9 @@ def build(GA, SC):
         LUV = ts(U16(36), ps, -OFA, op.add, float(A - 1), op.min)
         for c in range(2):
             gat("s", W(oT + 288 * c, oT + 288 * (c + 1)), W(oU + 2 * A, oU + 3 * A), sub(LUV, 18 * c, 18 * (c + 1)))
-        act(W(oC, oC + 576), UVb, None, sub(EC, 36, 37))
-        act(W(oFA, oFA + 576), W(oFL, oFL + 576), None, sub(EC, 18, 19))
-        act(W(oF2, oF2 + 576, 2), W(oFL + 1, oFL + 576, 2), None, sub(EC, 36, 37))
-        act(W(oF2 + 1, oF2 + 576, 2), W(oFL, oFL + 576, 2), None, sub(EC, 36, 37))
+        twin(CFG["tb"][1], W(oC, oC + 576), UVb)
+        twin(CFG["tb"][2], W(oF2, oF2 + 576, 2), W(oFL + 1, oFL + 576, 2))
+        twin(CFG["tb"][3], W(oF2 + 1, oF2 + 576, 2), W(oFL, oFL + 576, 2))
         XU = Bf(576)
         for c in range(2):
             gat("s", sub(XU, 288 * c, 288 * (c + 1)), x, sub(LUV, 18 * c, 18 * (c + 1)))
@@ -426,23 +479,18 @@ def build(GA, SC):
         ps = big(288)
         mm([(ps, [(ID, xe), (NID, xo)])])
         act(t(Xc, oXF + 1, oXF + 576, 2), ps, fn.Abs)
-        ps = big(288)
-        mm([(ps, [(ID, xe), (ID, xo)])])
-        xs = act(Bf(288), ps, fn.Sign, -15.5)
-        ps = big(288)
-        mm([(ps, [(ID, xe), (ID, xo), (N8, xs)])])
-        act(t(Xc, oXF, oXF + 576, 2), ps, None, -8.0)
+        act(t(Xc, oXF, oXF + 576, 2), mod16(big(288), [xe, xo]))
         n1 = act(F(1), sub(incc, 71, 72), None, 2 * 576.0 - 1.0, 2.0)
         n2 = ts(F(1), n1, nfe, op.min, 1.0 - 4095.0, op.add)
         g3 = ts(Bf(72), rfx, n2, op.is_ge, BIG, op.mult)
         ps = bank(216)
         rm, cm, rd_ = sub(ps, 0, 72), sub(ps, 72, 144), sub(ps, 144, 216)
-        mm([(rm, [(IDF, a1), (ID, g3)]), (cm, [(IDF, k0a), (NID, nd)]), (rd_, [(IDF, r), (NID, sub(P16, 0, 72)), (NID, nd)])])
+        mm([(rm, [(IDF, a1), (ID, g3)]), (cm, [(IDF, k0a), (NID, nd)]), (rd_, [(IDF, cp(F(72), sub(JL[0], 72, 144))), (NDF, sub(AW, 144, 216)), (NID, nd)])])
         x1 = act(F(72), rm, fn.Relu, oXF - DM + 4095.0, -1.0)
         Ra, Rb = F(216), F(216)
         ps2 = bank(216)
         grp = []
-        for i, (src, k1, k2) in enumerate(((cm, float(A), oT - oU), (cm, float(P), oC - oU - A), (rd_, iR, oF2 - oU - 2 * A))):
+        for i, (src, k1, k2) in enumerate(((cm, float(A), oT - oU), (cm, float(P), oC - oU - A), (rd_, float(P + A), oF2 - oU - 2 * A))):
             lo, hi = 72 * i, 72 * (i + 1)
             act(sub(Ra, lo, hi), src, fn.Relu, k1)
             act(sub(Rb, lo, hi), rm, fn.Relu, k2 + 4095.0, -1.0)
@@ -454,27 +502,35 @@ def build(GA, SC):
         if rnd:
             act(sub(Lw, 72, 232), wrap(cb5, BDA), None, -OFA)
         ps3 = bank(160)
-        mm([(sub(ps3, 72 * i, 72 * (i + 1)), [(IDF, sub(Lw, 72 * (i + 1), 72 * (i + 2))), (BI, nann), (ID, nd), (ID, g3)]) for i in range(2)]
-           + [(sub(ps3, 144, 160), [(IDF, sub(Lw, 216, 232)), (ID, C3)])])
-        ts(sub(LP, 72, 232), ps3, -3 * BIG, op.add, 0.0, op.max)
+        mm([(sub(ps3, 72 * i, 72 * (i + 1)), [(IDF, sub(Lw, 72 * (i + 1), 72 * (i + 2))), (BI, nann), (ID, nd), (NID, g3), (ID, CN)]) for i in range(2)]
+           + [(sub(ps3, 144, 160), [(IDF, sub(Lw, 216, 232))])])
+        ts(sub(LP, 72, 232), ps3, 0.0, op.max, float(P), op.min)
         ps = bank(72)
         mm([(ps, [(ID, sub(P16, 0, 72)), (IDF, x1)])])
         LX = ts(U16(72), ps, i16, op.add)
         hot(8.0)
-        for c in range(12):
-            act(t("UP", 288 * c, 288 * (c + 1)), ind(W(oU, WEND), sub(LS2, 18 * c, 18 * (c + 1))), None, -7.5 if last else 0.0)
-        cbp = Bf(A)
-        cast(CFG["up"][rnd], cbp, t("UP", 0, A))
-        ps = wrap(cbp, BDA)
-        ts(sub(LP, 0, 72), ps, -OFA, op.add)
+        ups = [t("UP", 384 * c, 384 * (c + 1)) for c in range(9)]
+        if rnd == 0:
+            cbp = Bf(A)
+            ups[:3] = [sub(cbp, 384 * c, 384 * (c + 1)) for c in range(3)]
+        for c in range(9):
+            act(ups[c], ind(W(oU, WEND), sub(LS2, 24 * c, 24 * (c + 1))), None, -7.5 if last else 0.0)
+        if rnd == 0:
+            ts(sub(LP, 0, 72), wrap(cbp, BDA), -OFA, op.add)
+        elif CFG["up"][rnd] == "t":
+            ts(sub(LP, 0, 72), wrap(t("UP", 0, A), BDF), -OFA - 0.47, op.add)
+        else:
+            cbp = Bf(A)
+            cast(CFG["up"][rnd], cbp, t("UP", 0, A))
+            ts(sub(LP, 0, 72), wrap(cbp, BDA), -OFA, op.add)
         hot(4.0)
         for c in range(4):
             gat("s", t(Xn, DM + 288 * c, DM + 288 * (c + 1)), t(Xc, DM, oXF + 576), sub(LX, 18 * c, 18 * (c + 1)))
         xn = t(Xn, DM, DM + A)
         U4b = U(3 * A, P)
-        tt(U4b, ind(VW[0], sub(LP, 216, 232)), W(oU + 3 * A, oU + P), op.add)
+        tt(U4b, ind(VF, sub(LP, 216, 232)), W(oU + 3 * A, oU + P), op.add)
         for c in range(6):
-            tt(U(576 * c, 576 * (c + 1)), ind(VW[0], sub(LP, 36 * c, 36 * (c + 1))), t("UP", 576 * c, 576 * (c + 1)), op.add)
+            tt(U(576 * c, 576 * (c + 1)), ind(VF, sub(LP, 36 * c, 36 * (c + 1))), sub(cbp if rnd == 0 and c < 2 else t("UP", 0, 3 * A), 576 * c, 576 * (c + 1)), op.add)
         top["set"] = (3, 4, 5, 6, 7)
         L4 = F(232)
         L4u = U16(232)
@@ -485,13 +541,12 @@ def build(GA, SC):
         ts(sub(L4u, 216, 232), ps, -OFA, op.add)
         Lb = act(sub(L4, 216, 232), ps, None, -OFA)
         PP, PX, PF = PAY[rnd]
+        ps = big(256)
         if last:
             pi1, pi2 = I32(256), I32(256)
-            pr = act(F(256), U4b, None, -7.5)
-            act(pr, pr, None, MAGIC)
-            act(pr, pr, None, MAGIC, -1.0)
-        ps = big(256)
-        mm([(ps, [(IDF, U4b), (IDF, pr) if last else (NID, sub(cb0, 3 * A, P))])])
+            mod16(ps, [U4b])
+        else:
+            mm([(ps, [(IDF, U4b), (NID, sub(cb0, 3 * A, P))])])
         act(PP, ps)
         LPv, LXv, LFv = t("LP%d" % rnd, 0, B), t("LX%d" % rnd, 0, B), t("LF%d" % rnd, 0, 16)
         send(rnd, 0, PP, LPv)
@@ -505,23 +560,38 @@ def build(GA, SC):
         send(rnd, 2, PF, LFv)
         for c in range(3):
             lo, hi = A * c, A * (c + 1)
-            cast(CFG["u4"][3 * rnd + c], sub(cb0, lo, hi), U(lo, hi))
-            ps = wrap(sub(cb0, lo, hi), BDA)
+            if CFG["u4"][3 * rnd + c] == "t":
+                ps = wrap(U(lo, hi), BDF)
+            else:
+                cast(CFG["u4"][3 * rnd + c], sub(cb0, lo, hi), U(lo, hi))
+                ps = wrap(sub(cb0, lo, hi), BDA)
             if c < 2:
                 act(sub(L4, 72 * c, 72 * (c + 1)), ps, None, -OFA)
             else:
-                ts(sub(L4u, 72 * c, 72 * (c + 1)), ps, -OFA, op.add)
+                ts(sub(L4u, 72 * c, 72 * (c + 1)), ps, -OFA - 0.24, op.add)
         if last:
+            if "b" in CFG["mod"].lower():
+                add("g", lambda q, T, x: q.affine_select(T["XC"][:, :], T["XC"][:, :], [[0, A]], op.is_gt, 7.5, 0, 0), [t("XC", 0, A)], [t("XC", 0, A)],
+                    0.17 + 2 * A * CY)
             for c in range(9):
                 lo, hi = 384 * c, 384 * (c + 1)
-                ps = big(384)
-                if CFG["mod"][c] == "v":
-                    ts(ps, U(lo, hi), MAGIC, op.add, -MAGIC, op.add)
+                ps, out, e = big(384), t("DR", DM + lo, DM + hi), CFG["mod"][c]
+                if e == "u":
+                    act(out, mod16(ps, [U(lo, hi)], True))
+                    continue
+                if e == "t":
+                    mm([(ps, [(IDF, U(lo, hi)), (IM, ONES), (NM, ONES), (N75, ONES)])])
+                elif e in "AB":
+                    act(ps, act(ps, U(lo, hi), None, MAGIC), None, -MAGIC)
                 else:
-                    act(ps, U(lo, hi), None, MAGIC)
-                    act(ps, ps, None, -MAGIC)
-                tt(t("DR", DM + lo, DM + hi), U(lo, hi), ps, op.subtract)
-                act(t("DR", DM + lo, DM + hi), t("DR", DM + lo, DM + hi), None, 7.5)
+                    ts(ps, U(lo, hi), MAGIC, op.add, -MAGIC, op.add)
+                tt(out, U(lo, hi), ps, op.subtract)
+                if e == "v":
+                    act(out, out, None, 7.5)
+                elif e in "abAB":
+                    l0 = lo if c == 0 or CFG["mod"][c - 1] not in "aA" else l0
+                    if e in "bB":
+                        accum(t("DR", DM + l0, DM + hi), t("XC", 0, hi - l0))
             dma("y", lambda q, T, x: q.dma_start(T["yp"][:, 2 * A:3 * A], T["DR"][:, DM + 2 * A:DM + 3 * A]), [t("DR", DM + 2 * A, DM + 3 * A)], [], 3.0)
             gat("s", t("SV", 256, 512), t("RHO", DM, DM + A), LB)
             act(t("SV", 0, 256), t("SV", 256, 512), None, float(A))
@@ -534,10 +604,13 @@ def build(GA, SC):
             act(t("SV", 256, 512), ps)
         ps = bank(72)
         mm([(ps, [(IDF, sub(L4, 72, 144)), (NDF, sub(L4, 0, 72))])])
-        dl = act(F(72), ps)
+        dl = act(F(72), ps, None, 0.0, 1.0 / (A * C))
         psq = bank(48)
-        mm([(sub(psq, 0, 16), [(IDF, Lb), (BI, PF), (BI, LFv)]), (sub(psq, 16, 32), [(IDF, Lb), (ID, CA), (BI, PF), (BI, LFv)]),
-            (sub(psq, 32, 48), [(ID, sub(P16, 0, 16)), (NBI, PF), (NBI, LFv)])])
+        q3 = [sub(psq, 16 * i, 16 * (i + 1)) for i in range(3)]
+        mm([(psq, [(ID, CA)])], True, False)
+        mm([(q3[0], [(IDF, Lb), (BI, PF)]), (q3[1], [(IDF, Lb), (BI, PF)]), (q3[2], [(NBI, PF)])], False, False)
+        mm([(q3[0], [(BI, LFv)]), (q3[1], [(BI, LFv)])], False, False)
+        mm([(q3[2], [(NBI, LFv)])], False, True)
         Q2 = tt(F(32), sub(psq, 0, 32), KK, op.max)
         LQ = ts(U16(32), Q2, DM - 2 * BIG, op.add)
         LK = ts(U16(16), sub(psq, 32, 48), iBB, op.add, 256.0, op.min)
@@ -545,44 +618,65 @@ def build(GA, SC):
         mk = "CB5" if last else "DR"
         if last:
             fill(t("CB5", 0, 832), 0)
-            fill(t("CB5", 832, DM + A), 0)
+            twin("y", t("CB5", 832, DM + A), t("CB5", 0, 832))
         cp(ind(t(mk, 0, DM + A), sub(LQ, 0, 16)), DS)
         ps = wrap(t(mk, DM, DM + A), BD)
-        m1 = ts(F(72), ps, 0.5, op.is_gt)
-        m2 = tt(F(72), m1, dl, op.mult)
-        ps = bank(144)
-        mm([(sub(ps, 0, 72), [(IDF, sub(L4, 0, 72)), (IDF, m2)]), (sub(ps, 72, 144), [(IDF, sub(L4, 72, 144)), (NDF, m2)])])
-        cp(sub(L4u, 0, 144), ps)
+        m2 = tt(F(72), ps, dl, op.mult)
+        L5 = tt(F(72), sub(L4, 0, 72), m2, op.add)
+        ts(sub(L4u, 0, 72), L5, -0.24, op.add)
+        ps = bank(72)
+        mm([(ps, [(IDF, sub(L4, 72, 144)), (NDF, m2)])])
+        ts(sub(L4u, 72, 144), ps, -0.24, op.add)
         if not last:
             ts(t("DR", DM + A, DM + 2 * A), t("DR", DM, DM + A), -1.0, op.mult)
-            cp(ind(t("U4", 0, DM + 2 * A), LQ), t("SV", 0, 512))
+            cp(ind(t("U4", 0, DM + A), sub(LQ, 0, 16)), t("SV", 0, 256))
             cp(ind(t(Xn, 0, DM + A), sub(LQ, 0, 16)), LXv)
-            for k, (lo, hi) in enumerate(((0, 38), (38, 74), (74, 98), (98, 122), (122, 144), (216, 232), (144, 168), (168, 192), (192, 216))):
-                if CFG["rn"][k] == "v":
-                    tt(W(oU + 16 * lo, oU + 16 * hi), ind(t("DR", DM, DM + P), sub(L4u, lo, hi)), U(16 * lo, 16 * hi), op.add)
-                else:
-                    d = gat("s", sub(cb0, 16 * lo, 16 * hi), t("DR", DM, DM + P), sub(L4u, lo, hi))
-                    ps = ("PS%d" % (3 + k % 2), 0, 16 * (hi - lo), 1)
-                    mm([(ps, [(IDF, U(16 * lo, 16 * hi)), (ID, d)])])
-                    act(W(oU + 16 * lo, oU + 16 * hi), ps)
+            cuts = ((0, 36), (36, 72), (72, 96), (96, 120), (120, 144), (216, 232), (144, 168), (168, 192), (192, 216))
+
+            def rename(ks, L4u=L4u):
+                for k in ks:
+                    lo, hi = cuts[k]
+                    if CFG["rn"][k] == "v":
+                        tt(W(oU + 16 * lo, oU + 16 * hi), ind(t("DR", DM, DM + P), sub(L4u, lo, hi)), U(16 * lo, 16 * hi), op.add)
+                    elif CFG["rn"][k] in "de":
+                        gat("s", W(oU + 16 * lo, oU + 16 * hi), t("DR", DM, DM + P), sub(L4u, lo, hi))
+                        l0 = lo if k == ks[0] or CFG["rn"][k - 1] != "d" else l0
+                        if CFG["rn"][k] == "e":
+                            accum(W(oU + 16 * l0, oU + 16 * hi), U(16 * l0, 16 * hi))
+                    else:
+                        d = gat("s", sub(cb0, 16 * lo, 16 * hi), t("DR", DM, DM + P), sub(L4u, lo, hi))
+                        ps = ("PS%d" % (3 + k % 2), 0, 16 * (hi - lo), 1)
+                        mm([(ps, [(IDF, U(16 * lo, 16 * hi)), (ID, d)])])
+                        act(W(oU + 16 * lo, oU + 16 * hi), ps)
+
+            def later(LQ=LQ, LK=LK, lpw=lpw):
+                cp(ind(t("U4", 0, DM + 2 * A), sub(LQ, 16, 32)), t("SV", 256, 512))
+                rename(range(2, 9))
+                tt(W(oU + 3 * A, oU + P), ind(lpw, LK), W(oU + 3 * A, oU + P), op.add)
+                cast("g", cb5, W(oU + A, oU + P))
+            rename(range(2))
             Lw = Lw1
-            for c in range(2):
-                gat("s", t("CB1", 576 * c, 576 * (c + 1)), t("DR", DM, DM + P), sub(L4u, 36 * c, 36 * (c + 1)))
             top["set"] = (5,)
-            ps = wrap(t("CB1", 0, A), BDA, [(IDF, sub(L4, 0, 72)), (IDF, m2)])
-            LC = ts(LC1, ps, float(A), op.min)
-            act(sub(Lw, 0, 72), ps)
-            tt(W(oU + 3 * A, oU + P), ind(lpw, LK), W(oU + 3 * A, oU + P), op.add)
-            cast("g", cb5, W(oU + A, oU + P))
+            if CFG["lc"] == "s":
+                for c in range(2):
+                    gat("s", t("CB1", 576 * c, 576 * (c + 1)), t("DR", DM, DM + P), sub(L4u, 36 * c, 36 * (c + 1)))
+                ps, off = wrap(t("CB1", 0, A), BDA, [(IDF, L5)]), 0.0
+            else:
+                ps, off = wrap(W(oU, oU + A), BDF), -OFA
+            LC = ts(LC1, ps, off, op.add, float(A), op.min)
+            act(sub(Lw, 0, 72), act(F(72), ps, None, MAGIC / 16 + off), None, -MAGIC / 16)
         else:
             cp(ind(t("RHO", 0, DM + 2 * A), LQ), t("SV", 0, 512))
             for k, (lo, hi) in enumerate(((144, 188), (188, 232), (0, 48), (48, 96), (96, 144))):
                 gat(CFG["yl"][k], W(oF + 16 * lo, oF + 16 * hi), t("RHO", DM, DM + P), sub(L4u, lo, hi))
             dma("y", lambda q, T, x: q.dma_start(T["yl"][:, 2 * A:P], T["W"][0:128:16, oF + 2 * A:oF + P]), [W(oF + 2 * A, oF + P)], [], 2.2)
             dma("y", lambda q, T, x: q.dma_start(T["yl"][:, 0:2 * A], T["W"][0:128:16, oF:oF + 2 * A]), [W(oF, oF + 2 * A)], [], 2.2)
-            tt(pi1, ind(lpw, LK), PP, op.add)
-            ts(pi2, pi1, 15, op.bitwise_and)
-            cp(sub(SVb, 256, 512), pi2)
+            if CFG["pi"] == "v":
+                tt(pi1, ind(lpw, LK), PP, op.add)
+                ts(pi2, pi1, 15, op.bitwise_and)
+                cp(sub(SVb, 256, 512), pi2)
+            else:
+                act(sub(SVb, 256, 512), mod16(big(256), [PP, gat("s", Bf(256), lpw, LK)]))
             dma("y", lambda q, T, x: q.dma_start(T["yp"][:, 3 * A:P], ap(T, sub(SVb, 256, 512))), [sub(SVb, 256, 512)], [], 2.2)
             cp(ind(t("DR", 0, DM + 2 * A), LQ), SVb)
             dma("y", lambda q, T, x: q.dma_start(T["yp"][:, 0:2 * A], T["DR"][:, DM:DM + 2 * A]), [t("DR", DM, DM + 2 * A)], [], 3.5)
@@ -600,7 +694,7 @@ def hit(a, b):
     return False
 
 
-def schedule(ops, costs):
+def schedule(ops, costs, slow):
     n = len(ops)
     anc, pre = [], []
     for j, o in enumerate(ops):
@@ -647,15 +741,15 @@ def schedule(ops, costs):
     def judge(st):
         tot = 0.0
         seq = sorted(range(n), key=lambda j: (st[j], j))
-        for cost in costs:
+        for cost, sl in zip(costs, slow):
             free, en, last = {e: 0.0 for e in eng}, [0.0] * n, 0.0
             for j in seq:
                 s = free[eng[j]]
                 for i, h in pre[j]:
-                    if en[i] + h > s:
-                        s = en[i] + h
+                    if en[i] + h * sl > s:
+                        s = en[i] + h * sl
                 en[j] = free[eng[j]] = s + cost[j]
-                last = max(last, en[j] + lat[j])
+                last = max(last, en[j] + lat[j] * sl)
             tot += last / sum(cost)
         return tot
 
@@ -708,10 +802,74 @@ def schedule(ops, costs):
             cur = (v, st)
             if v < best[0]:
                 best = cur
-    for j, o in enumerate(ops):
-        o["start"] = best[1][j]
-        o["end"] = o["start"] + o["cost"] + o["lat"]
-    order = sorted(range(n), key=lambda j: (ops[j]["start"], j))
+    order = sorted(range(n), key=lambda j: (best[1][j], j))
+    down = [0] * n
+    for j in range(n - 1, -1, -1):
+        down[j] = 1 << j
+        for i, h in suc[j]:
+            down[j] |= down[i]
+    pres = [[[(i, h * sl) for i, h in pre[j]] for j in range(n)] for sl in slow]
+    norm = [sum(c) for c in costs]
+
+    def run(seq, m):
+        cost, pr, sl = costs[m], pres[m], slow[m]
+        free, lastq = {e: 0.0 for e in eng}, {}
+        en, why, last, lj = [0.0] * n, [None] * n, 0.0, 0
+        for j in seq:
+            e = eng[j]
+            s, w = free[e], lastq.get(e)
+            for i, h in pr[j]:
+                if en[i] + h > s:
+                    s, w = en[i] + h, i
+            why[j], lastq[e] = w, j
+            en[j] = free[e] = s = s + cost[j]
+            if s + lat[j] * sl > last:
+                last, lj = s + lat[j] * sl, j
+        return last / norm[m], lj, why, en
+
+    def rerun(seq, a, m, old):
+        cost, pr = costs[m], pres[m]
+        en, free = list(old), {e: 0.0 for e in eng}
+        for j in seq[max(0, a - 150):a]:
+            free[eng[j]] = en[j]
+        for j in seq[a:]:
+            e = eng[j]
+            s = free[e]
+            for i, h in pr[j]:
+                if en[i] + h > s:
+                    s = en[i] + h
+            en[j] = free[e] = s + cost[j]
+        return max(en[j] + lat[j] * slow[m] for j in ends) / norm[m], en
+    ends = [j for j in range(n) if not suc[j]]
+    ens = [run(order, m)[3] for m in range(len(costs))]
+    cur = sum(run(order, m)[0] for m in range(len(costs)))
+    best, pairs = (cur, order), []
+    for k in range(SWAPS):
+        if k % 8 == 0 or not pairs:
+            v, j, why, en = run(order, int(rnd() * len(costs)))
+            pairs = []
+            while why[j] is not None:
+                if eng[why[j]] == eng[j] and not up[j] >> why[j] & 1:
+                    pairs.append((why[j], j))
+                j = why[j]
+        i, j = pairs[int(rnd() * len(pairs))]
+        a, b = order.index(i), order.index(j)
+        if a > b:
+            pairs = []
+            continue
+        if rnd() < 0.5:
+            a, m = max(0, a - int(rnd() ** 3 * 40)), up[j]
+            new = order[:a] + [v for v in order[a:b + 1] if m >> v & 1] + [v for v in order[a:b + 1] if not m >> v & 1] + order[b + 1:]
+        else:
+            b, m = min(n - 1, b + int(rnd() ** 3 * 60)), down[i]
+            new = order[:a] + [v for v in order[a:b + 1] if not m >> v & 1] + [v for v in order[a:b + 1] if m >> v & 1] + order[b + 1:]
+        res = [rerun(new, a, m, ens[m]) for m in range(len(costs))]
+        v = sum(r[0] for r in res)
+        if v <= cur + 0.5 * TEMP * (1.0 - k / SWAPS) * rnd() ** 2:
+            order, cur, pairs, ens = new, v, pairs if v == cur else [], [r[1] for r in res]
+            if v < best[0]:
+                best = (v, new)
+    order = best[1]
     pos = {j: k for k, j in enumerate(order)}
     seen = {}
     for j in order:
@@ -719,7 +877,7 @@ def schedule(ops, costs):
         need = {}
         for i, h in pre[j]:
             e = ops[i]
-            if o["kind"] == "a":
+            if o["kind"] == "a" or e["kind"] == "r":
                 continue
             key = e["sem"] if e["kind"] != "c" else "e" + e["eng"]
             if key not in need or pos[i] > pos[need[key]]:
@@ -741,7 +899,8 @@ def schedule(ops, costs):
 
 
 PLAN = {}
-ROUNDS, SEED, HOP, TEMP = 24000, 1, (0.08, 0.15), 0.003
+GUESS = ((1.5, 2.7, 1.1, {}), (1.8, 4.9, 0.8, {"s": 1.15}), (1.15, 3.5, 1.0, {"t": 1.45, "g": 1.3}))
+ROUNDS, SWAPS, SEED, HOP, TEMP = 3000, 60000, 1, (0.08, 0.15), 0.003
 
 
 def rank_program(g, core, T, topo):
@@ -750,8 +909,8 @@ def rank_program(g, core, T, topo):
         return
     if not PLAN:
         PLAN["ops"] = build(1.56, 3.8)
-        costs = [[o["cost"] for o in build(a, b)] for a, b in ((1.3, 2.7), (1.8, 4.9))]
-        PLAN["order"], PLAN["count"] = schedule(PLAN["ops"], costs)
+        costs = [[o["cost"] * f.get(o["eng"], 1.0) for o in build(a, b)] for a, b, d, f in GUESS]
+        PLAN["order"], PLAN["count"] = schedule(PLAN["ops"], costs, [v[2] for v in GUESS])
     ops = PLAN["ops"]
     x = {"pid": [], "rid": [], "mask": []}
     ne = []

@@ -12,12 +12,12 @@ oUL, oFL, oD, oU, oF = 0, 576, 1728, 2880, 6592
 oF2, oT, oC, WEND = 10304, 10880, 11456, 12032
 DM = 512
 oXF = DM + A + 16
-POOL = {"SF": 5300, "SU": 2400, "SB": 8800, "SI": 600}
-CFG = {"xc": "vvsvvs", "ll": "ssssss", "sh": ("ggs",) * 8, "rn": "vvddevdde", "up": "tg", "g2": "ssssss", "u4": "gsgggs",
-       "u0": "svsvss", "mod": "tAbaABaAb", "yl": "ssssv", "lc": "s", "in1": "eded", "ch": (0, 48, 96, 144),
-       "jl": ("sss",) * 8, "tb": "ggggg", "pi": "t"}
+POOL = {"SF": 4600, "SU": 2400, "SB": 9900, "SI": 64}
+CFG = {"xc": "vssvss", "ll": "ssssss", "sh": ("yyyy",) * 4 + ("ygyg",) * 4, "rn": "vvddevdde", "up": "ts", "g2": "ssssss", "u4": "ssgggg",
+       "u0": "svssss", "mod": "AAbtABtAb", "yl": "ssssvsv", "so": "ssssss", "sv": "svss", "free": True, "lc": "s", "in1": "vvvvvv",
+       "ch": (0, 36, 72, 108, 144), "wr": (0, 72, 144), "jl": ("gsgs",) * 4 + ("ssss",) * 4, "tb": "ggggg"}
 
-F32 = {"W": WEND, "V": 7184, "UP": 3 * A, "U4": DM + P, "IN1": 2 * A, "RHO": DM + P, "SV": 512, "SF": POOL["SF"]}
+F32 = {"W": WEND, "V": 7184, "UP": 3 * A, "U4": DM + P, "IN1": 2 * A, "RHO": DM + P, "SV": 512, "LR": B, "SF": POOL["SF"]}
 TWO = {"FB": P, "CB0": P, "CB1": 2 * A, "CB5": 2560, "DR": DM + P, "XA": oXF + 576, "XB": oXF + 576, "XC": A, "LL": A, "DIF": A + 16,
        "SB": POOL["SB"], "LP0": B + 16, "LP1": B + 16, "LX0": B, "LX1": B, "LF0": 16, "LF1": 16}
 I32S = {"XI": A + 16, "LKI": 232, "THI": 2, "SI": POOL["SI"]}
@@ -28,7 +28,7 @@ SCRATCH.update({k: ("sbuf", [128, v], "int32") for k, v in I32S.items()})
 SCRATCH.update({"PS%d" % k: ("psum", [128, 512], "float32") for k in range(8)})
 
 NDMA = 64
-SEMAPHORES = ["ev", "es", "et", "eg", "sent"] + ["dm%d" % k for k in range(NDMA)] + ["ar%d" % k for k in range(3 * RO)]
+SEMAPHORES = ["ev", "es", "et", "eg", "sent"] + ["dm%d" % k for k in range(NDMA)] + ["ar%d" % k for k in range(4 * RO - 1)]
 
 op = AluOpType
 fn = ActivationFunctionType
@@ -115,11 +115,40 @@ def build(GA, SC, PE=PE):
             r = (0.5 if all(v[0] in TWO for v in [out] + ins) else 1.0) * (2.0 if both else 1.0)
         return 0.06 + max(64, cnt(out) * r) * CY
 
+    def scost(out, a):
+        return 0.07 + max(64, cnt(out) * (GA if a[0] == "ind" else 1.0)) * CY
+
+    def real(*vs):
+        return vs[0][0] != "ind" and all((v[1] if v[0] == "ind" else v)[0] not in I32S and v[0] != "SU" for v in vs)
+
+    def lin(eng, out, a, bias, scale):
+        if scale == 1.0 and bias == 0.0:
+            fv = lambda q, T, x: q.tensor_copy(ap(T, out), ap(T, a))
+        else:
+            fv = lambda q, T, x: q.tensor_scalar(ap(T, out), ap(T, a), ap(T, scale), ap(T, bias), op.mult, op.add)
+        ways = {"v": (fv, vcost(out, [a])),
+                "s": (lambda q, T, x: q.activation(ap(T, out), ap(T, a), fn.Identity, ap(T, bias), ap(T, scale)), scost(out, a))}
+        add(eng, ways[eng][0], [a, bias, scale], [out], ways[eng][1])
+        ops[-1]["ways"] = ways
+        return out
+
     def cp(out, a):
+        if real(out, a):
+            return lin("v", out, a, 0.0, 1.0)
         add("v", lambda q, T, x: q.tensor_copy(ap(T, out), ap(T, a)), [a], [out], vcost(out, [a]))
         return out
 
+    def scat(eng, win, lst, a):
+        out = ind(win, lst)
+        ways = {"v": (lambda q, T, x: q.tensor_copy(ap(T, out), ap(T, a)), vcost(out, [a])),
+                "s": (lambda q, T, x: q.activation(ap(T, out), ap(T, a), fn.Silu), vcost(out, [a]) + 0.02)}
+        add(eng, ways[eng][0], [a], [out], ways[eng][1])
+        if CFG["free"]:
+            ops[-1]["ways"] = ways
+
     def ts(out, a, s1, o0, s2=None, o1=None):
+        if real(out, a) and (o0, o1) in ((op.add, None), (op.mult, None), (op.mult, op.add)):
+            return lin("v", out, a, s1, 1.0) if o0 == op.add else lin("v", out, a, 0.0 if o1 is None else s2, s1)
         if o1 is None:
             f = lambda q, T, x: q.tensor_scalar(ap(T, out), ap(T, a), ap(T, s1), None, o0)
         else:
@@ -137,9 +166,12 @@ def build(GA, SC, PE=PE):
         return out
 
     def act(out, a, func=None, bias=0.0, scale=1.0):
-        fu = fn.Identity if func is None else func
-        add("s", lambda q, T, x: q.activation(ap(T, out), ap(T, a), fu, ap(T, bias), ap(T, scale)), [a, bias, scale], [out],
-            0.07 + max(64, cnt(out) * (GA if a[0] == "ind" else 1.0)) * CY)
+        if func is None:
+            return lin("s", out, a, bias, scale)
+        add("s", lambda q, T, x: q.activation(ap(T, out), ap(T, a), func, ap(T, bias), ap(T, scale)), [a, bias, scale], [out], scost(out, a))
+        if func == fn.Relu and scale == 1.0:
+            ops[-1]["ways"] = {"s": (ops[-1]["f"], ops[-1]["cost"]), "v": (
+                lambda q, T, x: q.tensor_scalar(ap(T, out), ap(T, a), ap(T, bias), 0.0, op.add, op.max), vcost(out, [a]))}
         return out
 
     def gat(eng, out, win, lst):
@@ -178,19 +210,21 @@ def build(GA, SC, PE=PE):
     def fill(out, val):
         return iota(out, [[0, cnt(out)]], int(val), 0)
 
-    def dma(eng, f, rd, wr, lat):
-        add(eng, f, rd, wr, 0.1 if eng != "g" else 1.0, "d", lat, "dm%d" % top["dma"])
+    def dma(eng, f, rd, wr, row):
+        s = "dm%d" % top["dma"]
+        add(eng, f, rd, list(wr) + [(s, 0, 1, 1)], 0.1 if eng != "g" else 1.0, "d", 1.0 if eng != "g" else 1.3, s)
+        add("n", None, list(rd) + [(s, 0, 1, 1)], wr, 8 * (0.04 + row * 2.5e-5), "x", 0.5, s)
         top["dma"] += 1
 
     def cast(eng, out, a):
         if eng == "g":
-            dma("g", lambda q, T, x: q.dma_start(ap(T, out), ap(T, a)), [a], [out], 2.5 + cnt(out) * 0.0012)
+            dma("g", lambda q, T, x: q.dma_start(ap(T, out), ap(T, a)), [a], [out], cnt(out) * (3 if out[0] in TWO else 4))
         else:
             for lo in (0, 576):
                 (act if eng == "s" else cp)(sub(out, lo, lo + 576), sub(a, lo, lo + 576))
 
     def accum(out, a):
-        dma("g", lambda q, T, x: q.dma_start(ap(T, out), ap(T, a), accum_op=op.add), [a, out], [out], 2.5 + cnt(out) * (0.001 if out[0] in TWO else 0.002))
+        dma("g", lambda q, T, x: q.dma_start(ap(T, out), ap(T, a), accum_op=op.add), [a, out], [out], cnt(out) * (4 if out[0] in TWO else 8))
 
     def twin(eng, out, a):
         if eng == "g":
@@ -200,7 +234,7 @@ def build(GA, SC, PE=PE):
         elif eng == "v":
             cp(out, a)
         else:
-            dma("y", lambda q, T, x: q.dma_start(ap(T, out), ap(T, a)), [a], [out], 2.0 + cnt(a) * 0.0016)
+            dma("y", lambda q, T, x: q.dma_start(ap(T, out), ap(T, a)), [a], [out], cnt(a) * (2 if a[0] in TWO else 4))
 
     def mod16(ps, parts, shifted=False):
         one = sub(ONES, 0, cnt(ps))
@@ -210,17 +244,17 @@ def build(GA, SC, PE=PE):
         return ps
 
     def send(rnd, k, src, dst):
-        s = "ar%d" % (3 * rnd + k)
-        tok = ("tok%d" % (3 * rnd + k), 0, 1, 1)
+        s = "ar%d" % (4 * rnd + k)
+        tok = ("tok%d" % (4 * rnd + k), 0, 1, 1)
         add("g", lambda q, T, x: q.remote_dma(ap(T, dst), ap(T, src), T.sem[s], T.sem["sent"], x["pid"][rnd], x["rid"][rnd], x["mask"][rnd]),
             [src] + ([("tok0", 0, 1, 1)] if rnd == 0 and k else []), [tok], 0.6 if rnd or k else 2.5, "r")
-        add("n", None, [tok], [dst], 0.01, "a", 4.5 + cnt(src) * 0.006, s)
+        add("n", None, [tok], [dst], 16 * (0.08 + cnt(src) * (2e-4 if src[0] in TWO else 4e-4)), "a", 3.2, s)
 
     F, Bf, U16, I32 = (lambda n: new("SF", n)), (lambda n: new("SB", n)), (lambda n: new("SU", n)), (lambda n: new("SI", n))
 
-    dma("y", lambda q, T, x: q.dma_start(T["LKI"][:, :], T["lk"][:, :]), [], [t("LKI", 0, 232)], 2.2)
-    dma("s", lambda q, T, x: q.dma_start(T["XI"][:, 0:A], T["x0"][:, :]), [], [t("XI", 0, A)], 3.5)
-    dma("y", lambda q, T, x: q.dma_start(T["THI"][:, :], T["th"][:, :]), [], [t("THI", 0, 2)], 2.2)
+    dma("y", lambda q, T, x: q.dma_start(T["LKI"][:, :], T["lk"][:, :]), [], [t("LKI", 0, 232)], 928)
+    dma("s", lambda q, T, x: q.dma_start(T["XI"][:, 0:A], T["x0"][:, :]), [], [t("XI", 0, A)], 4 * A)
+    dma("y", lambda q, T, x: q.dma_start(T["THI"][:, :], T["th"][:, :]), [], [t("THI", 0, 2)], 8)
 
     pc = iota(I32(1), [[0, 1]], 0, 1)
     ROW = iota(F(144), [[1, 144]], 0, 0)
@@ -240,13 +274,13 @@ def build(GA, SC, PE=PE):
     ts(sub(FBv, 1024, 2048), sub(FBv, 0, 1024), sub(EC, 16, 17), op.add)
     act(sub(FBv, 2048, 2688), sub(FBv, 0, 640), None, sub(EC, 32, 33))
     ts(sub(FBv, 2688, P), sub(FBv, 0, 1024), sub(EC, 42, 43), op.add)
-    dma("g", lambda q, T, x: q.dma_start(T["W"][:, oF:oF + P], T["FB"][:, :]), [FBv], [W(oF, oF + P)], 7.0)
+    cast("g", W(oF, oF + A), sub(FBv, 0, A))
+    cast("g", W(oF + A, oF + P), sub(FBv, A, P))
     g16i = ts(I32(1), pc, 112, op.bitwise_and)
     g16 = cp(F(1), g16i)
     i16 = act(F(1), g16, None, pcf, -1.0)
     g15 = act(F(1), g16, None, 15.0)
     ioff = act(F(1), i16, None, -OFF)
-    iBB = act(F(1), i16, None, 2 * BIG)
     w0 = ts(F(1), i16, 0.0, op.is_equal, 64.0, op.mult)
     w1 = ts(F(1), i16, 1.0, op.is_equal, w0, op.add)
     BD = ts(Bf(144), ROW, g15, op.is_equal, w1, op.mult)
@@ -265,8 +299,8 @@ def build(GA, SC, PE=PE):
     IM, NM, I75, N75 = diag(Bf(128), MAGIC), diag(Bf(128), -MAGIC), diag(Bf(128), 7.5), diag(Bf(128), -7.5)
     ONES = fill(Bf(384), 1)
     BDF = act(F(144), BD, None, 0.0, 1.0 / C)
-    ifr = act(F(1), i16, None, -0.491)
-    ifg = act(F(1), i16, None, -0.3)
+    ifr = act(F(1), i16, None, -0.491) if "t" in "".join(CFG["jl"]) else None
+    ifg = act(F(1), i16, None, -0.3) if "g" in "".join(CFG["jl"]) else None
     N4 = diag(Bf(128), -4096.0)
     ps = bank(128)
     mm([(ps, [(ID, sub(BS, 15 - i, 143 - i)) for i in range(16)])])
@@ -283,17 +317,23 @@ def build(GA, SC, PE=PE):
     mm([(psth, [(BO, thb)])])
     TH = act(F(2), psth)
     aw = sub(AW, 0, 72)
-    u0, f0 = float(oU - oFL), float(oF - oFL)
-    BA = act(F(72), aw, None, f0 - u0)
+    BA = F(144)
+    act(sub(BA, 0, 72), sub(AW, 72, 144), None, float(P))
+    act(sub(BA, 72, 144), sub(AW, 144, 216), None, float(oF - oFL))
     AWB = act(F(16), sub(AW, 216, 232), None, OFA)
-    KK = act(F(32), sub(AW, 0, 32), None, 2 * BIG - DM)
-    CA = Bf(48)
-    fill(sub(CA, 0, 16), 0)
+    KK = F(48), F(48)
+    for rnd in range(RO):
+        act(sub(KK[rnd], 0, 32), sub(AW, 0, 32), None, 2 * BIG - DM)
+        act(sub(KK[rnd], 32, 48), sub(AW, 0, 16), None, 2 * BIG - B, -1.0 * rnd)
+    CA = fill(Bf(48), 0)
     fill(sub(CA, 16, 32), A)
-    iota(sub(CA, 32, 48), [[16, 16]], 0, 0)
     P4 = diag(Bf(128), 4096.0)
     BOH = act(F(128), BO, None, 0.0, 0.5)
-    CN = fill(Bf(72), -BIG)
+    N18 = act(F(1), evnC, None, 0.0, -18.0)
+    K0 = 1280.0
+    DG = [diag(Bf(128), v) for v in (oT - oU - K0, oC - oU - A - K0, oF2 - oU - 2 * A - K0, float(A - P), oXF - DM - K0)]
+    CT = {v: fill(Bf(72), v) for v in (P, A, 9344, -2, oU - oFL + 2 * A, P - A, -2 * BIG)}
+    const = lambda v: CT[v]
     act(t("V", 3 * A + P, 3 * A + P + 16), sub(ROW, 0, 16), None, sub(EC, 36, 37), 0.0)
     iP = act(F(1), i16, None, float(P))
     for xb in ("XA", "XB"):
@@ -316,7 +356,7 @@ def build(GA, SC, PE=PE):
         twin("y", t("DR", lo, hi), t("DR", 0, hi - lo))
     DS = act(Bf(256), sub(FBv, 0, 256), None, sub(EC, 18, 19), 0.0)
     for k in range(6):
-        iota(t("RHO", k * 704, (k + 1) * 704), [[1, 704]], k * 704 - DM, 0)
+        iota(t("RHO", k * 704, (k + 1) * 704), [[1, 704]], k * 704 - DM + 64, 0)
 
     L0 = cp(U16(232), t("LKI", 0, 232))
     Lw = cp(F(232), t("LKI", 0, 232))
@@ -332,7 +372,8 @@ def build(GA, SC, PE=PE):
     CBS = (t("CB0", 0, P), t("CB1", 0, 2 * A))
     cb5 = t("CB5", 0, 2560)
     Lw1, LC1 = F(232), U16(72)
-    PAY = [(Bf(256), Bf(256), Bf(16)) for rnd in range(RO)]
+    SVb = Bf(768)
+    PAY = [(sub(SVb, 512, 768), Bf(256), Bf(16)) for rnd in range(RO)]
     keep = (top["SF"], top["SB"], top["SU"])
 
     for rnd in range(RO):
@@ -367,16 +408,12 @@ def build(GA, SC, PE=PE):
         rfx = tt(F(72), incf, sub(psf, 72, 144), op.add)
         nf = sub(incf, 71, 72)
         nfh = act(F(1), nf, None, -0.25, 0.5)
-        nfi = act(F(1), nfh, None, MAGIC / 16)
-        nfj = act(F(1), nfi, None, -MAGIC / 16)
-        nfe = act(F(1), nfj, None, -1.0, 2.0)
-        nfb = act(F(1), nfj, None, 576.5, -1.0)
+        room = ts(F(1), nfh, MAGIC / 16, op.add, -MAGIC / 16 - 576.0, op.add)
+        nfb = act(F(1), nf, None, 576.75, -0.5)
         mn = tt(F(72), L, aw, op.min)
         a1 = tt(F(72), aw, rfx, op.subtract)
-        nfm = act(F(1), nf, None, -4095.0)
-        a2 = act(F(72), a1, None, nfm)
+        a2 = ts(F(72), a1, nf, op.add, -4095.0, op.add)
         pf = tt(F(72), a2, rfx, op.min)
-        fc = act(F(72), L, None, f0 - u0)
         near = ts(Bf(72), psD, thr, op.is_lt)
         u2 = tt(Bf(72), psD, LTh, op.is_lt)
         nbb = act(Bf(72), psD, fn.Relu, -240.5 * 4096.0, 4096.0)
@@ -389,68 +426,62 @@ def build(GA, SC, PE=PE):
         pm = tt(F(72), rcx, pf, op.min)
         LS = ts(U16(72), pm, 4671.0, op.add)
         for k in range(3):
-            cp(ind(W(0, oD), sub(LS, 24 * k, 24 * (k + 1))), sub(FBv, 384 * k, 384 * (k + 1)))
+            scat(CFG["so"][3 * rnd + k], W(0, oD), sub(LS, 24 * k, 24 * (k + 1)), W(oF + 384 * k, oF + 384 * (k + 1)))
         rca = tt(F(72), incc, sub(psc, 144, 216), op.add)
         sg, acc = F(72), F(1)
         add("s", lambda q, T, x, sg=sg, rca=rca, nfb=nfb, acc=acc: q.activation(ap(T, sg), ap(T, rca), fn.Sign, ap(T, nfb), 1.0, accum_out=ap(T, acc)),
             [rca, nfb], [sg, acc], 0.09 + 72 * CY)
-        ps = bank(2)
-        mm([(sub(ps, 0, 1), [(BOH, acc)])])
-        lim = act(F(1), sub(ps, 0, 1), None, 576.0, -1.0)
-        ps = bank(72)
-        mm([(ps, [(IDF, mn), (BI, near), (ID, nbb), (BI, free)])])
-        nd = ts(Bf(72), ps, lim, op.is_ge, BIG, op.mult)
-        rc2 = act(F(72), rcx, None, 2 * 4671.0, 2.0)
-        LG = ts(U16(72), rc2, 1.0, op.add, A - 1.0, op.min)
+        ps = bank(80)
+        mm([(sub(ps, 0, 72), [(IDF, mn), (BI, near), (ID, nbb), (BI, free)])])
+        mm([(sub(ps, 72, 73), [(BOH, acc)])])
+        nd = ts(Bf(72), sub(ps, 0, 72), sub(ps, 72, 73), op.add, 576.0, op.is_ge)
+        K12 = bank(216)
+        mm([(sub(K12, 0, 72), [(IDF, L), (ID, const(P)), (BI, nd)]), (sub(K12, 72, 144), [(IDF, L), (ID, const(oD - oFL)), (BI, nd)]),
+            (sub(K12, 144, 216), [(IDF, rcx), (IDF, rcx), (ID, const(9344)), (ID, const(-2)), (BI, nd)])])
+        LG = ts(U16(72), sub(K12, 144, 216), 1.0, op.add, A - 1.0, op.min)
         for k in range(3):
             gat(CFG["g2"][3 * rnd + k], W(oD + 384 * k, oD + 384 * (k + 1)), W(oFL, oD), sub(LG, 24 * k, 24 * (k + 1)))
-        r = tt(F(72), rc2, act(F(72), L, None, float(oD - oFL)), op.min)
-        pse = bank(144)
-        mm([(sub(pse, 0, 72), [(ID, sub(P16, 0, 72)), (BI, nann)]), (sub(pse, 72, 144), [(IDF, L), (BI, nann)])])
+        pse = bank(216)
+        mm([(sub(pse, 0, 72), [(ID, sub(P16, 0, 72)), (BI, nann)]), (sub(pse, 72, 144), [(IDF, L), (ID, const(A)), (BI, nann)]),
+            (sub(pse, 144, 216), [(IDF, L), (ID, const(oU - oFL + 2 * A)), (BI, nann)])])
         LD = ts(U16(72), sub(pse, 0, 72), i16, op.add, float(A), op.min)
         hot(5.0)
-        e0 = tt(F(72), sub(pse, 72, 144), BA, op.min)
+        E12 = tt(F(144), sub(pse, 72, 216), BA, op.min)
         for k in range(3):
-            act(t("LL", 384 * k, 384 * (k + 1)), ind(t("DIF", 0, A + 16), sub(LD, 24 * k, 24 * (k + 1))), None, 0.0, -1.0)
-        for i in range(2):
-            if CFG["in1"][2 * rnd + i] == "d":
-                if rnd:
-                    twin("y", t("IN1", i * A, (i + 1) * A), W(oF + (i + 1) * A, oF + (i + 2) * A))
-                else:
-                    cast("g", t("IN1", i * A, (i + 1) * A), sub(FBv, (i + 1) * A, (i + 2) * A))
-                accum(t("IN1", i * A, (i + 1) * A), t("LL", 0, A))
+            lo, hi = 384 * k, 384 * (k + 1)
+            if CFG["in1"][3 * rnd + k] == "v":
+                tt(t("IN1", lo, hi), ind(t("DIF", 0, A + 16), sub(LD, 24 * k, 24 * (k + 1))), sub(FBv, A + lo, A + hi), op.subtract)
             else:
-                for k in range(3 * i, 3 * i + 3):
-                    ps = big(384)
-                    mm([(ps, [(ID, sub(FBv, A + 384 * k, A + 384 * (k + 1))), (ID, t("LL", 384 * (k % 3), 384 * (k % 3 + 1)))])])
-                    act(t("IN1", 384 * k, 384 * (k + 1)), ps)
-        E12, S1, LS1 = F(144), F(144), U16(144)
-        act(sub(E12, 0, 72), e0, None, float(A))
-        act(sub(E12, 72, 144), e0, None, u0 + 2 * A)
-        K12 = bank(144)
-        mm([(sub(K12, 0, 72), [(IDF, fc), (ID, nd)]), (sub(K12, 72, 144), [(IDF, r), (ID, nd)])])
-        tt(S1, K12, E12, op.min)
-        cp(LS1, S1)
+                gat("s", t("LL", lo, hi), t("DIF", 0, A + 16), sub(LD, 24 * k, 24 * (k + 1)))
+                ps = big(384)
+                mm([(ps, [(NID, sub(FBv, A + lo, A + hi)), (ID, t("LL", lo, hi))])])
+                act(t("IN1", lo, hi), ps)
+            act(t("IN1", A + lo, A + hi), t("IN1", lo, hi), None, N18)
+        S1 = tt(F(144), sub(K12, 0, 144), E12, op.min)
+        tt(sub(S1, 72, 144), sub(K12, 144, 216), sub(S1, 72, 144), op.min)
+        LS1 = cp(U16(144), S1)
         JL = [U16(144) for k in range(4)]
         top["set"] = (3, 4)
 
         def jlist(k, c):
             lo, hi = CH[c], CH[c + 1]
-            src, own = sub(VX[k % 2], 16 * lo, 16 * hi), [(ID, sub(P16, 72 + lo, 72 + hi))]
-            cb, e = sub(CBS[k % 2], 16 * lo, 16 * hi), CFG["jl"][4 * rnd + k][c]
-            if e == "t":
-                ts(sub(JL[k], lo, hi), wrap(src, BDF, own), ifr, op.add)
-            elif e == "g":
-                twin("g", cb, src)
-                ts(sub(JL[k], lo, hi), wrap(cb, BDA, own), ifg, op.add)
-            else:
+            src, cb, e = sub(VX[k % 2], 16 * lo, 16 * hi), sub(CBS[k % 2], 16 * lo, 16 * hi), CFG["jl"][4 * rnd + k]
+            if "g" in e:
+                twin(e[c], cb, src)
+            elif e[c] == "s":
                 act(cb, src, None, 192.0, 1.0 / C)
-                ts(sub(JL[k], lo, hi), wrap(cb, BD, own), ioff, op.add)
             twin(CFG["sh"][4 * rnd + k][c], t("IN1", 16 * lo, 16 * hi), src)
+            if hi in CFG["wr"]:
+                lo = CFG["wr"][CFG["wr"].index(hi) - 1]
+                own = [(ID, sub(P16, 72 + lo, 72 + hi))]
+                if e[c] == "t":
+                    ts(sub(JL[k], lo, hi), wrap(sub(VX[k % 2], 16 * lo, 16 * hi), BDF, own), ifr, op.add)
+                else:
+                    ts(sub(JL[k], lo, hi), wrap(sub(CBS[k % 2], 16 * lo, 16 * hi), BDA if "g" in e else BD, own), ifg if "g" in e else ioff, op.add)
         cuts = sorted(set(CH) | {72})
         for lo, hi in zip(cuts, cuts[1:]):
             win = W(oU, oF + P) if lo < 72 else W(oFL, oF + P)
-            tt(sub(VX[0], 16 * lo, 16 * hi), ind(win, sub(LS1, lo, hi)), t("IN1", 16 * lo, 16 * hi), op.subtract)
+            tt(sub(VX[0], 16 * lo, 16 * hi), ind(win, sub(LS1, lo, hi)), t("IN1", 16 * lo, 16 * hi), op.add)
         for c in range(len(CH) - 1):
             jlist(0, c)
         for k in range(4):
@@ -480,33 +511,28 @@ def build(GA, SC, PE=PE):
         mm([(ps, [(ID, xe), (NID, xo)])])
         act(t(Xc, oXF + 1, oXF + 576, 2), ps, fn.Abs)
         act(t(Xc, oXF, oXF + 576, 2), mod16(big(288), [xe, xo]))
-        n1 = act(F(1), sub(incc, 71, 72), None, 2 * 576.0 - 1.0, 2.0)
-        n2 = ts(F(1), n1, nfe, op.min, 1.0 - 4095.0, op.add)
-        g3 = ts(Bf(72), rfx, n2, op.is_ge, BIG, op.mult)
+        n2 = ts(F(1), sub(incc, 71, 72), room, op.min, 2.0, op.mult)
+        used = ts(Bf(72), rfx, 4095.0 - A, op.add, n2, op.is_lt)
         ps = bank(216)
         rm, cm, rd_ = sub(ps, 0, 72), sub(ps, 72, 144), sub(ps, 144, 216)
-        mm([(rm, [(IDF, a1), (ID, g3)]), (cm, [(IDF, k0a), (NID, nd)]), (rd_, [(IDF, cp(F(72), sub(JL[0], 72, 144))), (NDF, sub(AW, 144, 216)), (NID, nd)])])
-        x1 = act(F(72), rm, fn.Relu, oXF - DM + 4095.0, -1.0)
-        Ra, Rb = F(216), F(216)
+        mm([(rm, [(IDF, a1), (NBI, used)]), (cm, [(IDF, k0a), (NBI, nd)]),
+            (rd_, [(IDF, cp(F(72), sub(JL[0], 72, 144))), (NDF, sub(AW, 144, 216)), (NBI, nd)])])
+        Rb = act(F(72), rm, fn.Relu, K0 + 4095.0 - BIG, -1.0)
+        Ra, Rd = act(F(72), cm, fn.Relu, float(A)), act(F(72), rd_, fn.Relu, float(P + A))
         ps2 = bank(216)
-        grp = []
-        for i, (src, k1, k2) in enumerate(((cm, float(A), oT - oU), (cm, float(P), oC - oU - A), (rd_, float(P + A), oF2 - oU - 2 * A))):
-            lo, hi = 72 * i, 72 * (i + 1)
-            act(sub(Ra, lo, hi), src, fn.Relu, k1)
-            act(sub(Rb, lo, hi), rm, fn.Relu, k2 + 4095.0, -1.0)
-            grp.append((sub(ps2, lo, hi), [(ID, sub(P16, lo, hi)), (NPI, nann), (IDF, sub(Ra, lo, hi)), (IDF, sub(Rb, lo, hi))]))
-        mm(grp)
+        more = ([(IDF, Ra)], [(IDF, Ra), (ID, const(P - A)), (DG[3], nd)], [(IDF, Rd)])
+        mm([(sub(ps2, 72 * i, 72 * (i + 1)), [(ID, sub(P16, 72 * i, 72 * (i + 1))), (NPI, nann), (IDF, Rb), (DG[i], used)] + more[i]) for i in range(3)])
         LS2 = ts(U16(216), ps2, iP, op.add)
         hot(8.0)
         LP = U16(232)
         if rnd:
             act(sub(Lw, 72, 232), wrap(cb5, BDA), None, -OFA)
         ps3 = bank(160)
-        mm([(sub(ps3, 72 * i, 72 * (i + 1)), [(IDF, sub(Lw, 72 * (i + 1), 72 * (i + 2))), (BI, nann), (ID, nd), (NID, g3), (ID, CN)]) for i in range(2)]
+        mm([(sub(ps3, 72 * i, 72 * (i + 1)), [(IDF, sub(Lw, 72 * (i + 1), 72 * (i + 2))), (BI, nann), (BI, nd), (BI, used), (ID, const(-2 * BIG))]) for i in range(2)]
            + [(sub(ps3, 144, 160), [(IDF, sub(Lw, 216, 232))])])
         ts(sub(LP, 72, 232), ps3, 0.0, op.max, float(P), op.min)
         ps = bank(72)
-        mm([(ps, [(ID, sub(P16, 0, 72)), (IDF, x1)])])
+        mm([(ps, [(ID, sub(P16, 0, 72)), (IDF, Rb), (DG[4], used)])])
         LX = ts(U16(72), ps, i16, op.add)
         hot(8.0)
         ups = [t("UP", 384 * c, 384 * (c + 1)) for c in range(9)]
@@ -529,6 +555,7 @@ def build(GA, SC, PE=PE):
         xn = t(Xn, DM, DM + A)
         U4b = U(3 * A, P)
         tt(U4b, ind(VF, sub(LP, 216, 232)), W(oU + 3 * A, oU + P), op.add)
+        ops[-1]["sent"] = rnd
         for c in range(6):
             tt(U(576 * c, 576 * (c + 1)), ind(VF, sub(LP, 36 * c, 36 * (c + 1))), sub(cbp if rnd == 0 and c < 2 else t("UP", 0, 3 * A), 576 * c, 576 * (c + 1)), op.add)
         top["set"] = (3, 4, 5, 6, 7)
@@ -541,15 +568,15 @@ def build(GA, SC, PE=PE):
         ts(sub(L4u, 216, 232), ps, -OFA, op.add)
         Lb = act(sub(L4, 216, 232), ps, None, -OFA)
         PP, PX, PF = PAY[rnd]
-        ps = big(256)
-        if last:
-            pi1, pi2 = I32(256), I32(256)
-            mod16(ps, [U4b])
-        else:
-            mm([(ps, [(IDF, U4b), (NID, sub(cb0, 3 * A, P))])])
-        act(PP, ps)
         LPv, LXv, LFv = t("LP%d" % rnd, 0, B), t("LX%d" % rnd, 0, B), t("LF%d" % rnd, 0, 16)
-        send(rnd, 0, PP, LPv)
+        if last:
+            send(rnd, 0, act(PP, mod16(big(256), [U4b])), LPv)
+        else:
+            send(rnd, 0, sub(U4b, 0, 64), t("LR", 0, 64))
+            send(rnd, 3, sub(U4b, 64, B), t("LR", 64, B))
+            ps = big(256)
+            mm([(ps, [(IDF, t("LR", 0, B)), (NID, act(Bf(256), t("LR", 0, B)))])])
+            act(LPv, ps)
         gat("s", PX, xn, LB)
         hot(10.0)
         send(rnd, 1, PX, LXv)
@@ -592,15 +619,15 @@ def build(GA, SC, PE=PE):
                     l0 = lo if c == 0 or CFG["mod"][c - 1] not in "aA" else l0
                     if e in "bB":
                         accum(t("DR", DM + l0, DM + hi), t("XC", 0, hi - l0))
-            dma("y", lambda q, T, x: q.dma_start(T["yp"][:, 2 * A:3 * A], T["DR"][:, DM + 2 * A:DM + 3 * A]), [t("DR", DM + 2 * A, DM + 3 * A)], [], 3.0)
+            dma("y", lambda q, T, x: q.dma_start(T["yp"][:, 2 * A:3 * A], T["DR"][:, DM + 2 * A:DM + 3 * A]), [t("DR", DM + 2 * A, DM + 3 * A)], [], 2 * A)
             gat("s", t("SV", 256, 512), t("RHO", DM, DM + A), LB)
             act(t("SV", 0, 256), t("SV", 256, 512), None, float(A))
-            SVb = Bf(512)
             gat("s", sub(SVb, 0, 256), t("DR", DM + A, DM + 2 * A), LB)
+            act(sub(SVb, 256, 512), mod16(big(256), [PP, LPv]))
         else:
             gat("s", t("SV", 0, 256), U(A, 2 * A), LB)
             ps = big(256)
-            mm([(ps, [(ID, sub(FBv, 3 * A, P)), (ID, PP), (ID, LPv)])])
+            mm([(ps, [(ID, sub(FBv, 3 * A, P)), (IDF, U4b), (NID, sub(cb0, 3 * A, P)), (ID, LPv)])])
             act(t("SV", 256, 512), ps)
         ps = bank(72)
         mm([(ps, [(IDF, sub(L4, 72, 144)), (NDF, sub(L4, 0, 72))])])
@@ -608,12 +635,12 @@ def build(GA, SC, PE=PE):
         psq = bank(48)
         q3 = [sub(psq, 16 * i, 16 * (i + 1)) for i in range(3)]
         mm([(psq, [(ID, CA)])], True, False)
-        mm([(q3[0], [(IDF, Lb), (BI, PF)]), (q3[1], [(IDF, Lb), (BI, PF)]), (q3[2], [(NBI, PF)])], False, False)
+        mm([(q3[0], [(IDF, Lb), (BI, PF)]), (q3[1], [(IDF, Lb), (BI, PF)]), (q3[2], [(NDF, sub(AW, 0, 16)), (BI, PF)])], False, False)
         mm([(q3[0], [(BI, LFv)]), (q3[1], [(BI, LFv)])], False, False)
-        mm([(q3[2], [(NBI, LFv)])], False, True)
-        Q2 = tt(F(32), sub(psq, 0, 32), KK, op.max)
-        LQ = ts(U16(32), Q2, DM - 2 * BIG, op.add)
-        LK = ts(U16(16), sub(psq, 32, 48), iBB, op.add, 256.0, op.min)
+        mm([(q3[2], [(BI, LFv)])], False, True)
+        Q2 = tt(F(48), psq, KK[rnd], op.max)
+        LQ = ts(U16(32), sub(Q2, 0, 32), DM - 2 * BIG, op.add)
+        LK = ts(U16(16), sub(Q2, 32, 48), -1.0, op.mult, 2 * BIG, op.add)
         lpw = t("LP%d" % rnd, 0, B + 16)
         mk = "CB5" if last else "DR"
         if last:
@@ -629,7 +656,7 @@ def build(GA, SC, PE=PE):
         ts(sub(L4u, 72, 144), ps, -0.24, op.add)
         if not last:
             ts(t("DR", DM + A, DM + 2 * A), t("DR", DM, DM + A), -1.0, op.mult)
-            cp(ind(t("U4", 0, DM + A), sub(LQ, 0, 16)), t("SV", 0, 256))
+            scat(CFG["sv"][0], t("U4", 0, DM + A), sub(LQ, 0, 16), t("SV", 0, 256))
             cp(ind(t(Xn, 0, DM + A), sub(LQ, 0, 16)), LXv)
             cuts = ((0, 36), (36, 72), (72, 96), (96, 120), (120, 144), (216, 232), (144, 168), (168, 192), (192, 216))
 
@@ -650,7 +677,7 @@ def build(GA, SC, PE=PE):
                         act(W(oU + 16 * lo, oU + 16 * hi), ps)
 
             def later(LQ=LQ, LK=LK, lpw=lpw):
-                cp(ind(t("U4", 0, DM + 2 * A), sub(LQ, 16, 32)), t("SV", 256, 512))
+                scat(CFG["sv"][1], t("U4", 0, DM + 2 * A), sub(LQ, 16, 32), t("SV", 256, 512))
                 rename(range(2, 9))
                 tt(W(oU + 3 * A, oU + P), ind(lpw, LK), W(oU + 3 * A, oU + P), op.add)
                 cast("g", cb5, W(oU + A, oU + P))
@@ -664,24 +691,22 @@ def build(GA, SC, PE=PE):
             else:
                 ps, off = wrap(W(oU, oU + A), BDF), -OFA
             LC = ts(LC1, ps, off, op.add, float(A), op.min)
-            act(sub(Lw, 0, 72), act(F(72), ps, None, MAGIC / 16 + off), None, -MAGIC / 16)
+            ts(sub(Lw, 0, 72), ps, MAGIC / 16 + off, op.add, -MAGIC / 16, op.add)
         else:
-            cp(ind(t("RHO", 0, DM + 2 * A), LQ), t("SV", 0, 512))
-            for k, (lo, hi) in enumerate(((144, 188), (188, 232), (0, 48), (48, 96), (96, 144))):
-                gat(CFG["yl"][k], W(oF + 16 * lo, oF + 16 * hi), t("RHO", DM, DM + P), sub(L4u, lo, hi))
-            dma("y", lambda q, T, x: q.dma_start(T["yl"][:, 2 * A:P], T["W"][0:128:16, oF + 2 * A:oF + P]), [W(oF + 2 * A, oF + P)], [], 2.2)
-            dma("y", lambda q, T, x: q.dma_start(T["yl"][:, 0:2 * A], T["W"][0:128:16, oF:oF + 2 * A]), [W(oF, oF + 2 * A)], [], 2.2)
-            if CFG["pi"] == "v":
-                tt(pi1, ind(lpw, LK), PP, op.add)
-                ts(pi2, pi1, 15, op.bitwise_and)
-                cp(sub(SVb, 256, 512), pi2)
-            else:
-                act(sub(SVb, 256, 512), mod16(big(256), [PP, gat("s", Bf(256), lpw, LK)]))
-            dma("y", lambda q, T, x: q.dma_start(T["yp"][:, 3 * A:P], ap(T, sub(SVb, 256, 512))), [sub(SVb, 256, 512)], [], 2.2)
-            cp(ind(t("DR", 0, DM + 2 * A), LQ), SVb)
-            dma("y", lambda q, T, x: q.dma_start(T["yp"][:, 0:2 * A], T["DR"][:, DM:DM + 2 * A]), [t("DR", DM, DM + 2 * A)], [], 3.5)
+            for c in range(2):
+                scat(CFG["sv"][2 + c], t("RHO", 0, DM + 2 * A), sub(LQ, 16 * c, 16 * (c + 1)), t("SV", 256 * c, 256 * (c + 1)))
+            for k, (lo, hi) in enumerate(((144, 174), (174, 204), (204, 232), (0, 36), (36, 72), (72, 108), (108, 144))):
+                lin(CFG["yl"][k], W(oF + 16 * lo, oF + 16 * hi), ind(t("RHO", DM, DM + P), sub(L4u, lo, hi)), -64.0, 1.0)
+            dma("y", lambda q, T, x: q.dma_start(T["yl"][:, 2 * A:P], T["W"][0:128:16, oF + 2 * A:oF + P]), [W(oF + 2 * A, oF + P)], [], 0)
+            dma("y", lambda q, T, x: q.dma_start(T["yl"][:, 0:2 * A], T["W"][0:128:16, oF:oF + 2 * A]), [W(oF, oF + 2 * A)], [], 0)
+            bp = gat("s", Bf(256), sub(SVb, 256, 768), LK)
+            dma("y", lambda q, T, x: q.dma_start(T["yp"][:, 3 * A:P], ap(T, bp)), [bp], [], 2 * B)
+            cp(ind(t("DR", 0, DM + 2 * A), LQ), sub(SVb, 0, 512))
+            for c, e in enumerate("ys"):
+                dma(e, lambda q, T, x, c=c: q.dma_start(T["yp"][:, c * A:(c + 1) * A], T["DR"][:, DM + c * A:DM + (c + 1) * A]),
+                    [t("DR", DM + c * A, DM + (c + 1) * A)], [], 2 * A)
             cp(ind(t(Xn, 0, DM + A), sub(LQ, 0, 16)), LXv)
-            dma("y", lambda q, T, x: q.dma_start(T["yx"][:, :], ap(T, xn)), [xn], [], 3.0)
+            dma("y", lambda q, T, x: q.dma_start(T["yx"][:, :], ap(T, xn)), [xn], [], 2 * A)
     assert top["dma"] <= NDMA
     return ops
 
@@ -694,13 +719,16 @@ def hit(a, b):
     return False
 
 
-def schedule(ops, costs, slow):
+def schedule(ops, guess):
     n = len(ops)
+    slow = [v[2] for v in guess]
+    both = [[{e: w[1] * f.get(e, 1.0) for e, w in o.get("ways", {o["eng"]: (0, o["cost"])}).items()} for o in build(a, b)] for a, b, d, f in guess]
+    costs = [[c[o["eng"]] for c, o in zip(row, ops)] for row in both]
     anc, pre = [], []
     for j, o in enumerate(ops):
         pj = [r for r in o["rd"] if r[0].startswith("PS")]
         o["dep"] = [i for i in range(j) if hit(ops[i]["wr"], o["rd"]) or hit(ops[i]["wr"], o["wr"]) or hit(ops[i]["rd"], o["wr"])
-                    or (pj and ops[i]["eng"] != o["eng"] and hit(ops[i]["rd"], pj))]
+                    or (pj and (ops[i]["eng"] != o["eng"] or "ways" in o or "ways" in ops[i]) and hit(ops[i]["rd"], pj))]
         m, keep = 0, []
         for i in reversed(o["dep"]):
             if not m >> i & 1:
@@ -810,66 +838,150 @@ def schedule(ops, costs, slow):
             down[j] |= down[i]
     pres = [[[(i, h * sl) for i, h in pre[j]] for j in range(n)] for sl in slow]
     norm = [sum(c) for c in costs]
+    glue = [() if o["eng"] == "n" else (j,) if o["kind"] == "c" else (j, j + 1) for j, o in enumerate(ops)]
+    for row in pres:
+        for j in range(n):
+            if eng[j] == "n":
+                row[j] = [v for v in row[j] if v[0] == j - 1]
 
-    def run(seq, m):
-        cost, pr, sl = costs[m], pres[m], slow[m]
-        free, lastq = {e: 0.0 for e in eng}, {}
-        en, why, last, lj = [0.0] * n, [None] * n, 0.0, 0
-        for j in seq:
-            e = eng[j]
-            s, w = free[e], lastq.get(e)
-            for i, h in pr[j]:
-                if en[i] + h > s:
-                    s, w = en[i] + h, i
-            why[j], lastq[e] = w, j
-            en[j] = free[e] = s = s + cost[j]
-            if s + lat[j] * sl > last:
-                last, lj = s + lat[j] * sl, j
-        return last / norm[m], lj, why, en
-
-    def rerun(seq, a, m, old):
+    def run(seq, m, a=0, old=None):
         cost, pr = costs[m], pres[m]
-        en, free = list(old), {e: 0.0 for e in eng}
-        for j in seq[max(0, a - 150):a]:
-            free[eng[j]] = en[j]
-        for j in seq[a:]:
-            e = eng[j]
-            s = free[e]
-            for i, h in pr[j]:
-                if en[i] + h > s:
-                    s = en[i] + h
-            en[j] = free[e] = s + cost[j]
-        return max(en[j] + lat[j] * slow[m] for j in ends) / norm[m], en
+        en, why = (list(old[2]), list(old[4])) if a else ([0.0] * n, [None] * n)
+        free, lastq = {e: 0.0 for e in "vstgyn"}, {e: None for e in "vstgyn"}
+        for v in seq[max(0, a - 150):a]:
+            for j in glue[v]:
+                free[eng[j]], lastq[eng[j]] = en[j], j
+        for v in seq[a:]:
+            for j in glue[v]:
+                e = eng[j]
+                s, w = free[e], lastq[e]
+                for i, h in pr[j]:
+                    h += en[i]
+                    if h > s:
+                        s, w = h, i
+                why[j], lastq[e] = w, j
+                en[j] = free[e] = s + cost[j]
+        last, lj = max((en[j] + lat[j] * slow[m], j) for j in ends)
+        return [last / norm[m], lj, en, None, why]
+
+    def back(seq, m, got, b=n, old=None):
+        cost, su, why = costs[m], sucs[m], got[4]
+        q, nxt = list(old[3]) if old else [0.0] * n, {e: 0.0 for e in "vstgyn"}
+        for v in seq[b + 150:b:-1]:
+            for j in glue[v][::-1]:
+                nxt[eng[j]] = q[j]
+        for v in seq[b::-1]:
+            for j in glue[v][::-1]:
+                e = eng[j]
+                s = nxt[e]
+                for i, h in su[j]:
+                    h += q[i]
+                    if h > s:
+                        s = h
+                q[j] = nxt[e] = s + cost[j]
+        pairs, j = [], got[1]
+        while why[j] is not None:
+            if eng[why[j]] == eng[j] and not up[j] >> why[j] & 1:
+                d = eng[j] == "n"
+                pairs.append((why[j] - d, j - d))
+            j = why[j]
+        got[1], got[3] = pairs, q
+        return got
     ends = [j for j in range(n) if not suc[j]]
-    ens = [run(order, m)[3] for m in range(len(costs))]
-    cur = sum(run(order, m)[0] for m in range(len(costs)))
-    best, pairs = (cur, order), []
+
+    def bound(seq, mid, a, b):
+        tot, inside, before, after = 0.0, [j for v in mid for j in glue[v]], {}, {}
+        for v in seq[max(0, a - 80):a]:
+            for j in glue[v]:
+                before[eng[j]] = j
+        for v in seq[b + 80:b:-1]:
+            for j in reversed(glue[v]):
+                after[eng[j]] = j
+        for m in res:
+            cost, pr, en, q = costs[m], pres[m], res[m][2], res[m][3]
+            new, free, last = {}, {e: en[j] for e, j in before.items()}, res[m][0] * norm[m]
+            if max(en[j] - cost[j] + q[j] for j in inside) > last - 0.7:
+                last = 0.0
+            for j in inside:
+                s = free.get(eng[j], 0.0)
+                for i, h in pr[j]:
+                    h += new[i] if i in new else en[i]
+                    if h > s:
+                        s = h
+                new[j] = free[eng[j]] = s + cost[j]
+            for j in inside:
+                for i, h in sucs[m][j]:
+                    if i not in new and new[j] + h + q[i] > last:
+                        last = new[j] + h + q[i]
+            for e, j in after.items():
+                if e in free and free[e] + q[j] > last:
+                    last = free[e] + q[j]
+            tot += last / norm[m]
+        return tot
+
+    def flip(j):
+        eng[j] = "s" if eng[j] == "v" else "v"
+        for m in range(len(costs)):
+            costs[m][j] = both[m][j][eng[j]]
+    sucs = [[[] for j in range(n)] for row in pres]
+    for m, row in enumerate(pres):
+        for j in range(n):
+            for i, h in row[j]:
+                sucs[m][i].append((j, h))
+    res, took = {}, 0
     for k in range(SWAPS):
-        if k % 8 == 0 or not pairs:
-            v, j, why, en = run(order, int(rnd() * len(costs)))
-            pairs = []
-            while why[j] is not None:
-                if eng[why[j]] == eng[j] and not up[j] >> why[j] & 1:
-                    pairs.append((why[j], j))
-                j = why[j]
+        if k in (0, SWAPS * 2 // 3):
+            ms = (0,) if k == 0 else range(1, len(costs))
+            if k:
+                order = best[1]
+                for j in range(n):
+                    if eng[j] != best[2][j]:
+                        flip(j)
+            res = {m: back(order, m, run(order, m)) for m in ms}
+            cur = sum(r[0] for r in res.values())
+            best, k0, k1 = (cur, order, list(eng)), k, SWAPS if k else SWAPS * 2 // 3
+            pos = {j: k for k, j in enumerate(order)}
+        pairs = res[ms[int(rnd() * len(ms))]][1]
         i, j = pairs[int(rnd() * len(pairs))]
-        a, b = order.index(i), order.index(j)
-        if a > b:
-            pairs = []
-            continue
-        if rnd() < 0.5:
+        a, b = pos[i], pos[j]
+        u, other = rnd(), None
+        if u < 0.2:
+            other = i if u < 0.1 else j
+            if "ways" not in ops[other]:
+                continue
+            flip(other)
+            mid = order[a:b + 1]
+        elif u < 0.6:
             a, m = max(0, a - int(rnd() ** 3 * 40)), up[j]
-            new = order[:a] + [v for v in order[a:b + 1] if m >> v & 1] + [v for v in order[a:b + 1] if not m >> v & 1] + order[b + 1:]
+            mid = [v for v in order[a:b + 1] if m >> v & 1] + [v for v in order[a:b + 1] if not m >> v & 1]
         else:
             b, m = min(n - 1, b + int(rnd() ** 3 * 60)), down[i]
-            new = order[:a] + [v for v in order[a:b + 1] if not m >> v & 1] + [v for v in order[a:b + 1] if m >> v & 1] + order[b + 1:]
-        res = [rerun(new, a, m, ens[m]) for m in range(len(costs))]
-        v = sum(r[0] for r in res)
-        if v <= cur + 0.5 * TEMP * (1.0 - k / SWAPS) * rnd() ** 2:
-            order, cur, pairs, ens = new, v, pairs if v == cur else [], [r[1] for r in res]
-            if v < best[0]:
-                best = (v, new)
+            mid = [v for v in order[a:b + 1] if not m >> v & 1] + [v for v in order[a:b + 1] if m >> v & 1]
+        lim = cur + TEMP * (k1 - k) / (k1 - k0) * rnd() ** 2
+        if bound(order, mid, a, b) <= lim:
+            new = order[:a] + mid + order[b + 1:]
+            got = {m: run(new, m, a, res[m]) for m in ms}
+            v = sum(r[0] for r in got.values())
+            if v <= lim:
+                took += 1
+                if took % 50 == 0:
+                    en = got[ms[0]][2]
+                    new = sorted(new, key=lambda j: en[j] - costs[ms[0]][j])
+                    got = {m: back(new, m, run(new, m)) for m in ms}
+                    v = sum(r[0] for r in got.values())
+                else:
+                    got = {m: back(new, m, got[m], b, res[m]) for m in ms}
+                order, cur, res = new, v, got
+                pos = {j: k for k, j in enumerate(order)}
+                if v < best[0]:
+                    best = (v, new, list(eng))
+                continue
+        if other is not None:
+            flip(other)
     order = best[1]
+    for o, e in zip(ops, best[2]):
+        if e != o["eng"]:
+            o["eng"], o["f"], o["cost"] = e, o["ways"][e][0], o["ways"][e][1]
     pos = {j: k for k, j in enumerate(order)}
     seen = {}
     for j in order:
@@ -877,7 +989,7 @@ def schedule(ops, costs, slow):
         need = {}
         for i, h in pre[j]:
             e = ops[i]
-            if o["kind"] == "a" or e["kind"] == "r":
+            if o["kind"] in "ax" or e["kind"] == "r":
                 continue
             key = e["sem"] if e["kind"] != "c" else "e" + e["eng"]
             if key not in need or pos[i] > pos[need[key]]:
@@ -899,8 +1011,8 @@ def schedule(ops, costs, slow):
 
 
 PLAN = {}
-GUESS = ((1.5, 2.7, 1.1, {}), (1.8, 4.9, 0.8, {"s": 1.15}), (1.15, 3.5, 1.0, {"t": 1.45, "g": 1.3}))
-ROUNDS, SWAPS, SEED, HOP, TEMP = 3000, 60000, 1, (0.08, 0.15), 0.003
+GUESS = ((1.5, 3.6, 1.1, {"t": 1.15, "g": 1.1}), (1.5, 2.7, 1.2, {}), (1.8, 4.9, 0.8, {}), (1.15, 3.5, 1.0, {"t": 1.45, "g": 1.3}))
+ROUNDS, SWAPS, SEED, HOP, TEMP = 200, 200000, 1, (0.08, 0.15), 0.0015
 
 
 def rank_program(g, core, T, topo):
@@ -909,12 +1021,11 @@ def rank_program(g, core, T, topo):
         return
     if not PLAN:
         PLAN["ops"] = build(1.56, 3.8)
-        costs = [[o["cost"] * f.get(o["eng"], 1.0) for o in build(a, b)] for a, b, d, f in GUESS]
-        PLAN["order"], PLAN["count"] = schedule(PLAN["ops"], costs, [v[2] for v in GUESS])
+        PLAN["order"], PLAN["count"] = schedule(PLAN["ops"], GUESS)
     ops = PLAN["ops"]
     x = {"pid": [], "rid": [], "mask": []}
     ne = []
-    sent = 0
+    sent = []
     for rnd in range(RO):
         peer = T.cores[rank ^ XM[rnd]]
         rid, pid = topo.addr(peer, core)
@@ -922,28 +1033,30 @@ def rank_program(g, core, T, topo):
         x["rid"].append(rid)
         x["mask"].append(topo.mask(core, peer))
         ne.append(len(topo.engines(peer, core)))
-        sent += 3 * len(topo.engines(core, peer))
+        sent.append(sum(o["kind"] == "a" and int(o["sem"][2:]) // 4 == rnd for o in ops) * len(topo.engines(core, peer)))
     queue = {"v": g.vector, "s": g.scalar, "t": g.tensor, "g": g, "y": g.sync}
 
     def full(e):
         if e["kind"] == "c":
             return e["val"]
-        if e["kind"] == "d":
+        if e["kind"] in "dx":
             return 16
-        return ne[int(e["sem"][2:]) // 3]
+        return ne[int(e["sem"][2:]) // 4]
     for j in PLAN["order"]:
         o = ops[j]
-        if o["kind"] == "a":
+        if o["kind"] in "ax":
             continue
         q = queue[o["eng"]]
         for key, i in o["wait"]:
             q.wait_ge(T.sem[key], full(ops[i]))
+        if o.get("sent"):
+            q.wait_ge(T.sem["sent"], sum(sent[:o["sent"]]))
         ins = o["f"](q, T, x)
         if o["kind"] == "d":
             ins.then_inc(T.sem[o["sem"]], 16)
         elif o["kind"] == "c" and o.get("sig"):
             ins.then_inc(T.sem["e" + o["eng"]], 1)
-    g.wait_ge(T.sem["sent"], sent)
+    g.wait_ge(T.sem["sent"], sum(sent))
     for e in sorted(PLAN["count"]):
         g.wait_ge(T.sem["e" + e], PLAN["count"][e])
     for o in ops:

from concourse.mybir import AluOpType, ActivationFunctionType

A, B, RO, XM = 1152, 256, 2, (2, 3)
P = 3 * A + B
C = 32768.0
Z = 128.0 * C
OFA = 65.0 * 128.0
OFF = 65.0 * 192.0
MAGIC = 1.5 * 2.0 ** 27
BIG = 16384.0
oUL, oFL, oD, oU, oF = 0, 576, 1728, 2880, 6592
oF2, oT, oC, WEND = 10304, 10880, 11456, 12032
DM = 512
oXF = DM + A + 16
POOL = {"SF": 4600, "SU": 2400, "SB": 9900, "SI": 64}
CFG = {"xc": "vssvss", "ll": "ssssss", "sh": ("yyyy",) * 4 + ("ygyg",) * 4, "rn": "vvddevdde", "up": "ts", "g2": "ssssss", "u4": "ssgggg",
       "u0": "svssss", "mod": "AAbtABtAb", "yl": "ssssvsv", "so": "ssssss", "sv": "svss", "free": True, "lc": "s", "in1": "vvvvvv",
       "ch": (0, 36, 72, 108, 144), "wr": (0, 72, 144), "jl": ("gsgs",) * 4 + ("ssss",) * 4, "tb": "ggggg"}

F32 = {"W": WEND, "V": 7184, "UP": 3 * A, "U4": DM + P, "IN1": 2 * A, "RHO": DM + P, "SV": 512, "LR": B, "SF": POOL["SF"]}
TWO = {"FB": P, "CB0": P, "CB1": 2 * A, "CB5": 2560, "DR": DM + P, "XA": oXF + 576, "XB": oXF + 576, "XC": A, "LL": A, "DIF": A + 16,
       "SB": POOL["SB"], "LP0": B + 16, "LP1": B + 16, "LX0": B, "LX1": B, "LF0": 16, "LF1": 16}
I32S = {"XI": A + 16, "LKI": 232, "THI": 2, "SI": POOL["SI"]}
SCRATCH = {"SU": ("sbuf", [128, POOL["SU"]], "uint16")}
SCRATCH.update({k: ("sbuf", [128, v], "float32") for k, v in F32.items()})
SCRATCH.update({k: ("sbuf", [128, v], "bfloat16") for k, v in TWO.items()})
SCRATCH.update({k: ("sbuf", [128, v], "int32") for k, v in I32S.items()})
SCRATCH.update({"PS%d" % k: ("psum", [128, 512], "float32") for k in range(8)})

NDMA = 64
SEMAPHORES = ["ev", "es", "et", "eg", "sent"] + ["dm%d" % k for k in range(NDMA)] + ["ar%d" % k for k in range(4 * RO - 1)]

op = AluOpType
fn = ActivationFunctionType
CY, PE = 0.00083 * 1.1, 0.000417 * 1.1


def sub(v, lo, hi, st=1):
    return (v[0], v[1] + lo, v[1] + hi, st)


def cnt(v):
    if v[0] == "ind":
        return 16 * cnt(v[2])
    return len(range(v[1], v[2], v[3]))


def ap(T, v):
    if not isinstance(v, tuple):
        return v
    if v[0] == "ind":
        return ap(T, v[1]).indirect(ap(T, v[2]))
    if v[3] == 1:
        return T[v[0]][:, v[1]:v[2]]
    return T[v[0]][:, v[1]:v[2]:v[3]]


def regs(vs):
    out = []
    for v in vs:
        if not isinstance(v, tuple):
            continue
        if v[0] == "ind":
            out += regs([v[1], v[2]])
        elif v[0].startswith("PS"):
            out.append((v[0], 0, 512))
        else:
            out.append((v[0], v[1], v[2]))
    return out


def build(GA, SC, PE=PE):
    ops = []
    top = {"SF": 0, "SU": 0, "SB": 0, "SI": 0, "bank": 0, "big": 0, "dma": 0, "set": (3, 4, 5, 6, 7)}

    def new(pool, n):
        lo = top[pool]
        top[pool] = lo + (n + 15) // 16 * 16
        assert top[pool] <= POOL[pool], pool
        return (pool, lo, lo + n, 1)

    def W(lo, hi, st=1):
        return ("W", lo, hi, st)

    def t(name, lo, hi, st=1):
        return (name, lo, hi, st)

    def U(lo, hi):
        return ("U4", DM + lo, DM + hi, 1)

    def hot(v):
        ops[-1]["bump"] = v

    def ind(win, lst):
        return ("ind", win, lst)

    def bank(n):
        top["bank"] += 1
        return ("PS%d" % top["set"][top["bank"] % len(top["set"])], 0, n, 1)

    def big(n):
        top["big"] += 1
        return ("PS%d" % (top["big"] % 3), 0, n, 1)

    def add(eng, f, rd, wr, cost, kind="c", lat=0.0, sem=None):
        ops.append({"eng": eng, "f": f, "rd": regs(list(rd) + [v[2] for v in wr if v[0] == "ind"]),
                    "wr": regs([v[1] if v[0] == "ind" else v for v in wr]), "cost": cost, "kind": kind, "lat": lat, "sem": sem, "bump": 0.0})

    def vcost(out, ins, both=False):
        if out[0] == "ind":
            r = SC
        elif ins[0][0] == "ind":
            r = GA
        else:
            r = (0.5 if all(v[0] in TWO for v in [out] + ins) else 1.0) * (2.0 if both else 1.0)
        return 0.06 + max(64, cnt(out) * r) * CY

    def scost(out, a):
        return 0.07 + max(64, cnt(out) * (GA if a[0] == "ind" else 1.0)) * CY

    def real(*vs):
        return vs[0][0] != "ind" and all((v[1] if v[0] == "ind" else v)[0] not in I32S and v[0] != "SU" for v in vs)

    def lin(eng, out, a, bias, scale):
        if scale == 1.0 and bias == 0.0:
            fv = lambda q, T, x: q.tensor_copy(ap(T, out), ap(T, a))
        else:
            fv = lambda q, T, x: q.tensor_scalar(ap(T, out), ap(T, a), ap(T, scale), ap(T, bias), op.mult, op.add)
        ways = {"v": (fv, vcost(out, [a])),
                "s": (lambda q, T, x: q.activation(ap(T, out), ap(T, a), fn.Identity, ap(T, bias), ap(T, scale)), scost(out, a))}
        add(eng, ways[eng][0], [a, bias, scale], [out], ways[eng][1])
        ops[-1]["ways"] = ways
        return out

    def cp(out, a):
        if real(out, a):
            return lin("v", out, a, 0.0, 1.0)
        add("v", lambda q, T, x: q.tensor_copy(ap(T, out), ap(T, a)), [a], [out], vcost(out, [a]))
        return out

    def scat(eng, win, lst, a):
        out = ind(win, lst)
        ways = {"v": (lambda q, T, x: q.tensor_copy(ap(T, out), ap(T, a)), vcost(out, [a])),
                "s": (lambda q, T, x: q.activation(ap(T, out), ap(T, a), fn.Silu), vcost(out, [a]) + 0.02)}
        add(eng, ways[eng][0], [a], [out], ways[eng][1])
        if CFG["free"]:
            ops[-1]["ways"] = ways

    def ts(out, a, s1, o0, s2=None, o1=None):
        if real(out, a) and (o0, o1) in ((op.add, None), (op.mult, None), (op.mult, op.add)):
            return lin("v", out, a, s1, 1.0) if o0 == op.add else lin("v", out, a, 0.0 if o1 is None else s2, s1)
        if o1 is None:
            f = lambda q, T, x: q.tensor_scalar(ap(T, out), ap(T, a), ap(T, s1), None, o0)
        else:
            f = lambda q, T, x: q.tensor_scalar(ap(T, out), ap(T, a), ap(T, s1), ap(T, s2), o0, o1)
        add("v", f, [a, s1, s2], [out], vcost(out, [a]))
        return out

    def tt(out, a, b, o):
        both = not (a[0].startswith("PS") or b[0].startswith("PS"))
        add("v", lambda q, T, x: q.tensor_tensor(ap(T, out), ap(T, a), ap(T, b), o), [a, b], [out], vcost(out, [a, b], both))
        return out

    def scan(out, d0, d1, init):
        add("v", lambda q, T, x: q.tensor_tensor_scan(ap(T, out), ap(T, d0), ap(T, d1), init, op.mult, op.add), [d0, d1], [out], 0.14)
        return out

    def act(out, a, func=None, bias=0.0, scale=1.0):
        if func is None:
            return lin("s", out, a, bias, scale)
        add("s", lambda q, T, x: q.activation(ap(T, out), ap(T, a), func, ap(T, bias), ap(T, scale)), [a, bias, scale], [out], scost(out, a))
        if func == fn.Relu and scale == 1.0:
            ops[-1]["ways"] = {"s": (ops[-1]["f"], ops[-1]["cost"]), "v": (
                lambda q, T, x: q.tensor_scalar(ap(T, out), ap(T, a), ap(T, bias), 0.0, op.add, op.max), vcost(out, [a]))}
        return out

    def gat(eng, out, win, lst):
        return act(out, ind(win, lst)) if eng == "s" else cp(out, ind(win, lst))

    def mm(groups, first=True, final=True):
        def f(q, T, x):
            last = None
            for out, terms in groups:
                for k, (l, r) in enumerate(terms):
                    last = q.matmul(ap(T, out), ap(T, l), ap(T, r), first and k == 0, final and k == len(terms) - 1)
            return last
        rd = [v for o, terms in groups for lr in terms for v in lr]
        add("t", f, rd, [o for o, terms in groups],
            0.06 + sum(max(64, cnt(r)) * (1 if r[0] in TWO else 4) for o, terms in groups for l, r in terms) * PE)

    def wrap(src, pick, extra=()):
        st = src[3]
        ps = bank(cnt(src) // 16)
        terms = [(sub(pick, 15 - i, 143 - i), (src[0], src[1] + i * st, src[2], 16 * st)) for i in range(16)]
        mm([(ps, terms + list(extra))])
        return ps

    def iota(out, pat, base, cm):
        if out[0] not in I32S:
            f = lambda q, T, x: q.iota(ap(T, out), pat, base, cm, allow_small_or_imprecise_dtypes=True)
        else:
            f = lambda q, T, x: q.iota(ap(T, out), pat, base, cm)
        add("g", f, [], [out], 0.15 + 2 * cnt(out) * CY)
        return out

    def sel(out, a, cmp):
        add("g", lambda q, T, x: q.affine_select(ap(T, out), ap(T, a), [[-1, 128]], cmp, 0.0, 0, 1), [a], [out], 0.17 + 256 * CY)
        return out

    def fill(out, val):
        return iota(out, [[0, cnt(out)]], int(val), 0)

    def dma(eng, f, rd, wr, row):
        s = "dm%d" % top["dma"]
        add(eng, f, rd, list(wr) + [(s, 0, 1, 1)], 0.1 if eng != "g" else 1.0, "d", 1.0 if eng != "g" else 1.3, s)
        add("n", None, list(rd) + [(s, 0, 1, 1)], wr, 8 * (0.04 + row * 2.5e-5), "x", 0.5, s)
        top["dma"] += 1

    def cast(eng, out, a):
        if eng == "g":
            dma("g", lambda q, T, x: q.dma_start(ap(T, out), ap(T, a)), [a], [out], cnt(out) * (3 if out[0] in TWO else 4))
        else:
            for lo in (0, 576):
                (act if eng == "s" else cp)(sub(out, lo, lo + 576), sub(a, lo, lo + 576))

    def accum(out, a):
        dma("g", lambda q, T, x: q.dma_start(ap(T, out), ap(T, a), accum_op=op.add), [a, out], [out], cnt(out) * (4 if out[0] in TWO else 8))

    def twin(eng, out, a):
        if eng == "g":
            add("g", lambda q, T, x: q.affine_select(ap(T, out), ap(T, a), [[0, cnt(a)]], op.is_ge, 0.0, 0, 0), [a], [out], 0.17 + 2 * cnt(a) * CY)
        elif eng == "s":
            act(out, a)
        elif eng == "v":
            cp(out, a)
        else:
            dma("y", lambda q, T, x: q.dma_start(ap(T, out), ap(T, a)), [a], [out], cnt(a) * (2 if a[0] in TWO else 4))

    def mod16(ps, parts, shifted=False):
        one = sub(ONES, 0, cnt(ps))
        neg = [(NDF if v[0] not in TWO else NID, v) for v in parts]
        pos = [(IDF if v[0] not in TWO else ID, v) for v in parts]
        mm([(ps, ([] if shifted else [(I75, one)]) + neg + [(NM, one), (IM, one)] + pos + ([(I75, one)] if shifted else []))])
        return ps

    def send(rnd, k, src, dst):
        s = "ar%d" % (4 * rnd + k)
        tok = ("tok%d" % (4 * rnd + k), 0, 1, 1)
        add("g", lambda q, T, x: q.remote_dma(ap(T, dst), ap(T, src), T.sem[s], T.sem["sent"], x["pid"][rnd], x["rid"][rnd], x["mask"][rnd]),
            [src] + ([("tok0", 0, 1, 1)] if rnd == 0 and k else []), [tok], 0.6 if rnd or k else 2.5, "r")
        add("n", None, [tok], [dst], 16 * (0.08 + cnt(src) * (2e-4 if src[0] in TWO else 4e-4)), "a", 3.2, s)

    F, Bf, U16, I32 = (lambda n: new("SF", n)), (lambda n: new("SB", n)), (lambda n: new("SU", n)), (lambda n: new("SI", n))

    dma("y", lambda q, T, x: q.dma_start(T["LKI"][:, :], T["lk"][:, :]), [], [t("LKI", 0, 232)], 928)
    dma("s", lambda q, T, x: q.dma_start(T["XI"][:, 0:A], T["x0"][:, :]), [], [t("XI", 0, A)], 4 * A)
    dma("y", lambda q, T, x: q.dma_start(T["THI"][:, :], T["th"][:, :]), [], [t("THI", 0, 2)], 8)

    pc = iota(I32(1), [[0, 1]], 0, 1)
    ROW = iota(F(144), [[1, 144]], 0, 0)
    I64 = sub(ROW, 0, 64)
    pcf = iota(F(1), [[0, 1]], 0, 1)
    AWp = iota(F(232), [[16, 232]], 0, 1)
    P16 = iota(Bf(232), [[16, 232]], 0, 0)
    oddi = ts(I32(1), pc, 1, op.bitwise_and)
    oddC = ts(F(1), oddi, C, op.mult)
    evnC = act(F(1), oddC, None, C, -1.0)
    FBv = t("FB", 0, P)
    ts(sub(FBv, 0, 64), I64, oddC, op.mult, Z, op.add)
    EC = act(F(64), I64, None, 0.0, evnC)
    for k in range(4):
        w = 64 << k
        ts(sub(FBv, w, 2 * w), sub(FBv, 0, w), sub(EC, 1 << k, (1 << k) + 1), op.add)
    ts(sub(FBv, 1024, 2048), sub(FBv, 0, 1024), sub(EC, 16, 17), op.add)
    act(sub(FBv, 2048, 2688), sub(FBv, 0, 640), None, sub(EC, 32, 33))
    ts(sub(FBv, 2688, P), sub(FBv, 0, 1024), sub(EC, 42, 43), op.add)
    cast("g", W(oF, oF + A), sub(FBv, 0, A))
    cast("g", W(oF + A, oF + P), sub(FBv, A, P))
    g16i = ts(I32(1), pc, 112, op.bitwise_and)
    g16 = cp(F(1), g16i)
    i16 = act(F(1), g16, None, pcf, -1.0)
    g15 = act(F(1), g16, None, 15.0)
    ioff = act(F(1), i16, None, -OFF)
    w0 = ts(F(1), i16, 0.0, op.is_equal, 64.0, op.mult)
    w1 = ts(F(1), i16, 1.0, op.is_equal, w0, op.add)
    BD = ts(Bf(144), ROW, g15, op.is_equal, w1, op.mult)
    BDA = act(Bf(144), BD, None, 0.0, 1.0 / C)
    BS = ts(Bf(144), ROW, g15, op.is_equal)
    ONE = fill(Bf(128), 1)
    ID = sel(Bf(128), ONE, op.is_equal)

    def diag(out, v, eng="g"):
        if eng == "s":
            return act(out, ID, None, 0.0, v)
        add("g", lambda q, T, x: q.affine_select(ap(T, out), ap(T, ID), [[-1, 128]], op.not_equal, v, 0, 1), [ID], [out], 0.17 + 256 * CY)
        return out
    NID, IDF, BI = diag(Bf(128), -1.0, "s"), diag(F(128), 1.0), diag(Bf(128), BIG)
    NDF, NBI, NPI = diag(F(128), -1.0), diag(Bf(128), -BIG), diag(Bf(128), -float(P))
    IM, NM, I75, N75 = diag(Bf(128), MAGIC), diag(Bf(128), -MAGIC), diag(Bf(128), 7.5), diag(Bf(128), -7.5)
    ONES = fill(Bf(384), 1)
    BDF = act(F(144), BD, None, 0.0, 1.0 / C)
    ifr = act(F(1), i16, None, -0.491) if "t" in "".join(CFG["jl"]) else None
    ifg = act(F(1), i16, None, -0.3) if "g" in "".join(CFG["jl"]) else None
    N4 = diag(Bf(128), -4096.0)
    ps = bank(128)
    mm([(ps, [(ID, sub(BS, 15 - i, 143 - i)) for i in range(16)])])
    BO = act(Bf(128), ps)
    b1 = sel(Bf(128), BO, op.is_gt)
    ps = bank(128)
    mm([(ps, [(NID, b1), (N4, ID)])])
    TRC = act(Bf(128), ps)
    ng16 = act(F(1), g16, None, 0.0, -1.0)
    AW = act(F(232), AWp, None, ng16)
    ONE = sub(ONE, 0, 72)
    thb = cp(Bf(2), t("THI", 0, 2))
    psth = bank(2)
    mm([(psth, [(BO, thb)])])
    TH = act(F(2), psth)
    aw = sub(AW, 0, 72)
    BA = F(144)
    act(sub(BA, 0, 72), sub(AW, 72, 144), None, float(P))
    act(sub(BA, 72, 144), sub(AW, 144, 216), None, float(oF - oFL))
    AWB = act(F(16), sub(AW, 216, 232), None, OFA)
    KK = F(48), F(48)
    for rnd in range(RO):
        act(sub(KK[rnd], 0, 32), sub(AW, 0, 32), None, 2 * BIG - DM)
        act(sub(KK[rnd], 32, 48), sub(AW, 0, 16), None, 2 * BIG - B, -1.0 * rnd)
    CA = fill(Bf(48), 0)
    fill(sub(CA, 16, 32), A)
    P4 = diag(Bf(128), 4096.0)
    BOH = act(F(128), BO, None, 0.0, 0.5)
    N18 = act(F(1), evnC, None, 0.0, -18.0)
    K0 = 1280.0
    DG = [diag(Bf(128), v) for v in (oT - oU - K0, oC - oU - A - K0, oF2 - oU - 2 * A - K0, float(A - P), oXF - DM - K0)]
    CT = {v: fill(Bf(72), v) for v in (P, A, 9344, -2, oU - oFL + 2 * A, P - A, -2 * BIG)}
    const = lambda v: CT[v]
    act(t("V", 3 * A + P, 3 * A + P + 16), sub(ROW, 0, 16), None, sub(EC, 36, 37), 0.0)
    iP = act(F(1), i16, None, float(P))
    for xb in ("XA", "XB"):
        fill(t(xb, DM + A, oXF), C / 2)
    fill(t("XI", A, A + 16), C / 2)
    fill(t("DIF", A, A + 16), 0)
    fill(W(0, oFL), Z)
    twin("y", W(oFL, oFL + 576), W(0, oFL))
    twin("y", W(oFL + 576, oD), W(0, oFL))
    fill(t("V", 0, 576), 0)
    for lo, hi in ((576, A), (3 * A, 3 * A + 576), (3 * A + 576, 4 * A), (6 * A, 6 * A + 256)):
        twin("y", t("V", lo, hi), t("V", 0, hi - lo))
    for rnd in range(RO):
        fill(t("LP%d" % rnd, B, B + 16), 0)
    twin("y", t("U4", 0, DM), t("V", 0, DM))
    fill(t("DR", 0, 832), 0)
    for xb in ("XA", "XB"):
        twin("y", t(xb, 0, DM), t("DR", 0, DM))
    for lo, hi in ((832, DM + A), (DM + 2 * A, DM + 2 * A + 704), (DM + 2 * A + 704, DM + P)):
        twin("y", t("DR", lo, hi), t("DR", 0, hi - lo))
    DS = act(Bf(256), sub(FBv, 0, 256), None, sub(EC, 18, 19), 0.0)
    for k in range(6):
        iota(t("RHO", k * 704, (k + 1) * 704), [[1, 704]], k * 704 - DM + 64, 0)

    L0 = cp(U16(232), t("LKI", 0, 232))
    Lw = cp(F(232), t("LKI", 0, 232))
    for k, (lo, hi) in enumerate(((0, 38), (38, 74), (74, 110), (110, 146), (146, 190), (190, 232))):
        gat(CFG["u0"][k], W(oU + 16 * lo, oU + 16 * hi), FBv, sub(L0, lo, hi))
    cp(t("XA", DM, DM + 576), t("XI", 0, 576))
    cp(t("XA", DM + 576, DM + A), t("XI", 576, A))

    VW = (t("V", 3 * A, 3 * A + P), t("V", 0, P))
    VX = (t("V", 4 * A, 6 * A), t("V", A, 3 * A))
    VF = t("V", 3 * A, 3 * A + P + 16)
    CH = CFG["ch"]
    CBS = (t("CB0", 0, P), t("CB1", 0, 2 * A))
    cb5 = t("CB5", 0, 2560)
    Lw1, LC1 = F(232), U16(72)
    SVb = Bf(768)
    PAY = [(sub(SVb, 512, 768), Bf(256), Bf(16)) for rnd in range(RO)]
    keep = (top["SF"], top["SB"], top["SU"])

    for rnd in range(RO):
        top["SF"], top["SB"], top["SU"] = keep
        last = rnd == RO - 1
        Xc, Xn = ("XA", "XB") if rnd % 2 == 0 else ("XB", "XA")
        x = t(Xc, DM, DM + A)
        top["set"] = (5, 6, 7)
        L = sub(Lw, 0, 72)
        thr = sub(TH, rnd, rnd + 1)
        if rnd == 0:
            LC = ts(U16(72), L, float(A), op.min)
        for k in range(3):
            lo, hi = 384 * k, 384 * (k + 1)
            lst = sub(LC, 24 * k, 24 * (k + 1))
            e = CFG["xc"][3 * rnd + k]
            gat(e, t("XC", lo, hi), t(Xc, DM, oXF) if rnd or e == "s" else t("XI", 0, A + 16), lst)
            gat(CFG["ll"][3 * rnd + k], t("LL", lo, hi), W(oU, oU + A + 16), lst)
            ps = big(384)
            mm([(ps, [(NID, sub(FBv, lo, hi)), (NID, sub(x, lo, hi))])], True, False)
            mm([(ps, [(ID, t("XC", lo, hi)), (ID, t("LL", lo, hi))])], False, True)
            act(t("DIF", lo, hi), ps, fn.Abs)
        if rnd:
            later()
        psD = wrap(t("DIF", 0, A), BS)
        k0a = tt(F(72), L, aw, op.subtract)
        free = ts(Bf(72), k0a, 0.0, op.is_equal)
        LTh = ts(F(72), k0a, 0.0, op.is_gt, 240.5, op.mult)
        psf = bank(144)
        mm([(sub(psf, 0, 72), [(BO, free)]), (sub(psf, 72, 144), [(TRC, free)])])
        incf = scan(F(72), ONE, sub(psf, 0, 72), 0.0)
        rfx = tt(F(72), incf, sub(psf, 72, 144), op.add)
        nf = sub(incf, 71, 72)
        nfh = act(F(1), nf, None, -0.25, 0.5)
        room = ts(F(1), nfh, MAGIC / 16, op.add, -MAGIC / 16 - 576.0, op.add)
        nfb = act(F(1), nf, None, 576.75, -0.5)
        mn = tt(F(72), L, aw, op.min)
        a1 = tt(F(72), aw, rfx, op.subtract)
        a2 = ts(F(72), a1, nf, op.add, -4095.0, op.add)
        pf = tt(F(72), a2, rfx, op.min)
        near = ts(Bf(72), psD, thr, op.is_lt)
        u2 = tt(Bf(72), psD, LTh, op.is_lt)
        nbb = act(Bf(72), psD, fn.Relu, -240.5 * 4096.0, 4096.0)
        cand = tt(Bf(72), u2, near, op.is_gt)
        nann = tt(Bf(72), near, free, op.is_le)
        psc = bank(216)
        mm([(sub(psc, 0, 72), [(BO, cand)]), (sub(psc, 72, 144), [(TRC, cand)]), (sub(psc, 144, 216), [(NID, cand), (TRC, cand), (P4, cand)])])
        incc = scan(F(72), ONE, sub(psc, 0, 72), -576.0)
        rcx = tt(F(72), incc, sub(psc, 72, 144), op.add)
        pm = tt(F(72), rcx, pf, op.min)
        LS = ts(U16(72), pm, 4671.0, op.add)
        for k in range(3):
            scat(CFG["so"][3 * rnd + k], W(0, oD), sub(LS, 24 * k, 24 * (k + 1)), W(oF + 384 * k, oF + 384 * (k + 1)))
        rca = tt(F(72), incc, sub(psc, 144, 216), op.add)
        sg, acc = F(72), F(1)
        add("s", lambda q, T, x, sg=sg, rca=rca, nfb=nfb, acc=acc: q.activation(ap(T, sg), ap(T, rca), fn.Sign, ap(T, nfb), 1.0, accum_out=ap(T, acc)),
            [rca, nfb], [sg, acc], 0.09 + 72 * CY)
        ps = bank(80)
        mm([(sub(ps, 0, 72), [(IDF, mn), (BI, near), (ID, nbb), (BI, free)])])
        mm([(sub(ps, 72, 73), [(BOH, acc)])])
        nd = ts(Bf(72), sub(ps, 0, 72), sub(ps, 72, 73), op.add, 576.0, op.is_ge)
        K12 = bank(216)
        mm([(sub(K12, 0, 72), [(IDF, L), (ID, const(P)), (BI, nd)]), (sub(K12, 72, 144), [(IDF, L), (ID, const(oD - oFL)), (BI, nd)]),
            (sub(K12, 144, 216), [(IDF, rcx), (IDF, rcx), (ID, const(9344)), (ID, const(-2)), (BI, nd)])])
        LG = ts(U16(72), sub(K12, 144, 216), 1.0, op.add, A - 1.0, op.min)
        for k in range(3):
            gat(CFG["g2"][3 * rnd + k], W(oD + 384 * k, oD + 384 * (k + 1)), W(oFL, oD), sub(LG, 24 * k, 24 * (k + 1)))
        pse = bank(216)
        mm([(sub(pse, 0, 72), [(ID, sub(P16, 0, 72)), (BI, nann)]), (sub(pse, 72, 144), [(IDF, L), (ID, const(A)), (BI, nann)]),
            (sub(pse, 144, 216), [(IDF, L), (ID, const(oU - oFL + 2 * A)), (BI, nann)])])
        LD = ts(U16(72), sub(pse, 0, 72), i16, op.add, float(A), op.min)
        hot(5.0)
        E12 = tt(F(144), sub(pse, 72, 216), BA, op.min)
        for k in range(3):
            lo, hi = 384 * k, 384 * (k + 1)
            if CFG["in1"][3 * rnd + k] == "v":
                tt(t("IN1", lo, hi), ind(t("DIF", 0, A + 16), sub(LD, 24 * k, 24 * (k + 1))), sub(FBv, A + lo, A + hi), op.subtract)
            else:
                gat("s", t("LL", lo, hi), t("DIF", 0, A + 16), sub(LD, 24 * k, 24 * (k + 1)))
                ps = big(384)
                mm([(ps, [(NID, sub(FBv, A + lo, A + hi)), (ID, t("LL", lo, hi))])])
                act(t("IN1", lo, hi), ps)
            act(t("IN1", A + lo, A + hi), t("IN1", lo, hi), None, N18)
        S1 = tt(F(144), sub(K12, 0, 144), E12, op.min)
        tt(sub(S1, 72, 144), sub(K12, 144, 216), sub(S1, 72, 144), op.min)
        LS1 = cp(U16(144), S1)
        JL = [U16(144) for k in range(4)]
        top["set"] = (3, 4)

        def jlist(k, c):
            lo, hi = CH[c], CH[c + 1]
            src, cb, e = sub(VX[k % 2], 16 * lo, 16 * hi), sub(CBS[k % 2], 16 * lo, 16 * hi), CFG["jl"][4 * rnd + k]
            if "g" in e:
                twin(e[c], cb, src)
            elif e[c] == "s":
                act(cb, src, None, 192.0, 1.0 / C)
            twin(CFG["sh"][4 * rnd + k][c], t("IN1", 16 * lo, 16 * hi), src)
            if hi in CFG["wr"]:
                lo = CFG["wr"][CFG["wr"].index(hi) - 1]
                own = [(ID, sub(P16, 72 + lo, 72 + hi))]
                if e[c] == "t":
                    ts(sub(JL[k], lo, hi), wrap(sub(VX[k % 2], 16 * lo, 16 * hi), BDF, own), ifr, op.add)
                else:
                    ts(sub(JL[k], lo, hi), wrap(sub(CBS[k % 2], 16 * lo, 16 * hi), BDA if "g" in e else BD, own), ifg if "g" in e else ioff, op.add)
        cuts = sorted(set(CH) | {72})
        for lo, hi in zip(cuts, cuts[1:]):
            win = W(oU, oF + P) if lo < 72 else W(oFL, oF + P)
            tt(sub(VX[0], 16 * lo, 16 * hi), ind(win, sub(LS1, lo, hi)), t("IN1", 16 * lo, 16 * hi), op.add)
        for c in range(len(CH) - 1):
            jlist(0, c)
        for k in range(4):
            for c in range(len(CH) - 1):
                lo, hi = CH[c], CH[c + 1]
                tt(sub(VX[(k + 1) % 2], 16 * lo, 16 * hi), ind(VW[k % 2], sub(JL[k], lo, hi)), t("IN1", 16 * lo, 16 * hi), op.add)
                if k < 3:
                    jlist(k + 1, c)
        top["set"] = (5, 6, 7)
        UVb = Bf(576)
        twin(CFG["tb"][0], sub(UVb, 0, 576, 2), W(oUL, oUL + 288))
        ps = wrap(sub(UVb, 0, 576, 2), BDA)
        LU = ts(U16(18), ps, -OFA, op.add)
        act(sub(UVb, 1, 576, 2), ind(W(oU, oU + A), LU))
        ps = wrap(UVb, BDA)
        LUV = ts(U16(36), ps, -OFA, op.add, float(A - 1), op.min)
        for c in range(2):
            gat("s", W(oT + 288 * c, oT + 288 * (c + 1)), W(oU + 2 * A, oU + 3 * A), sub(LUV, 18 * c, 18 * (c + 1)))
        twin(CFG["tb"][1], W(oC, oC + 576), UVb)
        twin(CFG["tb"][2], W(oF2, oF2 + 576, 2), W(oFL + 1, oFL + 576, 2))
        twin(CFG["tb"][3], W(oF2 + 1, oF2 + 576, 2), W(oFL, oFL + 576, 2))
        XU = Bf(576)
        for c in range(2):
            gat("s", sub(XU, 288 * c, 288 * (c + 1)), x, sub(LUV, 18 * c, 18 * (c + 1)))
        xe, xo = sub(XU, 0, 576, 2), sub(XU, 1, 576, 2)
        ps = big(288)
        mm([(ps, [(ID, xe), (NID, xo)])])
        act(t(Xc, oXF + 1, oXF + 576, 2), ps, fn.Abs)
        act(t(Xc, oXF, oXF + 576, 2), mod16(big(288), [xe, xo]))
        n2 = ts(F(1), sub(incc, 71, 72), room, op.min, 2.0, op.mult)
        used = ts(Bf(72), rfx, 4095.0 - A, op.add, n2, op.is_lt)
        ps = bank(216)
        rm, cm, rd_ = sub(ps, 0, 72), sub(ps, 72, 144), sub(ps, 144, 216)
        mm([(rm, [(IDF, a1), (NBI, used)]), (cm, [(IDF, k0a), (NBI, nd)]),
            (rd_, [(IDF, cp(F(72), sub(JL[0], 72, 144))), (NDF, sub(AW, 144, 216)), (NBI, nd)])])
        Rb = act(F(72), rm, fn.Relu, K0 + 4095.0 - BIG, -1.0)
        Ra, Rd = act(F(72), cm, fn.Relu, float(A)), act(F(72), rd_, fn.Relu, float(P + A))
        ps2 = bank(216)
        more = ([(IDF, Ra)], [(IDF, Ra), (ID, const(P - A)), (DG[3], nd)], [(IDF, Rd)])
        mm([(sub(ps2, 72 * i, 72 * (i + 1)), [(ID, sub(P16, 72 * i, 72 * (i + 1))), (NPI, nann), (IDF, Rb), (DG[i], used)] + more[i]) for i in range(3)])
        LS2 = ts(U16(216), ps2, iP, op.add)
        hot(8.0)
        LP = U16(232)
        if rnd:
            act(sub(Lw, 72, 232), wrap(cb5, BDA), None, -OFA)
        ps3 = bank(160)
        mm([(sub(ps3, 72 * i, 72 * (i + 1)), [(IDF, sub(Lw, 72 * (i + 1), 72 * (i + 2))), (BI, nann), (BI, nd), (BI, used), (ID, const(-2 * BIG))]) for i in range(2)]
           + [(sub(ps3, 144, 160), [(IDF, sub(Lw, 216, 232))])])
        ts(sub(LP, 72, 232), ps3, 0.0, op.max, float(P), op.min)
        ps = bank(72)
        mm([(ps, [(ID, sub(P16, 0, 72)), (IDF, Rb), (DG[4], used)])])
        LX = ts(U16(72), ps, i16, op.add)
        hot(8.0)
        ups = [t("UP", 384 * c, 384 * (c + 1)) for c in range(9)]
        if rnd == 0:
            cbp = Bf(A)
            ups[:3] = [sub(cbp, 384 * c, 384 * (c + 1)) for c in range(3)]
        for c in range(9):
            act(ups[c], ind(W(oU, WEND), sub(LS2, 24 * c, 24 * (c + 1))), None, -7.5 if last else 0.0)
        if rnd == 0:
            ts(sub(LP, 0, 72), wrap(cbp, BDA), -OFA, op.add)
        elif CFG["up"][rnd] == "t":
            ts(sub(LP, 0, 72), wrap(t("UP", 0, A), BDF), -OFA - 0.47, op.add)
        else:
            cbp = Bf(A)
            cast(CFG["up"][rnd], cbp, t("UP", 0, A))
            ts(sub(LP, 0, 72), wrap(cbp, BDA), -OFA, op.add)
        hot(4.0)
        for c in range(4):
            gat("s", t(Xn, DM + 288 * c, DM + 288 * (c + 1)), t(Xc, DM, oXF + 576), sub(LX, 18 * c, 18 * (c + 1)))
        xn = t(Xn, DM, DM + A)
        U4b = U(3 * A, P)
        tt(U4b, ind(VF, sub(LP, 216, 232)), W(oU + 3 * A, oU + P), op.add)
        ops[-1]["sent"] = rnd
        for c in range(6):
            tt(U(576 * c, 576 * (c + 1)), ind(VF, sub(LP, 36 * c, 36 * (c + 1))), sub(cbp if rnd == 0 and c < 2 else t("UP", 0, 3 * A), 576 * c, 576 * (c + 1)), op.add)
        top["set"] = (3, 4, 5, 6, 7)
        L4 = F(232)
        L4u = U16(232)
        cb0 = CBS[0]
        act(sub(cb0, 3 * A, P), U4b)
        ps = wrap(sub(cb0, 3 * A, P), BDA)
        LB = ts(U16(16), ps, -OFA, op.add, float(A - 1), op.min)
        ts(sub(L4u, 216, 232), ps, -OFA, op.add)
        Lb = act(sub(L4, 216, 232), ps, None, -OFA)
        PP, PX, PF = PAY[rnd]
        LPv, LXv, LFv = t("LP%d" % rnd, 0, B), t("LX%d" % rnd, 0, B), t("LF%d" % rnd, 0, 16)
        if last:
            send(rnd, 0, act(PP, mod16(big(256), [U4b])), LPv)
        else:
            send(rnd, 0, sub(U4b, 0, 64), t("LR", 0, 64))
            send(rnd, 3, sub(U4b, 64, B), t("LR", 64, B))
            ps = big(256)
            mm([(ps, [(IDF, t("LR", 0, B)), (NID, act(Bf(256), t("LR", 0, B)))])])
            act(LPv, ps)
        gat("s", PX, xn, LB)
        hot(10.0)
        send(rnd, 1, PX, LXv)
        bk = act(Bf(256), ind(U(0, A), LB))
        h1 = act(Bf(16), Lb, fn.Relu, (1.0 - A) * 8192.0, 8192.0)
        psb = wrap(bk, BDA, [(ID, h1)])
        tt(PF, psb, AWB, op.is_equal)
        send(rnd, 2, PF, LFv)
        for c in range(3):
            lo, hi = A * c, A * (c + 1)
            if CFG["u4"][3 * rnd + c] == "t":
                ps = wrap(U(lo, hi), BDF)
            else:
                cast(CFG["u4"][3 * rnd + c], sub(cb0, lo, hi), U(lo, hi))
                ps = wrap(sub(cb0, lo, hi), BDA)
            if c < 2:
                act(sub(L4, 72 * c, 72 * (c + 1)), ps, None, -OFA)
            else:
                ts(sub(L4u, 72 * c, 72 * (c + 1)), ps, -OFA - 0.24, op.add)
        if last:
            if "b" in CFG["mod"].lower():
                add("g", lambda q, T, x: q.affine_select(T["XC"][:, :], T["XC"][:, :], [[0, A]], op.is_gt, 7.5, 0, 0), [t("XC", 0, A)], [t("XC", 0, A)],
                    0.17 + 2 * A * CY)
            for c in range(9):
                lo, hi = 384 * c, 384 * (c + 1)
                ps, out, e = big(384), t("DR", DM + lo, DM + hi), CFG["mod"][c]
                if e == "u":
                    act(out, mod16(ps, [U(lo, hi)], True))
                    continue
                if e == "t":
                    mm([(ps, [(IDF, U(lo, hi)), (IM, ONES), (NM, ONES), (N75, ONES)])])
                elif e in "AB":
                    act(ps, act(ps, U(lo, hi), None, MAGIC), None, -MAGIC)
                else:
                    ts(ps, U(lo, hi), MAGIC, op.add, -MAGIC, op.add)
                tt(out, U(lo, hi), ps, op.subtract)
                if e == "v":
                    act(out, out, None, 7.5)
                elif e in "abAB":
                    l0 = lo if c == 0 or CFG["mod"][c - 1] not in "aA" else l0
                    if e in "bB":
                        accum(t("DR", DM + l0, DM + hi), t("XC", 0, hi - l0))
            dma("y", lambda q, T, x: q.dma_start(T["yp"][:, 2 * A:3 * A], T["DR"][:, DM + 2 * A:DM + 3 * A]), [t("DR", DM + 2 * A, DM + 3 * A)], [], 2 * A)
            gat("s", t("SV", 256, 512), t("RHO", DM, DM + A), LB)
            act(t("SV", 0, 256), t("SV", 256, 512), None, float(A))
            gat("s", sub(SVb, 0, 256), t("DR", DM + A, DM + 2 * A), LB)
            act(sub(SVb, 256, 512), mod16(big(256), [PP, LPv]))
        else:
            gat("s", t("SV", 0, 256), U(A, 2 * A), LB)
            ps = big(256)
            mm([(ps, [(ID, sub(FBv, 3 * A, P)), (IDF, U4b), (NID, sub(cb0, 3 * A, P)), (ID, LPv)])])
            act(t("SV", 256, 512), ps)
        ps = bank(72)
        mm([(ps, [(IDF, sub(L4, 72, 144)), (NDF, sub(L4, 0, 72))])])
        dl = act(F(72), ps, None, 0.0, 1.0 / (A * C))
        psq = bank(48)
        q3 = [sub(psq, 16 * i, 16 * (i + 1)) for i in range(3)]
        mm([(psq, [(ID, CA)])], True, False)
        mm([(q3[0], [(IDF, Lb), (BI, PF)]), (q3[1], [(IDF, Lb), (BI, PF)]), (q3[2], [(NDF, sub(AW, 0, 16)), (BI, PF)])], False, False)
        mm([(q3[0], [(BI, LFv)]), (q3[1], [(BI, LFv)])], False, False)
        mm([(q3[2], [(BI, LFv)])], False, True)
        Q2 = tt(F(48), psq, KK[rnd], op.max)
        LQ = ts(U16(32), sub(Q2, 0, 32), DM - 2 * BIG, op.add)
        LK = ts(U16(16), sub(Q2, 32, 48), -1.0, op.mult, 2 * BIG, op.add)
        lpw = t("LP%d" % rnd, 0, B + 16)
        mk = "CB5" if last else "DR"
        if last:
            fill(t("CB5", 0, 832), 0)
            twin("y", t("CB5", 832, DM + A), t("CB5", 0, 832))
        cp(ind(t(mk, 0, DM + A), sub(LQ, 0, 16)), DS)
        ps = wrap(t(mk, DM, DM + A), BD)
        m2 = tt(F(72), ps, dl, op.mult)
        L5 = tt(F(72), sub(L4, 0, 72), m2, op.add)
        ts(sub(L4u, 0, 72), L5, -0.24, op.add)
        ps = bank(72)
        mm([(ps, [(IDF, sub(L4, 72, 144)), (NDF, m2)])])
        ts(sub(L4u, 72, 144), ps, -0.24, op.add)
        if not last:
            ts(t("DR", DM + A, DM + 2 * A), t("DR", DM, DM + A), -1.0, op.mult)
            scat(CFG["sv"][0], t("U4", 0, DM + A), sub(LQ, 0, 16), t("SV", 0, 256))
            cp(ind(t(Xn, 0, DM + A), sub(LQ, 0, 16)), LXv)
            cuts = ((0, 36), (36, 72), (72, 96), (96, 120), (120, 144), (216, 232), (144, 168), (168, 192), (192, 216))

            def rename(ks, L4u=L4u):
                for k in ks:
                    lo, hi = cuts[k]
                    if CFG["rn"][k] == "v":
                        tt(W(oU + 16 * lo, oU + 16 * hi), ind(t("DR", DM, DM + P), sub(L4u, lo, hi)), U(16 * lo, 16 * hi), op.add)
                    elif CFG["rn"][k] in "de":
                        gat("s", W(oU + 16 * lo, oU + 16 * hi), t("DR", DM, DM + P), sub(L4u, lo, hi))
                        l0 = lo if k == ks[0] or CFG["rn"][k - 1] != "d" else l0
                        if CFG["rn"][k] == "e":
                            accum(W(oU + 16 * l0, oU + 16 * hi), U(16 * l0, 16 * hi))
                    else:
                        d = gat("s", sub(cb0, 16 * lo, 16 * hi), t("DR", DM, DM + P), sub(L4u, lo, hi))
                        ps = ("PS%d" % (3 + k % 2), 0, 16 * (hi - lo), 1)
                        mm([(ps, [(IDF, U(16 * lo, 16 * hi)), (ID, d)])])
                        act(W(oU + 16 * lo, oU + 16 * hi), ps)

            def later(LQ=LQ, LK=LK, lpw=lpw):
                scat(CFG["sv"][1], t("U4", 0, DM + 2 * A), sub(LQ, 16, 32), t("SV", 256, 512))
                rename(range(2, 9))
                tt(W(oU + 3 * A, oU + P), ind(lpw, LK), W(oU + 3 * A, oU + P), op.add)
                cast("g", cb5, W(oU + A, oU + P))
            rename(range(2))
            Lw = Lw1
            top["set"] = (5,)
            if CFG["lc"] == "s":
                for c in range(2):
                    gat("s", t("CB1", 576 * c, 576 * (c + 1)), t("DR", DM, DM + P), sub(L4u, 36 * c, 36 * (c + 1)))
                ps, off = wrap(t("CB1", 0, A), BDA, [(IDF, L5)]), 0.0
            else:
                ps, off = wrap(W(oU, oU + A), BDF), -OFA
            LC = ts(LC1, ps, off, op.add, float(A), op.min)
            ts(sub(Lw, 0, 72), ps, MAGIC / 16 + off, op.add, -MAGIC / 16, op.add)
        else:
            for c in range(2):
                scat(CFG["sv"][2 + c], t("RHO", 0, DM + 2 * A), sub(LQ, 16 * c, 16 * (c + 1)), t("SV", 256 * c, 256 * (c + 1)))
            for k, (lo, hi) in enumerate(((144, 174), (174, 204), (204, 232), (0, 36), (36, 72), (72, 108), (108, 144))):
                lin(CFG["yl"][k], W(oF + 16 * lo, oF + 16 * hi), ind(t("RHO", DM, DM + P), sub(L4u, lo, hi)), -64.0, 1.0)
            dma("y", lambda q, T, x: q.dma_start(T["yl"][:, 2 * A:P], T["W"][0:128:16, oF + 2 * A:oF + P]), [W(oF + 2 * A, oF + P)], [], 0)
            dma("y", lambda q, T, x: q.dma_start(T["yl"][:, 0:2 * A], T["W"][0:128:16, oF:oF + 2 * A]), [W(oF, oF + 2 * A)], [], 0)
            bp = gat("s", Bf(256), sub(SVb, 256, 768), LK)
            dma("y", lambda q, T, x: q.dma_start(T["yp"][:, 3 * A:P], ap(T, bp)), [bp], [], 2 * B)
            cp(ind(t("DR", 0, DM + 2 * A), LQ), sub(SVb, 0, 512))
            for c, e in enumerate("ys"):
                dma(e, lambda q, T, x, c=c: q.dma_start(T["yp"][:, c * A:(c + 1) * A], T["DR"][:, DM + c * A:DM + (c + 1) * A]),
                    [t("DR", DM + c * A, DM + (c + 1) * A)], [], 2 * A)
            cp(ind(t(Xn, 0, DM + A), sub(LQ, 0, 16)), LXv)
            dma("y", lambda q, T, x: q.dma_start(T["yx"][:, :], ap(T, xn)), [xn], [], 2 * A)
    assert top["dma"] <= NDMA
    return ops


def hit(a, b):
    for n, lo, hi in a:
        for m, l2, h2 in b:
            if n == m and lo < h2 and l2 < hi:
                return True
    return False


def schedule(ops, guess):
    n = len(ops)
    slow = [v[2] for v in guess]
    both = [[{e: w[1] * f.get(e, 1.0) for e, w in o.get("ways", {o["eng"]: (0, o["cost"])}).items()} for o in build(a, b)] for a, b, d, f in guess]
    costs = [[c[o["eng"]] for c, o in zip(row, ops)] for row in both]
    anc, pre = [], []
    for j, o in enumerate(ops):
        pj = [r for r in o["rd"] if r[0].startswith("PS")]
        o["dep"] = [i for i in range(j) if hit(ops[i]["wr"], o["rd"]) or hit(ops[i]["wr"], o["wr"]) or hit(ops[i]["rd"], o["wr"])
                    or (pj and (ops[i]["eng"] != o["eng"] or "ways" in o or "ways" in ops[i]) and hit(ops[i]["rd"], pj))]
        m, keep = 0, []
        for i in reversed(o["dep"]):
            if not m >> i & 1:
                keep.append((i, (HOP[0] if ops[i]["eng"] == o["eng"] else HOP[1]) + ops[i]["lat"]))
                m |= anc[i] | 1 << i
        anc.append(0 if o["kind"] == "a" else m)
        pre.append(keep)
    eng = [o["eng"] for o in ops]
    lat = [o["lat"] for o in ops]
    suc = [[] for o in ops]
    up = []
    for j in range(n):
        m = 1 << j
        for i, h in pre[j]:
            suc[i].append((j, h))
            m |= up[i]
        up.append(m)

    def place(key, back=False):
        busy, st, en = {e: [] for e in eng}, [0.0] * n, [0.0] * n
        for j in sorted(range(n), key=lambda j: key[j]):
            c = ops[j]["cost"]
            s = lat[j] if back else 0.0
            for i, h in (suc[j] if back else pre[j]):
                if en[i] + h > s:
                    s = en[i] + h
            iv = busy[eng[j]]
            k = len(iv)
            while k > 0 and iv[k - 1][1] > s:
                k -= 1
            while k < len(iv) and s + c > iv[k][0]:
                s = max(s, iv[k][1])
                k += 1
            iv.insert(k, (s, s + c))
            st[j], en[j] = s, s + c
        return [-v for v in en] if back else st

    def judge(st):
        tot = 0.0
        seq = sorted(range(n), key=lambda j: (st[j], j))
        for cost, sl in zip(costs, slow):
            free, en, last = {e: 0.0 for e in eng}, [0.0] * n, 0.0
            for j in seq:
                s = free[eng[j]]
                for i, h in pre[j]:
                    if en[i] + h * sl > s:
                        s = en[i] + h * sl
                en[j] = free[eng[j]] = s + cost[j]
                last = max(last, en[j] + lat[j] * sl)
            tot += last / sum(cost)
        return tot

    def ranks(bump):
        rk = [0.0] * n
        for j in range(n - 1, -1, -1):
            rk[j] += ops[j]["cost"] + bump[j] + (lat[j] if rk[j] == 0.0 else 0.0)
            for i, h in pre[j]:
                rk[i] = max(rk[i], rk[j] + h)
        return rk

    def chain(st):
        en = [st[j] + ops[j]["cost"] for j in range(n)]
        prev, lastq = [None] * n, {}
        for j in sorted(range(n), key=lambda j: (st[j], j)):
            prev[j] = lastq.get(eng[j])
            lastq[eng[j]] = j
        j, out = max(range(n), key=lambda j: en[j] + lat[j]), []
        while j is not None:
            out.append(j)
            c = [(en[i] + h, i) for i, h in pre[j]] + ([(en[prev[j]] - 0.001, prev[j])] if prev[j] is not None else [])
            j = max(c)[1] if c else None
        return out
    seed = [SEED]

    def rnd():
        seed[0] = (seed[0] * 6364136223846793005 + 1442695040888963407) % 2 ** 64
        return (seed[0] >> 11) / 2.0 ** 53
    st = place([-v for v in ranks([o["bump"] for o in ops])])
    cur = best = (judge(st), st)
    crit = []
    for k in range(ROUNDS):
        if k % 20 == 0:
            crit = chain(cur[1])
        key = list(cur[1])
        u = rnd()
        if u < 0.03:
            key = place([-key[j] - ops[j]["cost"] for j in range(n)], True)
        else:
            j = crit[int(rnd() * len(crit))] if u < 0.6 else int(rnd() * n)
            d = 0.1 + rnd() ** 3 * 12.0
            if rnd() < 0.7:
                m = up[j]
                key = [key[i] - d if m >> i & 1 else key[i] for i in range(n)]
            else:
                key = [key[i] + d if up[i] >> j & 1 else key[i] for i in range(n)]
        st = place(key)
        v = judge(st)
        if v <= cur[0] + TEMP * (1.0 - k / ROUNDS) * rnd():
            cur = (v, st)
            if v < best[0]:
                best = cur
    order = sorted(range(n), key=lambda j: (best[1][j], j))
    down = [0] * n
    for j in range(n - 1, -1, -1):
        down[j] = 1 << j
        for i, h in suc[j]:
            down[j] |= down[i]
    pres = [[[(i, h * sl) for i, h in pre[j]] for j in range(n)] for sl in slow]
    norm = [sum(c) for c in costs]
    glue = [() if o["eng"] == "n" else (j,) if o["kind"] == "c" else (j, j + 1) for j, o in enumerate(ops)]
    for row in pres:
        for j in range(n):
            if eng[j] == "n":
                row[j] = [v for v in row[j] if v[0] == j - 1]

    def run(seq, m, a=0, old=None):
        cost, pr = costs[m], pres[m]
        en, why = (list(old[2]), list(old[4])) if a else ([0.0] * n, [None] * n)
        free, lastq = {e: 0.0 for e in "vstgyn"}, {e: None for e in "vstgyn"}
        for v in seq[max(0, a - 150):a]:
            for j in glue[v]:
                free[eng[j]], lastq[eng[j]] = en[j], j
        for v in seq[a:]:
            for j in glue[v]:
                e = eng[j]
                s, w = free[e], lastq[e]
                for i, h in pr[j]:
                    h += en[i]
                    if h > s:
                        s, w = h, i
                why[j], lastq[e] = w, j
                en[j] = free[e] = s + cost[j]
        last, lj = max((en[j] + lat[j] * slow[m], j) for j in ends)
        return [last / norm[m], lj, en, None, why]

    def back(seq, m, got, b=n, old=None):
        cost, su, why = costs[m], sucs[m], got[4]
        q, nxt = list(old[3]) if old else [0.0] * n, {e: 0.0 for e in "vstgyn"}
        for v in seq[b + 150:b:-1]:
            for j in glue[v][::-1]:
                nxt[eng[j]] = q[j]
        for v in seq[b::-1]:
            for j in glue[v][::-1]:
                e = eng[j]
                s = nxt[e]
                for i, h in su[j]:
                    h += q[i]
                    if h > s:
                        s = h
                q[j] = nxt[e] = s + cost[j]
        pairs, j = [], got[1]
        while why[j] is not None:
            if eng[why[j]] == eng[j] and not up[j] >> why[j] & 1:
                d = eng[j] == "n"
                pairs.append((why[j] - d, j - d))
            j = why[j]
        got[1], got[3] = pairs, q
        return got
    ends = [j for j in range(n) if not suc[j]]

    def bound(seq, mid, a, b):
        tot, inside, before, after = 0.0, [j for v in mid for j in glue[v]], {}, {}
        for v in seq[max(0, a - 80):a]:
            for j in glue[v]:
                before[eng[j]] = j
        for v in seq[b + 80:b:-1]:
            for j in reversed(glue[v]):
                after[eng[j]] = j
        for m in res:
            cost, pr, en, q = costs[m], pres[m], res[m][2], res[m][3]
            new, free, last = {}, {e: en[j] for e, j in before.items()}, res[m][0] * norm[m]
            if max(en[j] - cost[j] + q[j] for j in inside) > last - 0.7:
                last = 0.0
            for j in inside:
                s = free.get(eng[j], 0.0)
                for i, h in pr[j]:
                    h += new[i] if i in new else en[i]
                    if h > s:
                        s = h
                new[j] = free[eng[j]] = s + cost[j]
            for j in inside:
                for i, h in sucs[m][j]:
                    if i not in new and new[j] + h + q[i] > last:
                        last = new[j] + h + q[i]
            for e, j in after.items():
                if e in free and free[e] + q[j] > last:
                    last = free[e] + q[j]
            tot += last / norm[m]
        return tot

    def flip(j):
        eng[j] = "s" if eng[j] == "v" else "v"
        for m in range(len(costs)):
            costs[m][j] = both[m][j][eng[j]]
    sucs = [[[] for j in range(n)] for row in pres]
    for m, row in enumerate(pres):
        for j in range(n):
            for i, h in row[j]:
                sucs[m][i].append((j, h))
    res, took = {}, 0
    for k in range(SWAPS):
        if k in (0, SWAPS * 2 // 3):
            ms = (0,) if k == 0 else range(1, len(costs))
            if k:
                order = best[1]
                for j in range(n):
                    if eng[j] != best[2][j]:
                        flip(j)
            res = {m: back(order, m, run(order, m)) for m in ms}
            cur = sum(r[0] for r in res.values())
            best, k0, k1 = (cur, order, list(eng)), k, SWAPS if k else SWAPS * 2 // 3
            pos = {j: k for k, j in enumerate(order)}
        pairs = res[ms[int(rnd() * len(ms))]][1]
        i, j = pairs[int(rnd() * len(pairs))]
        a, b = pos[i], pos[j]
        u, other = rnd(), None
        if u < 0.2:
            other = i if u < 0.1 else j
            if "ways" not in ops[other]:
                continue
            flip(other)
            mid = order[a:b + 1]
        elif u < 0.6:
            a, m = max(0, a - int(rnd() ** 3 * 40)), up[j]
            mid = [v for v in order[a:b + 1] if m >> v & 1] + [v for v in order[a:b + 1] if not m >> v & 1]
        else:
            b, m = min(n - 1, b + int(rnd() ** 3 * 60)), down[i]
            mid = [v for v in order[a:b + 1] if not m >> v & 1] + [v for v in order[a:b + 1] if m >> v & 1]
        lim = cur + TEMP * (k1 - k) / (k1 - k0) * rnd() ** 2
        if bound(order, mid, a, b) <= lim:
            new = order[:a] + mid + order[b + 1:]
            got = {m: run(new, m, a, res[m]) for m in ms}
            v = sum(r[0] for r in got.values())
            if v <= lim:
                took += 1
                if took % 50 == 0:
                    en = got[ms[0]][2]
                    new = sorted(new, key=lambda j: en[j] - costs[ms[0]][j])
                    got = {m: back(new, m, run(new, m)) for m in ms}
                    v = sum(r[0] for r in got.values())
                else:
                    got = {m: back(new, m, got[m], b, res[m]) for m in ms}
                order, cur, res = new, v, got
                pos = {j: k for k, j in enumerate(order)}
                if v < best[0]:
                    best = (v, new, list(eng))
                continue
        if other is not None:
            flip(other)
    order = best[1]
    for o, e in zip(ops, best[2]):
        if e != o["eng"]:
            o["eng"], o["f"], o["cost"] = e, o["ways"][e][0], o["ways"][e][1]
    pos = {j: k for k, j in enumerate(order)}
    seen = {}
    for j in order:
        o = ops[j]
        need = {}
        for i, h in pre[j]:
            e = ops[i]
            if o["kind"] in "ax" or e["kind"] == "r":
                continue
            key = e["sem"] if e["kind"] != "c" else "e" + e["eng"]
            if key not in need or pos[i] > pos[need[key]]:
                need[key] = i
        o["wait"] = []
        for key in sorted(need):
            i = need[key]
            if seen.get((o["eng"], key), -1) < pos[i]:
                seen[(o["eng"], key)] = pos[i]
                o["wait"].append((key, i))
                ops[i]["sig"] = True
    count = {}
    for j in order:
        o = ops[j]
        if o["kind"] == "c" and o.get("sig"):
            count[o["eng"]] = count.get(o["eng"], 0) + 1
            o["val"] = count[o["eng"]]
    return order, count


PLAN = {}
GUESS = ((1.5, 3.6, 1.1, {"t": 1.15, "g": 1.1}), (1.5, 2.7, 1.2, {}), (1.8, 4.9, 0.8, {}), (1.15, 3.5, 1.0, {"t": 1.45, "g": 1.3}))
ROUNDS, SWAPS, SEED, HOP, TEMP = 200, 200000, 1, (0.08, 0.15), 0.0015


def rank_program(g, core, T, topo):
    rank = T.rank_of(core)
    if rank is None:
        return
    if not PLAN:
        PLAN["ops"] = build(1.56, 3.8)
        PLAN["order"], PLAN["count"] = schedule(PLAN["ops"], GUESS)
    ops = PLAN["ops"]
    x = {"pid": [], "rid": [], "mask": []}
    ne = []
    sent = []
    for rnd in range(RO):
        peer = T.cores[rank ^ XM[rnd]]
        rid, pid = topo.addr(peer, core)
        x["pid"].append(pid)
        x["rid"].append(rid)
        x["mask"].append(topo.mask(core, peer))
        ne.append(len(topo.engines(peer, core)))
        sent.append(sum(o["kind"] == "a" and int(o["sem"][2:]) // 4 == rnd for o in ops) * len(topo.engines(core, peer)))
    queue = {"v": g.vector, "s": g.scalar, "t": g.tensor, "g": g, "y": g.sync}

    def full(e):
        if e["kind"] == "c":
            return e["val"]
        if e["kind"] in "dx":
            return 16
        return ne[int(e["sem"][2:]) // 4]
    for j in PLAN["order"]:
        o = ops[j]
        if o["kind"] in "ax":
            continue
        q = queue[o["eng"]]
        for key, i in o["wait"]:
            q.wait_ge(T.sem[key], full(ops[i]))
        if o.get("sent"):
            q.wait_ge(T.sem["sent"], sum(sent[:o["sent"]]))
        ins = o["f"](q, T, x)
        if o["kind"] == "d":
            ins.then_inc(T.sem[o["sem"]], 16)
        elif o["kind"] == "c" and o.get("sig"):
            ins.then_inc(T.sem["e" + o["eng"]], 1)
    g.wait_ge(T.sem["sent"], sum(sent))
    for e in sorted(PLAN["count"]):
        g.wait_ge(T.sem["e" + e], PLAN["count"][e])
    for o in ops:
        if o["kind"] in ("d", "a"):
            g.wait_ge(T.sem[o["sem"]], full(o))
